import numpy as np, ml_dtypes
CORES = [3,11,19,27,35,43,51,59]
N = 8
import mx_ref
BF = ml_dtypes.bfloat16
def entries(a):
    return np.ascontiguousarray(a.T).reshape(-1)
def table(e):
    return np.ascontiguousarray(np.reshape(e, (-1, 16)).T).astype(np.int32)
def pick(q, e):
    c = np.concatenate([q[0].reshape(128, -1, 4), np.zeros((128, 1, 4), np.uint8)], axis=1); s = np.concatenate([q[1], np.ones((16, 1), np.uint8)], axis=1)
    return (np.ascontiguousarray(c[:, e].reshape(128, -1)), np.ascontiguousarray(s[:, e]))
def join(*qs):
    return (np.concatenate([q[0] for q in qs], axis=1), np.concatenate([q[1] for q in qs], axis=1))
def put(q, e, v):
    c, s = q[0].reshape(128, -1, 4).copy(), q[1].copy(); c[:, e] = v[0].reshape(128, -1, 4); s[:, e] = v[1]
    return (c.reshape(128, -1), s)
def pk(c, s):
    return (np.ascontiguousarray(c), mx_ref.live(s))
def emit(q):
    return q[0], q[1]
def cols(t, e):
    v = np.concatenate([t.reshape(128, -1, 4), np.zeros((128, 1, 4), BF)], axis=1)
    return np.ascontiguousarray(v[:, e]).reshape(128, -1)
def cut(t, i, w=512):
    return t[:, w * i:w * i + w]
def f(rng, *shape):
    return mx_ref.flush((rng.standard_normal(shape, dtype=np.float32) * np.exp2(rng.integers(-2, 3, shape[:-1] + (1,)))).astype(BF))
def wide(rng, *shape, cols=0):
    v = rng.standard_normal(shape, dtype=np.float32) * np.exp2(rng.integers(-12, 13, shape)).astype(np.float32)
    if cols: v *= np.repeat(np.exp2(rng.integers(-cols, cols + 1, shape[:-2] + (1, shape[-1] // 4))) * (rng.random(shape[:-2] + (1, shape[-1] // 4)) > 0.0625), 4, axis=-1).astype(np.float32)
    return mx_ref.flush(v.astype(BF))
P, CAPP, LC = 256, 32, 128
def choose(e, g, d):
    c = e[np.arange(P), np.argmax(g[e], axis=1)]
    for s in range(N):
        if s != d:
            late = np.flatnonzero(c // P == s)[CAPP:]
            c[late] = e[late, 0]
    return c
def play(e0, e1, e2, p1, p2, u, a):
    k = [mx_ref.quantize(u[d]) for d in range(N)]
    A = [[mx_ref.quantize(np.ascontiguousarray(cut(a[d], i))) for i in range(4)] for d in range(N)]
    H = [mx_ref.quantize(e0[d]) for d in range(N)]
    g = np.stack([mx_ref.matmul(k[d], H[d])[0] for d in range(N)]) + np.float32(0)
    chosen, tiles, scores = [], [], [g]
    for e, p in ((e1, p1), (e2, p2)):
        every, before = join(*H), g.reshape(-1)
        H, g = [], np.zeros((N, P), np.float32)
        for d in range(N):
            c = choose(entries(p[d]).reshape(P, 4), before, d)
            x = pick(every, c)
            R = np.stack([mx_ref.matmul(A[d][i], x) for i in range(4)], axis=2).reshape(128, 4 * P)
            h = (R * np.float32(0.05) + e[d].astype(np.float32)).astype(BF)
            q = mx_ref.quantize(h)
            g[d] = before[c] + mx_ref.matmul(k[d], q)[0]
            H.append(q)
            chosen.append(c)
            tiles.append(h)
        scores.append(g)
    return np.stack(chosen).reshape(2, N, P), tiles, scores, H
def large(v):
    v = v.astype(np.float32)
    v[np.abs(v) < np.float32(0.03125)] = 0
    return v.astype(BF)
def lean(v, u, s):
    t = np.abs(v.astype(np.float32)).reshape(128, -1, 4) * np.sign(u[:, None, :4].astype(np.float32)) * np.asarray(s, np.float32)[None, :, None]
    return t.reshape(128, -1).astype(BF)
def near(t, u, score):
    size = np.concatenate([[0.0], np.exp2(np.arange(-26, -7))])[:, None] * np.array([1, 1.25, 1.5, 1.75])
    v = np.repeat(t.astype(np.float32).reshape(128, 1, 4), 80, axis=1)
    v[:8] = np.sign(u[:8, None, :4].astype(np.float32)) * size.reshape(1, 80, 1)
    v = np.ascontiguousarray(v.reshape(128, 320).astype(BF))
    s = score(v)
    i = int(np.argmin(np.abs(s - s[0] - np.float32(2.5) * np.spacing(np.abs(s[0])))))
    return cols(v, [0, i])
def strong(u):
    return (u.astype(np.float32) * np.float32(2.0 ** 24)).astype(BF)
def lists(rng):
    out = []
    for d in range(N):
        others = np.delete(np.arange(N), d)
        rank = others[np.argsort(rng.random((P, N - 1)), axis=1)[:, :3]]
        pool = np.stack([rng.permutation(P)[:LC] for s in range(N)])
        e = np.zeros((P, 4), int)
        e[:, 0] = d * P + rng.integers(0, P, P)
        e[:, 1:] = rank * P + pool[rank, rng.integers(0, LC, (P, 3))]
        out.append(table(e.reshape(-1)))
    return np.stack(out)
def crowd(rng, s):
    out, half = [], LC // 2
    for d in range(N):
        x = rng.permutation(np.delete(np.arange(N), d))
        hi = np.stack([rng.permutation(np.flatnonzero(s[r]))[:half] for r in range(N)])
        lo = np.stack([rng.permutation(np.flatnonzero(~s[r]))[:half] for r in range(N)])
        j = rng.permutation(P)
        one, two, home = j[:P // 2], j[P // 2:P // 2 + CAPP], j[P // 2 + CAPP:]
        rank = np.stack([np.full(P, x[0]), np.full(P, x[1]), x[rng.integers(2, N - 1, P)]], axis=1)
        n = rng.integers(0, half, (P, 3))
        n[j, 0] = np.arange(P) % (P // 2) % half
        n[two, 1] = rng.permutation(half)[:CAPP]
        at = lo[rank, n]
        at[one, 0] = hi[x[0], n[one, 0]]
        at[two, 1] = hi[x[1], n[two, 1]]
        e = np.zeros((P, 4), int)
        e[:, 0] = d * P + np.flatnonzero(~s[d])[rng.integers(0, P // 2, P)]
        e[home, 0] = d * P + np.flatnonzero(s[d])[rng.integers(0, P // 2, home.size)]
        e[:, 1:] = rng.permuted(rank * P + at, axis=1)
        out.append(table(e.reshape(-1)))
    return np.stack(out)
def plain(rng):
    u = np.array(f(rng, 128, 512))
    u[:, 4:] = 0
    return {"e0": np.array(f(rng, N, 128, 4 * P)), "e1": large(f(rng, N, 128, 4 * P)), "e2": large(f(rng, N, 128, 4 * P)), "p1": lists(rng), "p2": lists(rng),
            "u": np.stack([u] * N), "a": f(rng, N, 128, 2048), "w": f(rng, N, 128, 512)}
def setup_inputs(rng):
    return plain(rng)
def setup_inputs_full(rng):
    d = plain(rng)
    for e, p, size in (("e0", "p1", 1), ("e1", "p2", 64)):
        s = np.stack([rng.permutation(P) < P // 2 for r in range(N)])
        for r in range(N): d[e][r] = lean(d[e][r], d["u"][r], size * np.where(s[r], 1, -1))
        d[p] = crowd(rng, s)
    return d
def setup_inputs_ties(rng):
    d = plain(rng)
    u, a = np.ascontiguousarray(d["u"][0]), np.array(d["a"][0])
    a.reshape(128, 4, 512)[:, :, :32] = 0
    k = mx_ref.quantize(u)
    def row(t): return mx_ref.matmul(k, mx_ref.quantize(t))[0]
    x = np.concatenate([f(rng, 128, 16), near(lean(f(rng, 128, 4), u, [1]), u, row)], axis=1)
    best = cols(x, [5] * 4)
    top, q = row(best)[0], mx_ref.quantize(best)
    R = np.stack([mx_ref.matmul(mx_ref.quantize(np.ascontiguousarray(cut(a, i))), q)[:, 0] for i in range(4)], axis=1)
    def later(t): return top + row((np.tile(R, 80) * np.float32(0.05) + t.astype(np.float32)).astype(BF))
    z = near(lean(large(f(rng, 128, 4)), u, [8]), u, later)
    d["e0"] = np.stack([cols(x, rng.integers(0, 6, P)) for r in range(N)])
    d["e1"] = np.stack([cols(z, rng.integers(0, 2, P)) for r in range(N)])
    d["a"] = np.stack([a] * N)
    return d
def setup_inputs_own(rng):
    d = plain(rng)
    d["u"] = strong(d["u"])
    best, worst = rng.permutation(N)[:2]
    for r, s in ((best, 1), (worst, -1)):
        d["e0"][r] = lean(d["e0"][r], d["u"][r], np.full(P, 8 * s))
        d["e1"][r] = lean(d["e1"][r], d["u"][r], np.full(P, 256 * s))
    return d
def setup_inputs_flip(rng):
    d = plain(rng)
    d["u"] = strong(d["u"])
    for r in range(N):
        s = rng.permutation(P) % 2 * 2 - 1
        d["e0"][r] = lean(d["e0"][r], d["u"][r], 1024 * s)
        d["e1"][r] = lean(d["e1"][r], d["u"][r], -16384 * s)
    return d
def setup_inputs_spread(rng):
    d = plain(rng)
    d["e0"] = wide(rng, N, 128, 4 * P, cols=4)
    d["e1"] = large(wide(rng, N, 128, 4 * P, cols=4))
    d["e2"] = large(wide(rng, N, 128, 4 * P, cols=4))
    return d
def check_inputs(d):
    b = []
    for k in ("e0", "e1", "e2", "u", "a", "w"):
        v = np.abs(d[k].astype(np.float32))
        if not (np.isfinite(v).all() and ((v == 0) | (v >= 2.0 ** -30) & (v <= 2.0 ** 30)).all()): b.append("a value of " + k)
    u = d["u"].astype(np.float32)
    if (u[:, :, 4:] != 0).any(): b.append("u has numbers behind its column 0")
    if (u != u[:1]).any(): b.append("u isn't the same on all ranks")
    for k in ("p1", "p2"):
        for r in range(N):
            e = entries(d[k][r]).reshape(P, 4)
            if e.min() < 0 or e.max() >= N * P:
                b.append(k + " out of range")
                continue
            o = np.sort(e[:, 1:] // P, axis=1)
            if (e[:, 0] // P != r).any(): b.append(k + ": predecessor 0")
            if (o == r).any() or (o[:, 1:] == o[:, :-1]).any(): b.append(k + ": predecessors 1 to 3")
            if np.bincount(np.unique(e[:, 1:]) // P, minlength=N).max() > LC: b.append(k + ": too many columns of one rank")
    if not b:
        chosen, tiles, scores, H = play(*[d[k] for k in ("e0", "e1", "e2", "p1", "p2", "u", "a")])
        v = np.abs(np.stack(tiles).astype(np.float32))
        if not (np.isfinite(v).all() and ((v == 0) | (v >= 2.0 ** -30) & (v <= 2.0 ** 30)).all()): b.append("a value of h_1 or h_2")
        if not np.isfinite(np.stack(scores)).all(): b.append("a score")
    return b
def reference(e0, e1, e2, p1, p2, u, a, w):
    chosen, tiles, scores, H = play(e0, e1, e2, p1, p2, u, a)
    ch, g = np.zeros((N, 2, P), np.float32), np.zeros((N, 1, P), np.float32)
    oc, osc, y = np.zeros((N, 128, 4 * P), np.uint8), np.zeros((N, 16, P), np.uint8), np.zeros((N, 128, P), np.float32)
    for r in range(N):
        ch[r] = chosen[:, r]
        g[r, 0] = scores[2][r]
        oc[r], osc[r] = emit(H[r])
        y[r] = mx_ref.matmul(mx_ref.quantize(w[r]), H[r])
    return {"ch": ch, "g": g, "oc": oc, "osc": osc, "y": y}

@@ -1,0 +1,326 @@
+from concourse.bass import DstId, RemoteDMATransfer
+from concourse.mybir import dt, AluOpType as A, AxisListType, ActivationFunctionType as F
+
+N, P, CAP = 8, 256, 32
+PRED = 4 * P
+BIG = 9e29
+U = 1.0 / 4096.0
+
+_f32 = "float32"
+SCRATCH = {
+    "e0t": ("sbuf", [128, 1024], "bfloat16"), "e1t": ("sbuf", [128, 1024], "bfloat16"), "e2t": ("sbuf", [128, 1024], "bfloat16"),
+    "ut": ("sbuf", [128, 16], "bfloat16"), "ub": ("sbuf", [128, 512], "bfloat16"), "ones": ("sbuf", [128, 128], "bfloat16"),
+    "at": ("sbuf", [128, 2048], "bfloat16"), "wt": ("sbuf", [128, 512], "bfloat16"),
+    "h1": ("sbuf", [128, 1024], "bfloat16"), "h2": ("sbuf", [128, 1024], "bfloat16"),
+    "tm1": ("sbuf", [128, 1024], _f32), "tm2": ("sbuf", [128, 1024], _f32),
+    "ps": ("psum", [128, 2048], _f32), "pr": ("psum", [128, 2048], _f32),
+    "sc": ("sbuf", [128, 2048], _f32), "s2": ("sbuf", [128, 2048], _f32),
+    "iot": ("sbuf", [128, 2048], _f32), "ab": ("sbuf", [128, 2048], _f32),
+    "rs": ("sbuf", [128, 1024], _f32), "zer": ("sbuf", [128, 256], _f32),
+    "pt": ("sbuf", [128, 128], "int32"), "pa": ("sbuf", [128, 128], "int32"), "np": ("sbuf", [128, 128], "int32"),
+    "lo": ("sbuf", [128, 64], "int32"), "hb": ("sbuf", [128, 64], "int32"), "tl": ("sbuf", [128, 64], "int32"),
+    "hm": ("sbuf", [128, 64], "int32"), "po": ("sbuf", [128, 64], "int32"),
+    "of": ("sbuf", [128, 128], "uint16"), "op2": ("sbuf", [128, 64], "uint16"),
+    "ic": ("sbuf", [128, 8], "int32"), "fc": ("sbuf", [128, 16], _f32),
+    "iy": ("sbuf", [128, 32], "int32"), "dup": ("sbuf", [128, 32], "uint16"), "dup4": ("sbuf", [128, 32], "uint16"),
+    "cr": ("sbuf", [128, 256], _f32), "d0": ("sbuf", [128, 256], _f32), "d1": ("sbuf", [128, 256], _f32),
+    "rv": ("sbuf", [128, 2], _f32), "rq": ("sbuf", [128, 2], "uint16"), "rqs": ("sbuf", [128, 16], "uint16"),
+    "ofq": ("sbuf", [128, 16], "uint16"),
+    "scr1": ("sbuf", [128, 256], _f32), "scr2": ("sbuf", [128, 256], _f32), "dg": ("sbuf", [128, 256], _f32),
+    "dgo": ("sbuf", [128, 256], _f32), "scc": ("sbuf", [128, 2], _f32), "g1c": ("sbuf", [128, 2], _f32),
+    "sld": ("dram", [8, 128, 2], _f32),
+    "chr1": ("sbuf", [128, 256], _f32), "chr2": ("sbuf", [128, 256], _f32), "go": ("sbuf", [128, 256], _f32),
+    "ys": ("sbuf", [128, 256], _f32),
+    "ofx1": ("sbuf", [128, 16], "uint16"), "ofx2": ("sbuf", [128, 16], "uint16"), "ofs2": ("sbuf", [128, 16], "uint16"),
+    "ofc2": ("sbuf", [128, 16], "uint16"),
+}
+for _n, _c in (("uq", 128), ("aq", 512), ("wq", 128), ("hw", 2048), ("x1", 256), ("hq", 256), ("sp", 224), ("w2", 512), ("x2", 256), ("zq", 256)):
+    SCRATCH[_n] = ("sbuf", [128, _c], "float8_e4m3fn_x4")
+    SCRATCH[_n + "s"] = ("sbuf", [128, _c], "uint8")
+for _t in ("1", "2"):
+    for _n, _c in (("ga", 1024), ("mx", 1024), ("fl", 1024), ("cn", 1024), ("nr", 1024), ("vd", 1024),
+                   ("ad", 256), ("mk", 256), ("ct", 256), ("kb", 256), ("zz", 256), ("ex", 512), ("tr", 512), ("nx", 512), ("nt", 512),
+                   ("m4", 64), ("m2", 32), ("m1", 16)):
+        SCRATCH[_n + _t] = ("sbuf", [128, _c], _f32)
+    SCRATCH["ti" + _t] = ("sbuf", [128, 16 * 16], "int32")
+
+SEMAPHORES = ["cv", "cs", "ct", "cg", "ls", "rg", "rr", "rc"] + ["h%d" % i for i in range(N)]
+SEMAPHORES += ["de0", "du", "dp1", "dp2", "da", "de1", "dw", "de2", "dog", "ds2", "dofq", "dch1", "dch2", "dout"]
+
+
+def rank_program(g, core, T, topo):
+    d = T.rank_of(core)
+    if d is None:
+        return
+    cores = T.cores
+    Q = {"v": g.vector, "s": g.scalar, "t": g.tensor, "g": g, "y": g.sync}
+    total, seen = {}, {}
+
+    def wait(q, deps):
+        need = {}
+        for name, val in deps:
+            need[name] = max(val, need.get(name, 0))
+        for name in need:
+            if seen.get((q, name), 0) < need[name]:
+                Q[q].wait_ge(T.sem[name], need[name])
+                seen[(q, name)] = need[name]
+
+    def note(ins, name, n):
+        ins.then_inc(T.sem[name], n)
+        total[name] = total.get(name, 0) + n
+        return (name, total[name])
+
+    def V(call, deps, *args, **kw):
+        wait("v", deps)
+        return note(call(*args, **kw), "cv", 1)
+
+    def S(deps, *args, **kw):
+        wait("s", deps)
+        return note(g.scalar.activation(*args, **kw), "cs", 1)
+
+    def MM(deps, out, w, ws, x, xs):
+        wait("t", deps)
+        return note(g.tensor.matmul_mx(out, w, ws, x, xs, True, True), "ct", 1)
+
+    def G(call, deps, *args, **kw):
+        wait("g", deps)
+        return note(call(*args, **kw), "cg", 1)
+
+    def D(q, deps, name, out, in_):
+        wait(q, deps)
+        return note(Q[q].dma_start(out, in_), name, 16)
+
+    tt, ts, tc = g.vector.tensor_tensor, g.vector.tensor_scalar, g.vector.tensor_copy
+    ms, qz, scan, red = g.vector.memset, g.vector.quantize_mx, g.vector.tensor_tensor_scan, g.vector.tensor_reduce
+    u8, u32 = dt.uint8, dt.uint32
+
+    others = [(d + k) % N for k in range(1, N)]
+    ids = []
+    for i in others:
+        rid, pid, _ = topo.addr(cores[i])
+        ids.append(DstId(rid=rid, pnc=pid))
+    mask = topo.mask(core, cores[others[0]])
+    for i in others:
+        mask &= topo.mask(core, cores[i])
+    engs = [e for e in topo.engines(core, cores[others[0]]) if mask >> e & 1]
+    neng = len(engs)
+    lsum = [0]
+
+    def send_all(deps, sem, src, dsts):
+        wait("g", deps)
+        g.remote_dma_fused([RemoteDMATransfer(dst_ids=ids, dma_engine_mask=mask, remote_sem=T.sem[sem], srcs=[src], dsts=dsts)],
+                           local_sem=T.sem.ls)
+        lsum[0] += neng
+
+    def send_each(deps, sem, pairs):
+        wait("g", deps)
+        g.remote_dma_fused([RemoteDMATransfer(dst_ids=[ids[k]], dma_engine_mask=1 << engs[k], remote_sem=T.sem[sem], srcs=[a], dsts=[b])
+                            for k, (a, b) in enumerate(pairs)], local_sem=T.sem.ls)
+        lsum[0] += len(pairs)
+
+    def rel(s, r):
+        return (s - r) % N
+
+    e0 = D("y", [], "de0", T.e0t[:], T.e0[:, :])
+    uu = D("y", [], "du", T.ut[:, 0:8], T.u[:, 0:8])
+    for k in range(8):
+        p1 = D("y", [], "dp1", T.pt[16 * k:16 * k + 16, 0:64], T.p1[:, :])
+    for k in range(8):
+        p2 = D("y", [], "dp2", T.pt[16 * k:16 * k + 16, 64:128], T.p2[:, :])
+    da = D("s", [], "da", T.at[:], T.a[:, :])
+    e1 = D("s", [], "de1", T.e1t[:], T.e1[:, :])
+    e2 = D("s", [], "de2", T.e2t[:], T.e2[:, :])
+    dw = D("s", [], "dw", T.wt[:], T.w[:, :])
+
+    gp = G(g.iota, [], T.ic[:, 0:1], [[0, 1]], 0, 1)
+    giy = G(g.iota, [], T.iy[:], [[16, 16], [0, 2]], 0, 0)
+    on = V(ms, [], T.ones[:], 1.0)
+    q0 = V(qz, [e0], T.hw[:, 0:P], T.hws[:, 0:P], T.e0t[:])
+    send_all([q0], "h%d" % d, T.hw[:, 0:P].bitcast(u8), [T.hw[:, P * rel(d, i):P * rel(d, i) + P].bitcast(u8) for i in others])
+    send_all([q0], "h%d" % d, T.hws[:, 0:P], [T.hws[:, P * rel(d, i):P * rel(d, i) + P] for i in others])
+    gi = G(g.iota, [], T.iot[:], [[1, 2048]], 0, 0, allow_small_or_imprecise_dtypes=True)
+    cut = 2048 - P * d
+    ga = G(g.iota, [], T.ab[:, 0:cut], [[1, cut]], P * d, 0, allow_small_or_imprecise_dtypes=True)
+    if d:
+        ga = G(g.iota, [], T.ab[:, cut:2048], [[1, 2048 - cut]], 0, 0, allow_small_or_imprecise_dtypes=True)
+
+    for k in range(4):
+        ubk = V(ts, [on, uu], T.ub[:, k:512:4], T.ones[:], T.ut[:, k:k + 1], None, A.mult)
+    quq = V(qz, [ubk], T.uq[:], T.uqs[:], T.ub[:])
+
+    x = V(ts, [p1, p2], T.pa[:], T.pt[:], float(2048 - P * d), None, A.add)
+    x = V(ts, [x], T.np[:], T.pa[:], 2047, None, A.bitwise_and)
+    of = V(tc, [x], T.of[:], T.np[:])
+    n2 = T.np[:, 64:128]
+    a1 = V(ts, [x], T.lo[:], n2, 127, None, A.bitwise_and)
+    a2 = V(ts, [x], T.hb[:], n2, 7, 1, A.logical_shift_right, A.bitwise_and)
+    a3 = V(tt, [a1], T.tl[:], n2, T.lo[:], A.add)
+    a4 = V(ts, [a2], T.hm[:], T.hb[:], -127.0, None, A.mult)
+    a5 = V(tt, [a3, a4], T.po[:], T.tl[:], T.hm[:], A.add)
+    op2 = V(tc, [a5], T.op2[:], T.po[:])
+    nr = {}
+    for t in (1, 2):
+        nr[t] = S([gi, of], T["nr%d" % t][:], T.iot[:].indirect(T.of[:, 64 * t - 64:64 * t]), F.Copy, scale=U)
+
+    ic, fc = T.ic, T.fc
+    b1 = V(ts, [gp], ic[:, 1:2], ic[:, 0:1], 7, None, A.bitwise_and)
+    b2 = V(ts, [b1], ic[:, 2:3], ic[:, 1:2], float(N - d), None, A.add)
+    b3 = V(ts, [b2], ic[:, 3:4], ic[:, 2:3], 7, None, A.bitwise_and)
+    b4 = V(ts, [gp], ic[:, 4:5], ic[:, 0:1], 3, None, A.logical_shift_right)
+    b5 = V(ts, [gp], ic[:, 5:6], ic[:, 0:1], 15, None, A.bitwise_and)
+    b6 = V(tc, [b3, b4, b5], fc[:, 0:3], ic[:, 3:6])
+    c1 = V(ts, [b6], fc[:, 3:4], fc[:, 0:1], -256.0 * U, -127.5 * U, A.mult, A.add)
+    c2 = V(ts, [b6], fc[:, 4:5], fc[:, 0:1], 0.0, -100.0, A.is_equal, A.mult)
+    nbc = V(tt, [c1, c2], fc[:, 5:6], fc[:, 3:4], fc[:, 4:5], A.add)
+    i5c = V(ts, [b6], fc[:, 6:7], fc[:, 0:1], 512.0, None, A.mult)
+    c3 = V(ts, [b6], fc[:, 7:8], fc[:, 0:1], 512.0 + 256.0 * U, 1.0, A.mult, A.add)
+    t0c = V(tt, [c3], fc[:, 8:9], fc[:, 7:8], fc[:, 1:2], A.add)
+    t1c = V(ts, [t0c], fc[:, 9:10], fc[:, 8:9], -1.0, -16.0, A.mult, A.add)
+    dup = V(ts, [b6, giy], T.dup[:], T.iy[:], fc[:, 2:3], None, A.add)
+    dup4 = V(ts, [b6, giy], T.dup4[:], T.iy[:], fc[:, 2:3], 4.0, A.add, A.mult)
+    r1 = V(ms, [], T.rs[:], BIG)
+    rs = V(ms, [r1], T.rs[:, 0:1024:4], -BIG)
+    zr = V(ms, [], T.zer[:], 0.0)
+    fl0 = {t: V(ms, [], T["fl%d" % t][:], 0.0) for t in (1, 2)}
+    qa = V(qz, [da], T.aq[:], T.aqs[:], T.at[:])
+    vd, n0 = {}, {}
+    for t in (1, 2):
+        r, v = T["nr%d" % t], T["vd%d" % t]
+        z = V(tt, [nr[t]], v[:, 0:1023], r[:, 0:1023], r[:, 1:1024], A.subtract)
+        vd[t] = V(tc, [z], v[:, 3:1024:4], r[:, 3:1024:4])
+        z = S([nr[t], dup4], T["nx%d" % t][:], r[:].indirect(T.dup4[:]), F.Copy)
+        z = V(g.vector.transpose, [z], T["nt%d" % t][:], T["nx%d" % t][:])
+        n0[t] = V(ts, [z], T["ti%d" % t][:, 0:16], T["nt%d" % t][:, 0:512:32], 4096.0, None, A.mult)
+    s20 = V(ms, [], T.s2[:], 0.0)
+    qw = V(qz, [dw], T.wq[:], T.wqs[:], T.wt[:])
+
+    scd = []
+    for b in range(4):
+        deps = [quq, q0]
+        for k in (2 * b, 2 * b + 1):
+            if k:
+                deps.append(("h%d" % ((d + k) % N), 2 * neng))
+        mt = MM(deps, T.ps[:, 512 * b:512 * b + 512], T.uq[:], T.uqs[:], T.hw[:, 512 * b:512 * b + 512], T.hws[:, 512 * b:512 * b + 512])
+        o, i = T.sc[:, 512 * b:512 * b + 512], T.ps[:, 512 * b:512 * b + 512]
+        scd.append(V(tc, [mt], o, i) if b % 2 else S([mt], o, i, F.Copy))
+
+    def choose(t, win, off, deps):
+        ga_, mx_, fl_, cn_ = T["ga%d" % t], T["mx%d" % t], T["fl%d" % t], T["cn%d" % t]
+        x1 = V(tc, deps, ga_[:, 0:512], win.indirect(off[:, 0:32]))
+        x2 = S(deps, ga_[:, 512:1024], win.indirect(off[:, 32:64]), F.Copy)
+        m = V(scan, [x1, x2, rs], mx_[:], T.rs[:], ga_[:], -BIG, A.min, A.max)
+        for k in (1, 2, 3):
+            f = V(tt, [m, fl0[t]], fl_[:, k:1024:4], ga_[:, k:1024:4], mx_[:, k - 1:1024:4], A.is_le)
+        return V(scan, [f, vd[t]], cn_[:], fl_[:], T["vd%d" % t][:], 0.0, A.mult, A.add)
+
+    def count(t, c, deps):
+        x = S(deps + [nbc], T["ad%d" % t][:], c, F.Abs, bias=fc[:, 5:6])
+        x = V(ts, [x], T["mk%d" % t][:], T["ad%d" % t][:], 128.0 * U, None, A.is_lt)
+        x = V(scan, [x, zr, i5c], T["ct%d" % t][:], T["mk%d" % t][:], T.zer[:], fc[:, 6:7], A.add, A.add)
+        x = V(tt, [x], T["kb%d" % t][:], T["mk%d" % t][:], T["ct%d" % t][:], A.mult)
+        return V(tt, [x] + deps, T["zz%d" % t][:], T["kb%d" % t][:], c, A.add)
+
+    def onto(t, z):
+        ex, tr, m4, m2, m1, ti = [T[n + str(t)] for n in ("ex", "tr", "m4", "m2", "m1", "ti")]
+        x1 = V(tc, [z, dup], ex[:, 0:256], T["zz%d" % t][:].indirect(T.dup[:, 0:16]))
+        x2 = S([z, dup], ex[:, 256:512], T["zz%d" % t][:].indirect(T.dup[:, 16:32]), F.Copy)
+        x = V(g.vector.transpose, [x1, x2], tr[:], ex[:])
+        for k in range(4):
+            y = V(tt, [x], m4[:, 16 * k:16 * k + 16], tr[:, k:512:32], tr[:, k + 4:512:32], A.max)
+        y = V(tt, [y], m2[:], m4[:, 0:32], m4[:, 32:64], A.max)
+        y = V(tt, [y], m1[:], m2[:, 0:16], m2[:, 16:32], A.max)
+        zi = V(ts, [y], ti[:, 16:32], m1[:], 4096.0, None, A.mult)
+        ky = V(ts, [zi], ti[:, 48:64], ti[:, 16:32], 12, 511, A.logical_shift_right, A.bitwise_and)
+        ci = V(ts, [zi], ti[:, 32:48], ti[:, 16:32], 4095, None, A.bitwise_and)
+        kf = V(ts, [ky], ti[:, 64:80], ti[:, 48:64], float(CAP), None, A.is_le)
+        kc = V(tt, [kf, ci], ti[:, 80:96], ti[:, 64:80], ti[:, 32:48], A.mult)
+        return V(tt, [kc, n0[t]], ti[:, 96:112], ti[:, 80:96], ti[:, 0:16], A.max), zi, ky, kf
+
+    def states(t, x, xs, ps, et, h, tm, edep, deps):
+        for i in range(4):
+            m = MM(deps + [qa], ps[:, 512 * i:512 * i + P], T.aq[:, 128 * i:128 * i + 128], T.aqs[:, 128 * i:128 * i + 128], x[:], xs[:])
+            s = S([m], tm[:, P * i:P * i + P], ps[:, 512 * i:512 * i + P], F.Copy, scale=0.05)
+            a = V(tt, [s, edep], h[:, i:1024:4], tm[:, P * i:P * i + P], et[:, i:1024:4], A.add)
+        return a
+
+    ch = choose(1, T.sc[:], T.of[:, 0:64], scd + [of])
+    z = count(1, T.cn1[:, 3:1024:4], [ch])
+    cf = onto(1, z)[0]
+    ox = V(tc, [cf], T.ofx1[:], T.ti1[:, 96:112])
+    pc = V(tc, [ox], T.x1[:].bitcast(u32), T.hw[:].bitcast(u32).indirect(T.ofx1[:]))
+    pk = S([ox], T.x1s[:], T.hws[:].indirect(T.ofx1[:]), F.Copy)
+    hd = states(1, T.x1, T.x1s, T.pr, T.e1t, T.h1, T.tm1, e1, [pc, pk])
+    sr = S([ox], T.scr1[:], T.sc[:].indirect(T.ofx1[:]), F.Copy)
+    for k in (0, 1):
+        dg = G(g.affine_select, [sr], T.dg[:, 128 * k:128 * k + 128], T.scr1[:, 128 * k:128 * k + 128], [[-1, 128]], A.is_equal, 0.0, 0, 1)
+        sc1 = S([dg], T.dgo[:, 128 * k:128 * k + 128], T.dg[:, 128 * k:128 * k + 128], F.Copy, accum_out=T.scc[:, k:k + 1])
+    q1 = V(qz, [hd], T.hq[:], T.hqs[:], T.h1[:])
+    for k in (0, 1):
+        mg = MM([q1, scd[1], scd[0]], T.ps[:, 512 * k:512 * k + 128], T.hq[:, 128 * k:128 * k + 128], T.hqs[:, 128 * k:128 * k + 128], T.uq[:], T.uqs[:])
+    q1b = V(qz, [hd], T.w2[:, 0:P], T.w2s[:, 0:P], T.h1[:])
+    g1 = V(tt, [mg, sc1], T.g1c[:], T.ps[:, 0:1024:512], T.scc[:], A.add)
+
+    send_all([g1], "rg", T.g1c[:], [T.sld[rel(d, i)] for i in others])
+    og = D("y", [g1], "dog", T.sld[0], T.g1c[:])
+    s2 = D("y", [og, ("rg", 7 * neng), s20], "ds2", T.s2[0:1, :], T.sld[:])
+    c1r = S([ox, ga], T.chr1[:], T.ab[:].indirect(T.ofx1[:]), F.Copy)
+    dc1 = D("s", [c1r], "dch1", T.ch[0:1, :], T.chr1[0:1, :])
+
+    ch = choose(2, T.s2[:], T.op2, [s2, op2])
+    bc = G(g.partition_broadcast, [ch], T.cr[:], T.cn2[0:1, 3:1024:4], 128)
+    z = count(2, T.cr[:], [bc])
+    y1 = S([z, t1c], T.d1[:], T.zz2[:], F.Identity, bias=fc[:, 9:10])
+    y0 = V(ts, [z, t0c], T.d0[:], T.zz2[:], fc[:, 8:9], None, A.subtract)
+    y0 = V(red, [y0], T.rv[:, 0:1], T.d0[:], AxisListType.X, A.min, apply_absolute_value=True)
+    y1 = V(red, [y1], T.rv[:, 1:2], T.d1[:], AxisListType.X, A.min, apply_absolute_value=True)
+    rq = V(ts, [y0, y1], T.rq[:], T.rv[:], 255.0 * U, 4096.0, A.min, A.mult)
+    send_all([rq], "rr", T.rq[:], [T.rqs[:, 2 * rel(d, i):2 * rel(d, i) + 2] for i in others])
+    for k in range(8):
+        oq = D("y", [("rr", 7 * neng)], "dofq", T.ofq[16 * k:16 * k + 16, 2:16], T.rqs[d:128:8, 2:16])
+    cf, zi, ky, kf = onto(2, z)
+    ti = T.ti2
+    x = V(ts, [zi], ti[:, 112:128], ti[:, 16:32], 21, 5, A.logical_shift_right, A.arith_shift_right) if False else V(ts, [zi], ti[:, 112:128], ti[:, 16:32], 21, None, A.logical_shift_right)
+    x = V(ts, [x], ti[:, 128:144], ti[:, 112:128], 32.0, None, A.mult)
+    x = V(tt, [x, ky], ti[:, 144:160], ti[:, 128:144], ti[:, 48:64], A.add)
+    x = V(tt, [x, kf], ti[:, 160:176], ti[:, 144:160], ti[:, 64:80], A.mult)
+    y = V(ts, [x], ti[:, 176:192], ti[:, 160:176], 0.0, 223.0, A.is_gt, A.mult)
+    x = V(tt, [y], ti[:, 192:208], ti[:, 160:176], ti[:, 176:192], A.add)
+    x = V(tt, [x], ti[:, 208:224], ti[:, 192:208], ti[:, 0:16], A.max)
+    ox2 = V(tc, [x], T.ofx2[:], ti[:, 208:224])
+    pc = V(tc, [oq, q1], T.sp[:].bitcast(u32), T.hq[:].bitcast(u32).indirect(T.ofq[:, 2:16]))
+    pk = S([oq, q1], T.sps[:], T.hqs[:].indirect(T.ofq[:, 2:16]), F.Copy)
+    ca, cb = [], []
+    for i in others:
+        a, b = CAP * (rel(i, d) - 1), P + CAP * (rel(d, i) - 1)
+        ca.append((T.sp[:, a:a + CAP].bitcast(u8), T.w2[:, b:b + CAP].bitcast(u8)))
+        cb.append((T.sps[:, a:a + CAP], T.w2s[:, b:b + CAP]))
+    send_each([pc], "rc", ca)
+    send_each([pk], "rc", cb)
+    oc2 = V(tc, [cf], T.ofc2[:], ti[:, 96:112])
+    lo = V(ts, [cf], ti[:, 112:128], ti[:, 96:112], 127, None, A.bitwise_and)
+    hb = V(ts, [cf], ti[:, 128:144], ti[:, 96:112], 7, 1, A.logical_shift_right, A.bitwise_and)
+    tl = V(tt, [lo], ti[:, 144:160], ti[:, 96:112], ti[:, 112:128], A.add)
+    hm = V(ts, [hb], ti[:, 160:176], ti[:, 128:144], -127.0, None, A.mult)
+    x = V(tt, [tl, hm], ti[:, 224:240], ti[:, 144:160], ti[:, 160:176], A.add)
+    os2 = V(tc, [x], T.ofs2[:], ti[:, 224:240])
+    sr2 = S([os2], T.scr2[:], T.s2[:].indirect(T.ofs2[:]), F.Copy)
+    c2r = S([oc2, ga], T.chr2[:], T.ab[:].indirect(T.ofc2[:]), F.Copy)
+    dc2 = D("s", [c2r], "dch2", T.ch[1:2, :], T.chr2[0:1, :])
+
+    arr = ("rc", 14)
+    pc = V(tc, [arr, ox2, q1b], T.x2[:].bitcast(u32), T.w2[:, 0:480].bitcast(u32).indirect(T.ofx2[:]))
+    pk = S([arr, ox2, q1b], T.x2s[:], T.w2s[:, 0:480].indirect(T.ofx2[:]), F.Copy)
+    hd = states(2, T.x2, T.x2s, T.ps, T.e2t, T.h2, T.tm2, e2, [pc, pk, g1])
+    q2 = V(qz, [hd], T.zq[:], T.zqs[:], T.h2[:])
+    m1 = MM([q2, qw], T.ps[:, 0:P], T.wq[:], T.wqs[:], T.zq[:], T.zqs[:])
+    m2 = MM([q2], T.ps[:, 512:512 + P], T.uq[:], T.uqs[:], T.zq[:], T.zqs[:])
+    D("y", [q2], "dout", T.oc[:, :], T.zq[:].bitcast(u8))
+    yy = S([m1], T.ys[:], T.ps[:, 0:P], F.Copy)
+    gg = V(tt, [m2, sr2], T.go[0:1, :], T.ps[0:1, 512:512 + P], T.scr2[0:1, :], A.add)
+    D("y", [yy], "dout", T.y[:, :], T.ys[:])
+    for k in range(4):
+        D("y", [q2], "dout", T.osc[4 * k:4 * k + 4, :], T.zqs[32 * k:32 * k + 4, :])
+    D("y", [gg], "dout", T.g[0:1, :], T.go[0:1, :])
+
+    fin = [(n, total[n]) for n in total]
+    wait("g", fin + [("ls", lsum[0])])

@@ -2,50 +2,31 @@ from concourse.bass import DstId, RemoteDMATransfer
 from concourse.mybir import dt, AluOpType as A, AxisListType, ActivationFunctionType as F
 
 N, P, CAP = 8, 256, 32
-PRED = 4 * P
 BIG = 9e29
 U = 1.0 / 4096.0
 
-_f32 = "float32"
-SCRATCH = {
-    "e0t": ("sbuf", [128, 1024], "bfloat16"), "e1t": ("sbuf", [128, 1024], "bfloat16"), "e2t": ("sbuf", [128, 1024], "bfloat16"),
-    "ut": ("sbuf", [128, 16], "bfloat16"), "ub": ("sbuf", [128, 512], "bfloat16"), "ones": ("sbuf", [128, 128], "bfloat16"),
-    "at": ("sbuf", [128, 2048], "bfloat16"), "wt": ("sbuf", [128, 512], "bfloat16"),
-    "h1": ("sbuf", [128, 1024], "bfloat16"), "h2": ("sbuf", [128, 1024], "bfloat16"),
-    "tm1": ("sbuf", [128, 1024], _f32), "tm2": ("sbuf", [128, 1024], _f32),
-    "ps": ("psum", [128, 2048], _f32), "pr": ("psum", [128, 2048], _f32),
-    "sc": ("sbuf", [128, 2048], _f32), "s2": ("sbuf", [128, 2048], _f32),
-    "iot": ("sbuf", [128, 2048], _f32), "ab": ("sbuf", [128, 2048], _f32),
-    "rs": ("sbuf", [128, 1024], _f32), "zer": ("sbuf", [128, 256], _f32),
-    "pt": ("sbuf", [128, 128], "int32"), "pa": ("sbuf", [128, 128], "int32"), "np": ("sbuf", [128, 128], "int32"),
-    "lo": ("sbuf", [128, 64], "int32"), "hb": ("sbuf", [128, 64], "int32"), "tl": ("sbuf", [128, 64], "int32"),
-    "hm": ("sbuf", [128, 64], "int32"), "po": ("sbuf", [128, 64], "int32"),
-    "of": ("sbuf", [128, 128], "uint16"), "op2": ("sbuf", [128, 64], "uint16"),
-    "ic": ("sbuf", [128, 8], "int32"), "fc": ("sbuf", [128, 16], _f32),
-    "iy": ("sbuf", [128, 32], "int32"), "dup": ("sbuf", [128, 32], "uint16"), "dup4": ("sbuf", [128, 32], "uint16"),
-    "cr": ("sbuf", [128, 256], _f32), "d0": ("sbuf", [128, 256], _f32), "d1": ("sbuf", [128, 256], _f32),
-    "rv": ("sbuf", [128, 2], _f32), "rq": ("sbuf", [128, 2], "uint16"), "rqs": ("sbuf", [128, 16], "uint16"),
-    "ofq": ("sbuf", [128, 16], "uint16"),
-    "scr1": ("sbuf", [128, 256], _f32), "scr2": ("sbuf", [128, 256], _f32), "dg": ("sbuf", [128, 256], _f32),
-    "dgo": ("sbuf", [128, 256], _f32), "scc": ("sbuf", [128, 2], _f32), "g1c": ("sbuf", [128, 2], _f32),
-    "sld": ("dram", [8, 128, 2], _f32),
-    "chr1": ("sbuf", [128, 256], _f32), "chr2": ("sbuf", [128, 256], _f32), "go": ("sbuf", [128, 256], _f32),
-    "ys": ("sbuf", [128, 256], _f32),
-    "ofx1": ("sbuf", [128, 16], "uint16"), "ofx2": ("sbuf", [128, 16], "uint16"), "ofs2": ("sbuf", [128, 16], "uint16"),
-    "ofc2": ("sbuf", [128, 16], "uint16"),
-}
+_f32, _i32, _u16, _bf = "float32", "int32", "uint16", "bfloat16"
+SCRATCH = {"ps": ("psum", [128, 2048], _f32), "pr": ("psum", [128, 2048], _f32), "sld": ("dram", [8, 128, 2], _f32)}
+for _d, _l in (
+        (_bf, "e0t 1024 e1t 1024 e2t 1024 ut 16 ub 512 ones 128 at 2048 wt 512 h1 1024 h2 1024"),
+        (_f32, "tm1 1024 tm2 1024 sc 2048 s2 2048 iot 2048 ab 2048 rs 512 zer 256 ta 32 sb 32 tb 32 ct3 128 cc 128 cct 128 cx 256 "
+               "fc 16 cr 256 d0 256 d1 256 rv 2 scr1 256 scr2 256 dg 256 dgo 256 scc 2 g1c 2 chr1 256 chr2 256 go 256 ys 256"),
+        (_i32, "pt 64 pa 64 np 64 lo 32 hb 32 tl 32 hm 32 po 32 iz 16 ic 8 iy 32 ti1 256 ti2 256"),
+        (_u16, "of 64 op2 32 rj 16 dup 32 dup4 32 rq 2 rqs 16 ofq 16 ofx1 16 ofx2 16 ofs2 16 ofc2 16")):
+    _w = _l.split()
+    for _k in range(0, len(_w), 2):
+        SCRATCH[_w[_k]] = ("sbuf", [128, int(_w[_k + 1])], _d)
 for _n, _c in (("uq", 128), ("aq", 512), ("wq", 128), ("hw", 2048), ("x1", 256), ("hq", 256), ("sp", 224), ("w2", 512), ("x2", 256), ("zq", 256)):
     SCRATCH[_n] = ("sbuf", [128, _c], "float8_e4m3fn_x4")
     SCRATCH[_n + "s"] = ("sbuf", [128, _c], "uint8")
 for _t in ("1", "2"):
-    for _n, _c in (("ga", 1024), ("mx", 1024), ("fl", 1024), ("cn", 1024), ("nr", 1024), ("vd", 1024),
-                   ("ad", 256), ("mk", 256), ("ct", 256), ("kb", 256), ("zz", 256), ("ex", 512), ("tr", 512), ("nx", 512), ("nt", 512),
+    for _n, _c in (("ga", 512), ("mx", 512), ("fl", 512), ("cn", 512), ("nr", 512), ("vd", 512),
+                   ("ad", 256), ("mk", 256), ("ct", 256), ("kb", 256), ("zz", 256), ("ex", 512), ("tr", 512), ("nx", 256), ("nt", 256),
                    ("m4", 64), ("m2", 32), ("m1", 16)):
         SCRATCH[_n + _t] = ("sbuf", [128, _c], _f32)
-    SCRATCH["ti" + _t] = ("sbuf", [128, 16 * 16], "int32")
 
-SEMAPHORES = ["cv", "cs", "ct", "cg", "ls", "rg", "rr", "rc"] + ["h%d" % i for i in range(N)]
-SEMAPHORES += ["de0", "du", "dp1", "dp2", "da", "de1", "dw", "de2", "dog", "ds2", "dofq", "dch1", "dch2", "dout"]
+SEMAPHORES = ["cv", "cs", "ct", "cg", "l0", "ls", "rg", "rr", "rc"] + ["h%d" % i for i in range(N)]
+SEMAPHORES += ["de0", "du", "dp1", "dp2", "da", "de1", "dw", "de2", "dog", "ds2", "ds3", "dofq", "dch1", "dch2", "dout"]
 
 
 def rank_program(g, core, T, topo):
@@ -91,7 +72,7 @@ def rank_program(g, core, T, topo):
         return note(Q[q].dma_start(out, in_), name, 16)
 
     tt, ts, tc = g.vector.tensor_tensor, g.vector.tensor_scalar, g.vector.tensor_copy
-    ms, qz, scan, red = g.vector.memset, g.vector.quantize_mx, g.vector.tensor_tensor_scan, g.vector.tensor_reduce
+    ms, qz, scan, red, tp = g.vector.memset, g.vector.quantize_mx, g.vector.tensor_tensor_scan, g.vector.tensor_reduce, g.vector.transpose
     u8, u32 = dt.uint8, dt.uint32
 
     others = [(d + k) % N for k in range(1, N)]
@@ -104,19 +85,22 @@ def rank_program(g, core, T, topo):
         mask &= topo.mask(core, cores[i])
     engs = [e for e in topo.engines(core, cores[others[0]]) if mask >> e & 1]
     neng = len(engs)
-    lsum = [0]
 
-    def send_all(deps, sem, src, dsts):
+    def sent(name, n):
+        total[name] = total.get(name, 0) + n
+        return (name, total[name])
+
+    def send_all(deps, sem, src, dsts, local="ls"):
         wait("g", deps)
         g.remote_dma_fused([RemoteDMATransfer(dst_ids=ids, dma_engine_mask=mask, remote_sem=T.sem[sem], srcs=[src], dsts=dsts)],
-                           local_sem=T.sem.ls)
-        lsum[0] += neng
+                           local_sem=T.sem[local])
+        return sent(local, neng)
 
     def send_each(deps, sem, pairs):
         wait("g", deps)
         g.remote_dma_fused([RemoteDMATransfer(dst_ids=[ids[k]], dma_engine_mask=1 << engs[k], remote_sem=T.sem[sem], srcs=[a], dsts=[b])
                             for k, (a, b) in enumerate(pairs)], local_sem=T.sem.ls)
-        lsum[0] += len(pairs)
+        return sent("ls", len(pairs))
 
     def rel(s, r):
         return (s - r) % N
@@ -124,25 +108,26 @@ def rank_program(g, core, T, topo):
     e0 = D("y", [], "de0", T.e0t[:], T.e0[:, :])
     uu = D("y", [], "du", T.ut[:, 0:8], T.u[:, 0:8])
     for k in range(8):
-        p1 = D("y", [], "dp1", T.pt[16 * k:16 * k + 16, 0:64], T.p1[:, :])
+        p1 = D("y", [], "dp1", T.pt[16 * k:16 * k + 16, 0:32], T.p1[:, 32 * (k % 2):32 * (k % 2) + 32])
     for k in range(8):
-        p2 = D("y", [], "dp2", T.pt[16 * k:16 * k + 16, 64:128], T.p2[:, :])
-    da = D("s", [], "da", T.at[:], T.a[:, :])
-    e1 = D("s", [], "de1", T.e1t[:], T.e1[:, :])
-    e2 = D("s", [], "de2", T.e2t[:], T.e2[:, :])
-    dw = D("s", [], "dw", T.wt[:], T.w[:, :])
+        p2 = D("y", [], "dp2", T.pt[16 * k:16 * k + 16, 32:64], T.p2[:, 32 * (k % 2):32 * (k % 2) + 32])
+    da = D("y", [e0], "da", T.at[:], T.a[:, :])
 
     gp = G(g.iota, [], T.ic[:, 0:1], [[0, 1]], 0, 1)
     giy = G(g.iota, [], T.iy[:], [[16, 16], [0, 2]], 0, 0)
+    giz = G(g.iota, [], T.iz[:], [[16, 2], [32, 4], [0, 2]], 0, 0)
     on = V(ms, [], T.ones[:], 1.0)
     q0 = V(qz, [e0], T.hw[:, 0:P], T.hws[:, 0:P], T.e0t[:])
-    send_all([q0], "h%d" % d, T.hw[:, 0:P].bitcast(u8), [T.hw[:, P * rel(d, i):P * rel(d, i) + P].bitcast(u8) for i in others])
-    send_all([q0], "h%d" % d, T.hws[:, 0:P], [T.hws[:, P * rel(d, i):P * rel(d, i) + P] for i in others])
+    send_all([q0], "h%d" % d, T.hw[:, 0:P].bitcast(u8), [T.hw[:, P * rel(d, i):P * rel(d, i) + P].bitcast(u8) for i in others], "l0")
+    l0 = send_all([q0], "h%d" % d, T.hws[:, 0:P], [T.hws[:, P * rel(d, i):P * rel(d, i) + P] for i in others], "l0")
     gi = G(g.iota, [], T.iot[:], [[1, 2048]], 0, 0, allow_small_or_imprecise_dtypes=True)
     cut = 2048 - P * d
     ga = G(g.iota, [], T.ab[:, 0:cut], [[1, cut]], P * d, 0, allow_small_or_imprecise_dtypes=True)
     if d:
         ga = G(g.iota, [], T.ab[:, cut:2048], [[1, 2048 - cut]], 0, 0, allow_small_or_imprecise_dtypes=True)
+    e1 = D("y", [l0], "de1", T.e1t[:], T.e1[:, :])
+    e2 = D("y", [l0], "de2", T.e2t[:], T.e2[:, :])
+    dw = D("y", [l0], "dw", T.wt[:], T.w[:, :])
 
     for k in range(4):
         ubk = V(ts, [on, uu], T.ub[:, k:512:4], T.ones[:], T.ut[:, k:k + 1], None, A.mult)
@@ -151,7 +136,7 @@ def rank_program(g, core, T, topo):
     x = V(ts, [p1, p2], T.pa[:], T.pt[:], float(2048 - P * d), None, A.add)
     x = V(ts, [x], T.np[:], T.pa[:], 2047, None, A.bitwise_and)
     of = V(tc, [x], T.of[:], T.np[:])
-    n2 = T.np[:, 64:128]
+    n2 = T.np[:, 32:64]
     a1 = V(ts, [x], T.lo[:], n2, 127, None, A.bitwise_and)
     a2 = V(ts, [x], T.hb[:], n2, 7, 1, A.logical_shift_right, A.bitwise_and)
     a3 = V(tt, [a1], T.tl[:], n2, T.lo[:], A.add)
@@ -160,7 +145,7 @@ def rank_program(g, core, T, topo):
     op2 = V(tc, [a5], T.op2[:], T.po[:])
     nr = {}
     for t in (1, 2):
-        nr[t] = S([gi, of], T["nr%d" % t][:], T.iot[:].indirect(T.of[:, 64 * t - 64:64 * t]), F.Copy, scale=U)
+        nr[t] = S([gi, of], T["nr%d" % t][:], T.iot[:].indirect(T.of[:, 32 * t - 32:32 * t]), F.Copy, scale=U)
 
     ic, fc = T.ic, T.fc
     b1 = V(ts, [gp], ic[:, 1:2], ic[:, 0:1], 7, None, A.bitwise_and)
@@ -178,55 +163,78 @@ def rank_program(g, core, T, topo):
     t1c = V(ts, [t0c], fc[:, 9:10], fc[:, 8:9], -1.0, -16.0, A.mult, A.add)
     dup = V(ts, [b6, giy], T.dup[:], T.iy[:], fc[:, 2:3], None, A.add)
     dup4 = V(ts, [b6, giy], T.dup4[:], T.iy[:], fc[:, 2:3], 4.0, A.add, A.mult)
+    rj = V(tc, [giz], T.rj[:], T.iz[:])
     r1 = V(ms, [], T.rs[:], BIG)
-    rs = V(ms, [r1], T.rs[:, 0:1024:4], -BIG)
+    rs = V(ms, [r1], T.rs[:, 0:512:4], -BIG)
     zr = V(ms, [], T.zer[:], 0.0)
+    sb0 = V(ms, [], T.sb[:], 0.0)
     fl0 = {t: V(ms, [], T["fl%d" % t][:], 0.0) for t in (1, 2)}
     qa = V(qz, [da], T.aq[:], T.aqs[:], T.at[:])
+    s20 = V(ms, [], T.s2[:], 0.0)
     vd, n0 = {}, {}
     for t in (1, 2):
         r, v = T["nr%d" % t], T["vd%d" % t]
-        z = V(tt, [nr[t]], v[:, 0:1023], r[:, 0:1023], r[:, 1:1024], A.subtract)
-        vd[t] = V(tc, [z], v[:, 3:1024:4], r[:, 3:1024:4])
-        z = S([nr[t], dup4], T["nx%d" % t][:], r[:].indirect(T.dup4[:]), F.Copy)
-        z = V(g.vector.transpose, [z], T["nt%d" % t][:], T["nx%d" % t][:])
-        n0[t] = V(ts, [z], T["ti%d" % t][:, 0:16], T["nt%d" % t][:, 0:512:32], 4096.0, None, A.mult)
-    s20 = V(ms, [], T.s2[:], 0.0)
-    qw = V(qz, [dw], T.wq[:], T.wqs[:], T.wt[:])
+        z = V(tt, [nr[t]], v[:, 0:511], r[:, 0:511], r[:, 1:512], A.subtract)
+        vd[t] = V(tc, [z], v[:, 3:512:4], r[:, 3:512:4])
+        z = S([nr[t], dup4], T["nx%d" % t][:], r[:].indirect(T.dup4[:, 0:16]), F.Copy)
+        z = V(tp, [z], T["nt%d" % t][:], T["nx%d" % t][:])
+        if t == 1:
+            n0[t] = V(ts, [z], T.ti1[:, 0:16], T.nt1[:, 0:256:16], 4096.0, None, A.mult)
+        else:
+            n0[t] = V(ts, [z], T.ti2[:, 0:8], T.nt2[:, 0:256:32], 4096.0, None, A.mult)
+            n0[t] = V(ts, [z], T.ti2[:, 8:16], T.nt2[:, 16:256:32], 4096.0, None, A.mult)
 
     scd = []
-    for b in range(4):
-        deps = [quq, q0]
-        for k in (2 * b, 2 * b + 1):
-            if k:
-                deps.append(("h%d" % ((d + k) % N), 2 * neng))
-        mt = MM(deps, T.ps[:, 512 * b:512 * b + 512], T.uq[:], T.uqs[:], T.hw[:, 512 * b:512 * b + 512], T.hws[:, 512 * b:512 * b + 512])
-        o, i = T.sc[:, 512 * b:512 * b + 512], T.ps[:, 512 * b:512 * b + 512]
-        scd.append(V(tc, [mt], o, i) if b % 2 else S([mt], o, i, F.Copy))
+    for j, k in enumerate([0] + list(range(N - 1, 0, -1))):
+        b = j % 4
+        deps = [quq, q0] + ([("h%d" % ((d + k) % N), 2 * neng)] if k else []) + ([scd[j - 4]] if j > 3 else [])
+        mt = MM(deps, T.ps[:, 512 * b:512 * b + P], T.uq[:], T.uqs[:], T.hw[:, P * k:P * k + P], T.hws[:, P * k:P * k + P])
+        o, i = T.sc[:, P * k:P * k + P], T.ps[:, 512 * b:512 * b + P]
+        scd.append(V(tc, [mt], o, i) if j % 2 else S([mt], o, i, F.Copy))
 
     def choose(t, win, off, deps):
         ga_, mx_, fl_, cn_ = T["ga%d" % t], T["mx%d" % t], T["fl%d" % t], T["cn%d" % t]
-        x1 = V(tc, deps, ga_[:, 0:512], win.indirect(off[:, 0:32]))
-        x2 = S(deps, ga_[:, 512:1024], win.indirect(off[:, 32:64]), F.Copy)
+        x1 = V(tc, deps, ga_[:, 0:256], win.indirect(off[:, 0:16]))
+        x2 = S(deps, ga_[:, 256:512], win.indirect(off[:, 16:32]), F.Copy)
         m = V(scan, [x1, x2, rs], mx_[:], T.rs[:], ga_[:], -BIG, A.min, A.max)
         for k in (1, 2, 3):
-            f = V(tt, [m, fl0[t]], fl_[:, k:1024:4], ga_[:, k:1024:4], mx_[:, k - 1:1024:4], A.is_le)
+            f = V(tt, [m, fl0[t]], fl_[:, k:512:4], ga_[:, k:512:4], mx_[:, k - 1:512:4], A.is_le)
         return V(scan, [f, vd[t]], cn_[:], fl_[:], T["vd%d" % t][:], 0.0, A.mult, A.add)
 
-    def count(t, c, deps):
-        x = S(deps + [nbc], T["ad%d" % t][:], c, F.Abs, bias=fc[:, 5:6])
-        x = V(ts, [x], T["mk%d" % t][:], T["ad%d" % t][:], 128.0 * U, None, A.is_lt)
-        x = V(scan, [x, zr, i5c], T["ct%d" % t][:], T["mk%d" % t][:], T.zer[:], fc[:, 6:7], A.add, A.add)
-        x = V(tt, [x], T["kb%d" % t][:], T["mk%d" % t][:], T["ct%d" % t][:], A.mult)
-        return V(tt, [x] + deps, T["zz%d" % t][:], T["kb%d" % t][:], c, A.add)
+    def count1(c, deps):
+        x = S(deps + [nbc], T.ad1[:, 0:128], c, F.Abs, bias=fc[:, 5:6])
+        x = V(ts, [x], T.mk1[:, 0:128], T.ad1[:, 0:128], 128.0 * U, None, A.is_lt)
+        x = V(scan, [x, zr], T.ct1[:, 0:128], T.mk1[:, 0:128], T.zer[:, 0:128], 0.0, A.add, A.add)
+        x = V(tp, [x], T.ta[:], T.ct1[:, 96:128])
+        x = V(tc, [x, sb0], T.sb[:, 16:32], T.ta[:, 0:16])
+        x = V(tp, [x], T.tb[:], T.sb[:])
+        x = V(ts, [x, i5c], T.ct3[:], T.ct1[:, 0:128], T.tb[:, 31:32], fc[:, 6:7], A.add, A.add)
+        x = V(tt, [x], T.kb1[:, 0:128], T.mk1[:, 0:128], T.ct3[:], A.mult)
+        return V(tt, [x] + deps, T.zz1[:, 0:128], T.kb1[:, 0:128], c, A.add)
+
+    def whole(cn, deps):
+        x = V(tc, deps, T.cc[:], cn)
+        x = V(tp, [x], T.cct[:], T.cc[:])
+        x1 = V(tc, [x, rj], T.cx[:, 0:128], T.cct[:].indirect(T.rj[:, 0:8]))
+        x2 = S([x, rj], T.cx[:, 128:256], T.cct[:].indirect(T.rj[:, 8:16]), F.Copy)
+        return V(tp, [x1, x2], T.cr[:], T.cx[:])
+
+    def count2(c, deps):
+        x = S(deps + [nbc], T.ad2[:], c, F.Abs, bias=fc[:, 5:6])
+        x = V(ts, [x], T.mk2[:], T.ad2[:], 128.0 * U, None, A.is_lt)
+        x = V(scan, [x, zr, i5c], T.ct2[:], T.mk2[:], T.zer[:], fc[:, 6:7], A.add, A.add)
+        x = V(tt, [x], T.kb2[:], T.mk2[:], T.ct2[:], A.mult)
+        return V(tt, [x] + deps, T.zz2[:], T.kb2[:], c, A.add)
 
     def onto(t, z):
         ex, tr, m4, m2, m1, ti = [T[n + str(t)] for n in ("ex", "tr", "m4", "m2", "m1", "ti")]
-        x1 = V(tc, [z, dup], ex[:, 0:256], T["zz%d" % t][:].indirect(T.dup[:, 0:16]))
-        x2 = S([z, dup], ex[:, 256:512], T["zz%d" % t][:].indirect(T.dup[:, 16:32]), F.Copy)
-        x = V(g.vector.transpose, [x1, x2], tr[:], ex[:])
+        w = P * t
+        zz = T["zz%d" % t][:, 0:w // 2]
+        x1 = V(tc, [z, dup], ex[:, 0:w // 2], zz.indirect(T.dup[:, 0:8 * t]))
+        x2 = S([z, dup], ex[:, w // 2:w], zz.indirect(T.dup[:, 8 * t:16 * t]), F.Copy)
+        x = V(tp, [x1, x2], tr[:, 0:w], ex[:, 0:w])
         for k in range(4):
-            y = V(tt, [x], m4[:, 16 * k:16 * k + 16], tr[:, k:512:32], tr[:, k + 4:512:32], A.max)
+            y = V(tt, [x], m4[:, 16 * k:16 * k + 16], tr[:, k:w:16 * t], tr[:, k + 4:w:16 * t], A.max)
         y = V(tt, [y], m2[:], m4[:, 0:32], m4[:, 32:64], A.max)
         y = V(tt, [y], m1[:], m2[:, 0:16], m2[:, 16:32], A.max)
         zi = V(ts, [y], ti[:, 16:32], m1[:], 4096.0, None, A.mult)
@@ -236,39 +244,41 @@ def rank_program(g, core, T, topo):
         kc = V(tt, [kf, ci], ti[:, 80:96], ti[:, 64:80], ti[:, 32:48], A.mult)
         return V(tt, [kc, n0[t]], ti[:, 96:112], ti[:, 80:96], ti[:, 0:16], A.max), zi, ky, kf
 
-    def states(t, x, xs, ps, et, h, tm, edep, deps):
+    def states(x, xs, ps, et, h, tm, edep, deps):
         for i in range(4):
             m = MM(deps + [qa], ps[:, 512 * i:512 * i + P], T.aq[:, 128 * i:128 * i + 128], T.aqs[:, 128 * i:128 * i + 128], x[:], xs[:])
             s = S([m], tm[:, P * i:P * i + P], ps[:, 512 * i:512 * i + P], F.Copy, scale=0.05)
             a = V(tt, [s, edep], h[:, i:1024:4], tm[:, P * i:P * i + P], et[:, i:1024:4], A.add)
         return a
 
-    ch = choose(1, T.sc[:], T.of[:, 0:64], scd + [of])
-    z = count(1, T.cn1[:, 3:1024:4], [ch])
+    ch = choose(1, T.sc[:], T.of[:, 0:32], scd + [of])
+    z = count1(T.cn1[:, 3:512:4], [ch])
     cf = onto(1, z)[0]
-    ox = V(tc, [cf], T.ofx1[:], T.ti1[:, 96:112])
+    ox = V(tc, [cf], T.ofx1[:, 0:8], T.ti1[:, 96:112:2])
+    ox = V(tc, [cf], T.ofx1[:, 8:16], T.ti1[:, 97:112:2])
     pc = V(tc, [ox], T.x1[:].bitcast(u32), T.hw[:].bitcast(u32).indirect(T.ofx1[:]))
     pk = S([ox], T.x1s[:], T.hws[:].indirect(T.ofx1[:]), F.Copy)
-    hd = states(1, T.x1, T.x1s, T.pr, T.e1t, T.h1, T.tm1, e1, [pc, pk])
+    hd = states(T.x1, T.x1s, T.pr, T.e1t, T.h1, T.tm1, e1, [pc, pk])
     sr = S([ox], T.scr1[:], T.sc[:].indirect(T.ofx1[:]), F.Copy)
     for k in (0, 1):
         dg = G(g.affine_select, [sr], T.dg[:, 128 * k:128 * k + 128], T.scr1[:, 128 * k:128 * k + 128], [[-1, 128]], A.is_equal, 0.0, 0, 1)
         sc1 = S([dg], T.dgo[:, 128 * k:128 * k + 128], T.dg[:, 128 * k:128 * k + 128], F.Copy, accum_out=T.scc[:, k:k + 1])
+    c1r = S([ox, ga], T.chr1[:], T.ab[:].indirect(T.ofx1[:]), F.Copy)
     q1 = V(qz, [hd], T.hq[:], T.hqs[:], T.h1[:])
     for k in (0, 1):
-        mg = MM([q1, scd[1], scd[0]], T.ps[:, 512 * k:512 * k + 128], T.hq[:, 128 * k:128 * k + 128], T.hqs[:, 128 * k:128 * k + 128], T.uq[:], T.uqs[:])
+        mg = MM([q1] + scd, T.ps[:, 512 * k:512 * k + 128], T.hq[:, 128 * k:128 * k + 128], T.hqs[:, 128 * k:128 * k + 128], T.uq[:], T.uqs[:])
     q1b = V(qz, [hd], T.w2[:, 0:P], T.w2s[:, 0:P], T.h1[:])
     g1 = V(tt, [mg, sc1], T.g1c[:], T.ps[:, 0:1024:512], T.scc[:], A.add)
 
+    dc1 = D("s", [c1r], "dch1", T.ch[0:1, :], T.chr1[0:1, :])
     send_all([g1], "rg", T.g1c[:], [T.sld[rel(d, i)] for i in others])
     og = D("y", [g1], "dog", T.sld[0], T.g1c[:])
-    s2 = D("y", [og, ("rg", 7 * neng), s20], "ds2", T.s2[0:1, :], T.sld[:])
-    c1r = S([ox, ga], T.chr1[:], T.ab[:].indirect(T.ofx1[:]), F.Copy)
-    dc1 = D("s", [c1r], "dch1", T.ch[0:1, :], T.chr1[0:1, :])
+    qw = V(qz, [dw], T.wq[:], T.wqs[:], T.wt[:])
+    for k in range(8):
+        D("ys"[k % 2], [og, ("rg", 7 * neng), s20], ("ds2", "ds3")[k % 2], T.s2[16 * k:16 * k + 1, :], T.sld[:])
 
-    ch = choose(2, T.s2[:], T.op2, [s2, op2])
-    bc = G(g.partition_broadcast, [ch], T.cr[:], T.cn2[0:1, 3:1024:4], 128)
-    z = count(2, T.cr[:], [bc])
+    ch = choose(2, T.s2[:], T.op2, [("ds2", 64), ("ds3", 64), op2])
+    z = count2(T.cr[:], [whole(T.cn2[:, 3:512:4], [ch])])
     y1 = S([z, t1c], T.d1[:], T.zz2[:], F.Identity, bias=fc[:, 9:10])
     y0 = V(ts, [z, t0c], T.d0[:], T.zz2[:], fc[:, 8:9], None, A.subtract)
     y0 = V(red, [y0], T.rv[:, 0:1], T.d0[:], AxisListType.X, A.min, apply_absolute_value=True)
@@ -279,7 +289,7 @@ def rank_program(g, core, T, topo):
         oq = D("y", [("rr", 7 * neng)], "dofq", T.ofq[16 * k:16 * k + 16, 2:16], T.rqs[d:128:8, 2:16])
     cf, zi, ky, kf = onto(2, z)
     ti = T.ti2
-    x = V(ts, [zi], ti[:, 112:128], ti[:, 16:32], 21, 5, A.logical_shift_right, A.arith_shift_right) if False else V(ts, [zi], ti[:, 112:128], ti[:, 16:32], 21, None, A.logical_shift_right)
+    x = V(ts, [zi], ti[:, 112:128], ti[:, 16:32], 21, None, A.logical_shift_right)
     x = V(ts, [x], ti[:, 128:144], ti[:, 112:128], 32.0, None, A.mult)
     x = V(tt, [x, ky], ti[:, 144:160], ti[:, 128:144], ti[:, 48:64], A.add)
     x = V(tt, [x, kf], ti[:, 160:176], ti[:, 144:160], ti[:, 64:80], A.mult)
@@ -310,7 +320,7 @@ def rank_program(g, core, T, topo):
     arr = ("rc", 14)
     pc = V(tc, [arr, ox2, q1b], T.x2[:].bitcast(u32), T.w2[:, 0:480].bitcast(u32).indirect(T.ofx2[:]))
     pk = S([arr, ox2, q1b], T.x2s[:], T.w2s[:, 0:480].indirect(T.ofx2[:]), F.Copy)
-    hd = states(2, T.x2, T.x2s, T.ps, T.e2t, T.h2, T.tm2, e2, [pc, pk, g1])
+    hd = states(T.x2, T.x2s, T.ps, T.e2t, T.h2, T.tm2, e2, [pc, pk, g1])
     q2 = V(qz, [hd], T.zq[:], T.zqs[:], T.h2[:])
     m1 = MM([q2, qw], T.ps[:, 0:P], T.wq[:], T.wqs[:], T.zq[:], T.zqs[:])
     m2 = MM([q2], T.ps[:, 512:512 + P], T.uq[:], T.uqs[:], T.zq[:], T.zqs[:])
@@ -319,8 +329,7 @@ def rank_program(g, core, T, topo):
     gg = V(tt, [m2, sr2], T.go[0:1, :], T.ps[0:1, 512:512 + P], T.scr2[0:1, :], A.add)
     D("y", [yy], "dout", T.y[:, :], T.ys[:])
     for k in range(4):
-        D("y", [q2], "dout", T.osc[4 * k:4 * k + 4, :], T.zqs[32 * k:32 * k + 4, :])
+        D("s", [q2], "dch2", T.osc[4 * k:4 * k + 4, :], T.zqs[32 * k:32 * k + 4, :])
     D("y", [gg], "dout", T.g[0:1, :], T.go[0:1, :])
 
-    fin = [(n, total[n]) for n in total]
-    wait("g", fin + [("ls", lsum[0])])
+    wait("g", [(n, total[n]) for n in total])

@@ -9,9 +9,10 @@ _f32, _i32, _u16, _bf = "float32", "int32", "uint16", "bfloat16"
 SCRATCH = {"ps": ("psum", [128, 2048], _f32), "pr": ("psum", [128, 2048], _f32), "sld": ("dram", [8, 128, 2], _f32)}
 for _d, _l in (
         (_bf, "e0t 1024 e1t 1024 e2t 1024 ut 16 ub 512 ones 128 at 2048 wt 512 h1 1024 h2 1024"),
-        (_f32, "tm1 1024 tm2 1024 sc 2048 s2 2048 iot 2048 ab 2048 rs 512 zer 256 ta 32 sb 32 tb 32 ct3 128 cc 128 cct 128 cx 256 "
-               "fc 16 cr 256 d0 256 d1 256 rv 2 scr1 256 scr2 256 dg 256 dgo 256 scc 2 g1c 2 chr1 256 chr2 256 go 256 ys 256"),
-        (_i32, "pt 64 pa 64 np 64 lo 32 hb 32 tl 32 hm 32 po 32 iz 16 ic 8 iy 32 ti1 256 ti2 256"),
+        (_f32, "tm1 1024 tm2 1024 sc 2048 s2 2048 iot 2048 ab 2048 rs 512 zer 256 ta 32 sb 32 tb 32 nq 128 cc 128 cct 128 cx 256 "
+               "fc 16 cr 256 ca 256 cb 256 d0 256 d1 256 rv 2 scr1 256 scr2 256 dg 256 dgo 256 scc 2 g1c 2 chr1 256 chr2 256 go 256 ys 256 "
+               "mc 128 mn 128 k2 128 nx2 256 nt2 256"),
+        (_i32, "pt 64 pa 64 np 64 lo 32 hb 32 tl 32 hm 32 po 32 iz 16 ic 8 iy 32 ti 256"),
         (_u16, "of 64 op2 32 rj 16 dup 32 dup4 32 rq 2 rqs 16 ofq 16 ofx1 16 ofx2 16 ofs2 16 ofc2 16")):
     _w = _l.split()
     for _k in range(0, len(_w), 2):
@@ -21,9 +22,9 @@ for _n, _c in (("uq", 128), ("aq", 512), ("wq", 128), ("hw", 2048), ("x1", 256),
     SCRATCH[_n + "s"] = ("sbuf", [128, _c], "uint8")
 for _t in ("1", "2"):
     for _n, _c in (("ga", 512), ("mx", 512), ("fl", 512), ("cn", 512), ("nr", 512), ("vd", 512),
-                   ("ad", 256), ("mk", 256), ("ct", 256), ("kb", 256), ("zz", 256), ("ex", 512), ("tr", 512), ("nx", 256), ("nt", 256),
-                   ("m4", 64), ("m2", 32), ("m1", 16)):
+                   ("ad", 256), ("mk", 256), ("ct", 256), ("zz", 256), ("ex", 512), ("tr", 512), ("m4", 64), ("m2", 32), ("m1", 16)):
         SCRATCH[_n + _t] = ("sbuf", [128, _c], _f32)
+SCRATCH["kb2"] = ("sbuf", [128, 256], _f32)
 
 SEMAPHORES = ["cv", "cs", "ct", "cg", "l0", "ls", "rg", "rr", "rc"] + ["h%d" % i for i in range(N)]
 SEMAPHORES += ["de0", "du", "dp1", "dp2", "da", "de1", "dw", "de2", "dog", "ds2", "ds3", "dofq", "dch1", "dch2", "dout"]
@@ -113,18 +114,16 @@ def rank_program(g, core, T, topo):
         p2 = D("y", [], "dp2", T.pt[16 * k:16 * k + 16, 32:64], T.p2[:, 32 * (k % 2):32 * (k % 2) + 32])
     da = D("y", [e0], "da", T.at[:], T.a[:, :])
 
+    gi = G(g.iota, [], T.iot[:, 0:512], [[1, 512]], 0, 0, allow_small_or_imprecise_dtypes=True)
     gp = G(g.iota, [], T.ic[:, 0:1], [[0, 1]], 0, 1)
     giy = G(g.iota, [], T.iy[:], [[16, 16], [0, 2]], 0, 0)
     giz = G(g.iota, [], T.iz[:], [[16, 2], [32, 4], [0, 2]], 0, 0)
+    for k in (1, 2, 3):
+        io = S([gi], T.iot[:, 512 * k:512 * k + 512], T.iot[:, 0:512], F.Identity, bias=512.0 * k)
     on = V(ms, [], T.ones[:], 1.0)
     q0 = V(qz, [e0], T.hw[:, 0:P], T.hws[:, 0:P], T.e0t[:])
     send_all([q0], "h%d" % d, T.hw[:, 0:P].bitcast(u8), [T.hw[:, P * rel(d, i):P * rel(d, i) + P].bitcast(u8) for i in others], "l0")
     l0 = send_all([q0], "h%d" % d, T.hws[:, 0:P], [T.hws[:, P * rel(d, i):P * rel(d, i) + P] for i in others], "l0")
-    gi = G(g.iota, [], T.iot[:], [[1, 2048]], 0, 0, allow_small_or_imprecise_dtypes=True)
-    cut = 2048 - P * d
-    ga = G(g.iota, [], T.ab[:, 0:cut], [[1, cut]], P * d, 0, allow_small_or_imprecise_dtypes=True)
-    if d:
-        ga = G(g.iota, [], T.ab[:, cut:2048], [[1, 2048 - cut]], 0, 0, allow_small_or_imprecise_dtypes=True)
     e1 = D("y", [l0], "de1", T.e1t[:], T.e1[:, :])
     e2 = D("y", [l0], "de2", T.e2t[:], T.e2[:, :])
     dw = D("y", [l0], "dw", T.wt[:], T.w[:, :])
@@ -145,7 +144,7 @@ def rank_program(g, core, T, topo):
     op2 = V(tc, [a5], T.op2[:], T.po[:])
     nr = {}
     for t in (1, 2):
-        nr[t] = S([gi, of], T["nr%d" % t][:], T.iot[:].indirect(T.of[:, 32 * t - 32:32 * t]), F.Copy, scale=U)
+        nr[t] = S([gi, io, of], T["nr%d" % t][:], T.iot[:].indirect(T.of[:, 32 * t - 32:32 * t]), F.Copy, scale=U)
 
     ic, fc = T.ic, T.fc
     b1 = V(ts, [gp], ic[:, 1:2], ic[:, 0:1], 7, None, A.bitwise_and)
@@ -156,6 +155,7 @@ def rank_program(g, core, T, topo):
     b6 = V(tc, [b3, b4, b5], fc[:, 0:3], ic[:, 3:6])
     c1 = V(ts, [b6], fc[:, 3:4], fc[:, 0:1], -256.0 * U, -127.5 * U, A.mult, A.add)
     c2 = V(ts, [b6], fc[:, 4:5], fc[:, 0:1], 0.0, -100.0, A.is_equal, A.mult)
+    c4 = V(ts, [b6], fc[:, 10:11], fc[:, 0:1], 0.0, None, A.is_equal)
     nbc = V(tt, [c1, c2], fc[:, 5:6], fc[:, 3:4], fc[:, 4:5], A.add)
     i5c = V(ts, [b6], fc[:, 6:7], fc[:, 0:1], 512.0, None, A.mult)
     c3 = V(ts, [b6], fc[:, 7:8], fc[:, 0:1], 512.0 + 256.0 * U, 1.0, A.mult, A.add)
@@ -169,20 +169,22 @@ def rank_program(g, core, T, topo):
     zr = V(ms, [], T.zer[:], 0.0)
     sb0 = V(ms, [], T.sb[:], 0.0)
     fl0 = {t: V(ms, [], T["fl%d" % t][:], 0.0) for t in (1, 2)}
-    qa = V(qz, [da], T.aq[:], T.aqs[:], T.at[:])
-    s20 = V(ms, [], T.s2[:], 0.0)
-    vd, n0 = {}, {}
+    vd = {}
     for t in (1, 2):
         r, v = T["nr%d" % t], T["vd%d" % t]
         z = V(tt, [nr[t]], v[:, 0:511], r[:, 0:511], r[:, 1:512], A.subtract)
         vd[t] = V(tc, [z], v[:, 3:512:4], r[:, 3:512:4])
-        z = S([nr[t], dup4], T["nx%d" % t][:], r[:].indirect(T.dup4[:, 0:16]), F.Copy)
-        z = V(tp, [z], T["nt%d" % t][:], T["nx%d" % t][:])
-        if t == 1:
-            n0[t] = V(ts, [z], T.ti1[:, 0:16], T.nt1[:, 0:256:16], 4096.0, None, A.mult)
-        else:
-            n0[t] = V(ts, [z], T.ti2[:, 0:8], T.nt2[:, 0:256:32], 4096.0, None, A.mult)
-            n0[t] = V(ts, [z], T.ti2[:, 8:16], T.nt2[:, 16:256:32], 4096.0, None, A.mult)
+    nq = V(ts, [nr[1], c4], T.nq[:], T.nr1[:, 0:512:4], fc[:, 10:11], None, A.mult)
+    z = S([nr[2], dup4], T.nx2[:], T.nr2[:].indirect(T.dup4[:, 0:16]), F.Copy)
+    z = V(tp, [z], T.nt2[:], T.nx2[:])
+    n0 = V(ts, [z], T.ti[:, 0:8], T.nt2[:, 0:256:32], 4096.0, None, A.mult)
+    n0 = V(ts, [z], T.ti[:, 8:16], T.nt2[:, 16:256:32], 4096.0, None, A.mult)
+    qa = V(qz, [da], T.aq[:], T.aqs[:], T.at[:])
+    s20 = V(ms, [], T.s2[:], 0.0)
+    cut = 2048 - P * d
+    ga = S([gi, io], T.ab[:, 0:cut], T.iot[:, 0:cut], F.Identity, bias=float(P * d))
+    if d:
+        ga = S([gi, io], T.ab[:, cut:2048], T.iot[:, cut:2048], F.Identity, bias=float(P * d - 2048))
 
     scd = []
     for j, k in enumerate([0] + list(range(N - 1, 0, -1))):
@@ -201,16 +203,17 @@ def rank_program(g, core, T, topo):
             f = V(tt, [m, fl0[t]], fl_[:, k:512:4], ga_[:, k:512:4], mx_[:, k - 1:512:4], A.is_le)
         return V(scan, [f, vd[t]], cn_[:], fl_[:], T["vd%d" % t][:], 0.0, A.mult, A.add)
 
-    def count1(c, deps):
+    def keep1(c, deps):
         x = S(deps + [nbc], T.ad1[:, 0:128], c, F.Abs, bias=fc[:, 5:6])
-        x = V(ts, [x], T.mk1[:, 0:128], T.ad1[:, 0:128], 128.0 * U, None, A.is_lt)
-        x = V(scan, [x, zr], T.ct1[:, 0:128], T.mk1[:, 0:128], T.zer[:, 0:128], 0.0, A.add, A.add)
+        mk = V(ts, [x], T.mk1[:, 0:128], T.ad1[:, 0:128], 128.0 * U, None, A.is_lt)
+        x = V(scan, [mk, zr], T.ct1[:, 0:128], T.mk1[:, 0:128], T.zer[:, 0:128], 0.0, A.add, A.add)
+        y = V(tt, [mk] + deps, T.mc[:], T.mk1[:, 0:128], c, A.mult)
         x = V(tp, [x], T.ta[:], T.ct1[:, 96:128])
+        y = V(tt, [y, nq], T.mn[:], T.mc[:], T.nq[:], A.add)
         x = V(tc, [x, sb0], T.sb[:, 16:32], T.ta[:, 0:16])
         x = V(tp, [x], T.tb[:], T.sb[:])
-        x = V(ts, [x, i5c], T.ct3[:], T.ct1[:, 0:128], T.tb[:, 31:32], fc[:, 6:7], A.add, A.add)
-        x = V(tt, [x], T.kb1[:, 0:128], T.mk1[:, 0:128], T.ct3[:], A.mult)
-        return V(tt, [x] + deps, T.zz1[:, 0:128], T.kb1[:, 0:128], c, A.add)
+        x = V(ts, [x], T.k2[:], T.ct1[:, 0:128], T.tb[:, 31:32], float(CAP), A.add, A.is_le)
+        return V(tt, [x, y], T.zz1[:, 0:128], T.k2[:], T.mn[:], A.mult)
 
     def whole(cn, deps):
         x = V(tc, deps, T.cc[:], cn)
@@ -219,15 +222,8 @@ def rank_program(g, core, T, topo):
         x2 = S([x, rj], T.cx[:, 128:256], T.cct[:].indirect(T.rj[:, 8:16]), F.Copy)
         return V(tp, [x1, x2], T.cr[:], T.cx[:])
 
-    def count2(c, deps):
-        x = S(deps + [nbc], T.ad2[:], c, F.Abs, bias=fc[:, 5:6])
-        x = V(ts, [x], T.mk2[:], T.ad2[:], 128.0 * U, None, A.is_lt)
-        x = V(scan, [x, zr, i5c], T.ct2[:], T.mk2[:], T.zer[:], fc[:, 6:7], A.add, A.add)
-        x = V(tt, [x], T.kb2[:], T.mk2[:], T.ct2[:], A.mult)
-        return V(tt, [x] + deps, T.zz2[:], T.kb2[:], c, A.add)
-
     def onto(t, z):
-        ex, tr, m4, m2, m1, ti = [T[n + str(t)] for n in ("ex", "tr", "m4", "m2", "m1", "ti")]
+        ex, tr, m4, m2, m1 = [T[n + str(t)] for n in ("ex", "tr", "m4", "m2", "m1")]
         w = P * t
         zz = T["zz%d" % t][:, 0:w // 2]
         x1 = V(tc, [z, dup], ex[:, 0:w // 2], zz.indirect(T.dup[:, 0:8 * t]))
@@ -236,32 +232,29 @@ def rank_program(g, core, T, topo):
         for k in range(4):
             y = V(tt, [x], m4[:, 16 * k:16 * k + 16], tr[:, k:w:16 * t], tr[:, k + 4:w:16 * t], A.max)
         y = V(tt, [y], m2[:], m4[:, 0:32], m4[:, 32:64], A.max)
-        y = V(tt, [y], m1[:], m2[:, 0:16], m2[:, 16:32], A.max)
-        zi = V(ts, [y], ti[:, 16:32], m1[:], 4096.0, None, A.mult)
-        ky = V(ts, [zi], ti[:, 48:64], ti[:, 16:32], 12, 511, A.logical_shift_right, A.bitwise_and)
-        ci = V(ts, [zi], ti[:, 32:48], ti[:, 16:32], 4095, None, A.bitwise_and)
-        kf = V(ts, [ky], ti[:, 64:80], ti[:, 48:64], float(CAP), None, A.is_le)
-        kc = V(tt, [kf, ci], ti[:, 80:96], ti[:, 64:80], ti[:, 32:48], A.mult)
-        return V(tt, [kc, n0[t]], ti[:, 96:112], ti[:, 80:96], ti[:, 0:16], A.max), zi, ky, kf
+        return V(tt, [y], m1[:], m2[:, 0:16], m2[:, 16:32], A.max)
+
+    def product(i, x, xs, ps, tm, deps):
+        m = MM(deps + [qa], ps[:, 512 * i:512 * i + P], T.aq[:, 128 * i:128 * i + 128], T.aqs[:, 128 * i:128 * i + 128], x[:], xs[:])
+        return S([m], tm[:, P * i:P * i + P], ps[:, 512 * i:512 * i + P], F.Copy, scale=0.05)
 
     def states(x, xs, ps, et, h, tm, edep, deps):
         for i in range(4):
-            m = MM(deps + [qa], ps[:, 512 * i:512 * i + P], T.aq[:, 128 * i:128 * i + 128], T.aqs[:, 128 * i:128 * i + 128], x[:], xs[:])
-            s = S([m], tm[:, P * i:P * i + P], ps[:, 512 * i:512 * i + P], F.Copy, scale=0.05)
+            s = product(i, x, xs, ps, tm, deps)
             a = V(tt, [s, edep], h[:, i:1024:4], tm[:, P * i:P * i + P], et[:, i:1024:4], A.add)
         return a
 
     ch = choose(1, T.sc[:], T.of[:, 0:32], scd + [of])
-    z = count1(T.cn1[:, 3:512:4], [ch])
-    cf = onto(1, z)[0]
-    ox = V(tc, [cf], T.ofx1[:, 0:8], T.ti1[:, 96:112:2])
-    ox = V(tc, [cf], T.ofx1[:, 8:16], T.ti1[:, 97:112:2])
+    z = onto(1, keep1(T.cn1[:, 3:512:4], [ch]))
+    ox = V(ts, [z], T.ofx1[:, 0:8], T.m11[:, 0:16:2], 4096.0, None, A.mult)
+    ox = V(ts, [z], T.ofx1[:, 8:16], T.m11[:, 1:16:2], 4096.0, None, A.mult)
     pc = V(tc, [ox], T.x1[:].bitcast(u32), T.hw[:].bitcast(u32).indirect(T.ofx1[:]))
     pk = S([ox], T.x1s[:], T.hws[:].indirect(T.ofx1[:]), F.Copy)
-    hd = states(T.x1, T.x1s, T.pr, T.e1t, T.h1, T.tm1, e1, [pc, pk])
     sr = S([ox], T.scr1[:], T.sc[:].indirect(T.ofx1[:]), F.Copy)
     for k in (0, 1):
         dg = G(g.affine_select, [sr], T.dg[:, 128 * k:128 * k + 128], T.scr1[:, 128 * k:128 * k + 128], [[-1, 128]], A.is_equal, 0.0, 0, 1)
+    hd = states(T.x1, T.x1s, T.pr, T.e1t, T.h1, T.tm1, e1, [pc, pk])
+    for k in (0, 1):
         sc1 = S([dg], T.dgo[:, 128 * k:128 * k + 128], T.dg[:, 128 * k:128 * k + 128], F.Copy, accum_out=T.scc[:, k:k + 1])
     c1r = S([ox, ga], T.chr1[:], T.ab[:].indirect(T.ofx1[:]), F.Copy)
     q1 = V(qz, [hd], T.hq[:], T.hqs[:], T.h1[:])
@@ -278,25 +271,29 @@ def rank_program(g, core, T, topo):
         D("ys"[k % 2], [og, ("rg", 7 * neng), s20], ("ds2", "ds3")[k % 2], T.s2[16 * k:16 * k + 1, :], T.sld[:])
 
     ch = choose(2, T.s2[:], T.op2, [("ds2", 64), ("ds3", 64), op2])
-    z = count2(T.cr[:], [whole(T.cn2[:, 3:512:4], [ch])])
-    y1 = S([z, t1c], T.d1[:], T.zz2[:], F.Identity, bias=fc[:, 9:10])
-    y0 = V(ts, [z, t0c], T.d0[:], T.zz2[:], fc[:, 8:9], None, A.subtract)
+    cr = whole(T.cn2[:, 3:512:4], [ch])
+    x = S([cr, nbc], T.ad2[:], T.cr[:], F.Abs, bias=fc[:, 5:6])
+    y1 = S([cr, t1c], T.cb[:], T.cr[:], F.Identity, bias=fc[:, 9:10])
+    y0 = V(ts, [cr, t0c], T.ca[:], T.cr[:], fc[:, 8:9], None, A.subtract)
+    x = V(ts, [x], T.mk2[:], T.ad2[:], 128.0 * U, None, A.is_lt)
+    x = V(scan, [x, zr, i5c], T.ct2[:], T.mk2[:], T.zer[:], fc[:, 6:7], A.add, A.add)
+    kb = V(tt, [x], T.kb2[:], T.mk2[:], T.ct2[:], A.mult)
+    y0 = V(tt, [kb, y0], T.d0[:], T.kb2[:], T.ca[:], A.add)
+    y1 = V(tt, [kb, y1], T.d1[:], T.kb2[:], T.cb[:], A.add)
     y0 = V(red, [y0], T.rv[:, 0:1], T.d0[:], AxisListType.X, A.min, apply_absolute_value=True)
     y1 = V(red, [y1], T.rv[:, 1:2], T.d1[:], AxisListType.X, A.min, apply_absolute_value=True)
     rq = V(ts, [y0, y1], T.rq[:], T.rv[:], 255.0 * U, 4096.0, A.min, A.mult)
     send_all([rq], "rr", T.rq[:], [T.rqs[:, 2 * rel(d, i):2 * rel(d, i) + 2] for i in others])
     for k in range(8):
         oq = D("y", [("rr", 7 * neng)], "dofq", T.ofq[16 * k:16 * k + 16, 2:16], T.rqs[d:128:8, 2:16])
-    cf, zi, ky, kf = onto(2, z)
-    ti = T.ti2
-    x = V(ts, [zi], ti[:, 112:128], ti[:, 16:32], 21, None, A.logical_shift_right)
-    x = V(ts, [x], ti[:, 128:144], ti[:, 112:128], 32.0, None, A.mult)
-    x = V(tt, [x, ky], ti[:, 144:160], ti[:, 128:144], ti[:, 48:64], A.add)
-    x = V(tt, [x, kf], ti[:, 160:176], ti[:, 144:160], ti[:, 64:80], A.mult)
-    y = V(ts, [x], ti[:, 176:192], ti[:, 160:176], 0.0, 223.0, A.is_gt, A.mult)
-    x = V(tt, [y], ti[:, 192:208], ti[:, 160:176], ti[:, 176:192], A.add)
-    x = V(tt, [x], ti[:, 208:224], ti[:, 192:208], ti[:, 0:16], A.max)
-    ox2 = V(tc, [x], T.ofx2[:], ti[:, 208:224])
+    z = V(tt, [kb, cr], T.zz2[:], T.kb2[:], T.cr[:], A.add)
+    z = onto(2, z)
+    ti = T.ti
+    zi = V(ts, [z], ti[:, 16:32], T.m12[:], 4096.0, None, A.mult)
+    ky = V(ts, [zi], ti[:, 48:64], ti[:, 16:32], 12, 511, A.logical_shift_right, A.bitwise_and)
+    ci = V(ts, [zi], ti[:, 32:48], ti[:, 16:32], 4095, None, A.bitwise_and)
+    kq = V(ts, [zi], ti[:, 112:128], ti[:, 16:32], 21, None, A.logical_shift_right)
+    kf = V(ts, [ky], ti[:, 64:80], ti[:, 48:64], float(CAP), None, A.is_le)
     pc = V(tc, [oq, q1], T.sp[:].bitcast(u32), T.hq[:].bitcast(u32).indirect(T.ofq[:, 2:16]))
     pk = S([oq, q1], T.sps[:], T.hqs[:].indirect(T.ofq[:, 2:16]), F.Copy)
     ca, cb = [], []
@@ -306,12 +303,21 @@ def rank_program(g, core, T, topo):
         cb.append((T.sps[:, a:a + CAP], T.w2s[:, b:b + CAP]))
     send_each([pc], "rc", ca)
     send_each([pk], "rc", cb)
+    kc = V(tt, [kf, ci], ti[:, 80:96], ti[:, 64:80], ti[:, 32:48], A.mult)
+    x = V(ts, [kq], ti[:, 128:144], ti[:, 112:128], 32.0, None, A.mult)
+    cf = V(tt, [kc, n0], ti[:, 96:112], ti[:, 80:96], ti[:, 0:16], A.max)
+    x = V(tt, [x, ky], ti[:, 144:160], ti[:, 128:144], ti[:, 48:64], A.add)
+    x = V(tt, [x, kf], ti[:, 160:176], ti[:, 144:160], ti[:, 64:80], A.mult)
+    y = V(ts, [x], ti[:, 176:192], ti[:, 160:176], 0.0, 223.0, A.is_gt, A.mult)
+    x = V(tt, [y], ti[:, 192:208], ti[:, 160:176], ti[:, 176:192], A.add)
+    x = V(tt, [x], ti[:, 208:224], ti[:, 192:208], ti[:, 0:16], A.max)
+    ox2 = V(tc, [x], T.ofx2[:], ti[:, 208:224])
     oc2 = V(tc, [cf], T.ofc2[:], ti[:, 96:112])
     lo = V(ts, [cf], ti[:, 112:128], ti[:, 96:112], 127, None, A.bitwise_and)
-    hb = V(ts, [cf], ti[:, 128:144], ti[:, 96:112], 7, 1, A.logical_shift_right, A.bitwise_and)
+    hb = V(ts, [cf, ox2], ti[:, 128:144], ti[:, 96:112], 7, 1, A.logical_shift_right, A.bitwise_and)
     tl = V(tt, [lo], ti[:, 144:160], ti[:, 96:112], ti[:, 112:128], A.add)
-    hm = V(ts, [hb], ti[:, 160:176], ti[:, 128:144], -127.0, None, A.mult)
-    x = V(tt, [tl, hm], ti[:, 224:240], ti[:, 144:160], ti[:, 160:176], A.add)
+    hm = V(ts, [hb], ti[:, 176:192], ti[:, 128:144], -127.0, None, A.mult)
+    x = V(tt, [tl, hm], ti[:, 224:240], ti[:, 144:160], ti[:, 176:192], A.add)
     os2 = V(tc, [x], T.ofs2[:], ti[:, 224:240])
     sr2 = S([os2], T.scr2[:], T.s2[:].indirect(T.ofs2[:]), F.Copy)
     c2r = S([oc2, ga], T.chr2[:], T.ab[:].indirect(T.ofc2[:]), F.Copy)

@@ -2,6 +2,7 @@ from concourse.bass import DstId, RemoteDMATransfer
 from concourse.mybir import dt, AluOpType as A, AxisListType, ActivationFunctionType as F
 
 N, P, CAP = 8, 256, 32
+RELAYED = 2
 BIG = 9e29
 U = 1.0 / 4096.0
 
@@ -9,30 +10,67 @@ _f32, _i32, _u16, _bf = "float32", "int32", "uint16", "bfloat16"
 SCRATCH = {"ps": ("psum", [128, 2048], _f32), "pr": ("psum", [128, 2048], _f32), "sld": ("dram", [8, 128, 2], _f32)}
 for _d, _l in (
         (_bf, "e0t 1024 e1t 1024 e2t 1024 ut 16 ub 512 ones 128 at 2048 wt 512 h1 1024 h2 1024"),
-        (_f32, "tm1 1024 tm2 1024 sc 2048 s2 2048 iot 2048 ab 2048 rs 512 zer 256 ta 32 sb 32 tb 32 nq 128 cc 128 cct 128 cx 256 "
+        (_f32, "tm1 1024 tm2 1024 sc 2048 iot 2048 ab 2048 rs 512 rsb 512 zer 256 ta 32 sb 32 tb 32 nq 128 cc 128 cct 128 cx 256 "
                "fc 16 cr 256 ca 256 cb 256 d0 256 d1 256 rv 2 scr1 256 scr2 256 dg 256 dgo 256 scc 2 g1c 2 chr1 256 chr2 256 go 256 ys 256 "
-               "mc 128 mn 128 k2 128 nx2 256 nt2 256"),
+               "mc 128 mn 128 exm 256 k2 128 nx2 256 nt2 256 kb2 256 zz2 256"),
         (_i32, "pt 64 pa 64 np 64 lo 32 hb 32 tl 32 hm 32 po 32 iz 16 ic 8 iy 32 ti 256"),
         (_u16, "of 64 op2 32 rj 16 dup 32 dup4 32 rq 2 rqs 16 ofq 16 ofx1 16 ofx2 16 ofs2 16 ofc2 16")):
     _w = _l.split()
     for _k in range(0, len(_w), 2):
         SCRATCH[_w[_k]] = ("sbuf", [128, int(_w[_k + 1])], _d)
-for _n, _c in (("uq", 128), ("aq", 512), ("wq", 128), ("hw", 2048), ("x1", 256), ("hq", 256), ("sp", 224), ("w2", 512), ("x2", 256), ("zq", 256)):
+for _n, _c in (("uq", 128), ("aq", 512), ("wq", 128), ("hw", 2048), ("hr", 256), ("x1", 256), ("hq", 256), ("sp", 224), ("w2", 512), ("x2", 256),
+               ("zq", 256)):
     SCRATCH[_n] = ("sbuf", [128, _c], "float8_e4m3fn_x4")
     SCRATCH[_n + "s"] = ("sbuf", [128, _c], "uint8")
 for _t in ("1", "2"):
     for _n, _c in (("ga", 512), ("mx", 512), ("fl", 512), ("cn", 512), ("nr", 512), ("vd", 512),
-                   ("ad", 256), ("mk", 256), ("ct", 256), ("zz", 256), ("ex", 512), ("tr", 512), ("m4", 64), ("m2", 32), ("m1", 16)):
+                   ("ad", 256), ("mk", 256), ("ct", 256), ("ex", 512), ("tr", 512), ("mr", 512)):
         SCRATCH[_n + _t] = ("sbuf", [128, _c], _f32)
-SCRATCH["kb2"] = ("sbuf", [128, 256], _f32)
 
-SEMAPHORES = ["cv", "cs", "ct", "cg", "l0", "ls", "rg", "rr", "rc"] + ["h%d" % i for i in range(N)]
-SEMAPHORES += ["de0", "du", "dp1", "dp2", "da", "de1", "dw", "de2", "dog", "ds2", "ds3", "dofq", "dch1", "dch2", "dout"]
+SEMAPHORES = ["cv", "cs", "ct", "cg", "l0", "ls", "rg", "rr", "rc", "hc", "hk"] + ["h%d" % i for i in range(N)]
+SEMAPHORES += ["de0", "du", "dp1", "dp2", "da", "de1", "dw", "de2", "dog", "ds2", "ds3", "dofq", "dofs", "dch1", "dch2", "dout"]
+
+
+def relayed(d, cores, topo):
+    me = cores[d]
+    here = topo.chip(me)
+    far = [i for i in range(N) if i != d and not topo.mates(here, topo.chip(cores[i])) and not topo.same_plane(here, topo.chip(cores[i]))]
+    far.sort(key=lambda i: (-min((i - d) % N, (d - i) % N), (i - d) % N))
+    far = far[:RELAYED]
+    for h in topo.cores_of(me):
+        if topo.die(h) != topo.die(me) and all(topo.may_write(h, cores[i]) for i in far):
+            return far, h
+    return [], None
+
+
+def bits(m):
+    return bin(m).count("1")
+
+
+def hand_on(g, core, T, topo):
+    for d in range(N):
+        far, h = relayed(d, T.cores, topo)
+        if h != core:
+            continue
+        came = bits(topo.mask(T.cores[d], core) & ~topo.mask(T.cores[d], T.cores[far[0]]))
+        mask = topo.mask(core, T.cores[far[0]])
+        ids = []
+        for i in far:
+            rid, pid, _ = topo.addr(T.cores[i])
+            ids.append(DstId(rid=rid, pnc=pid))
+        o = [P * ((d - i) % N) for i in far]
+        for sem, src, dsts in (("hc", T.hr[:].bitcast(dt.uint8), [T.hw[:, a:a + P].bitcast(dt.uint8) for a in o]),
+                               ("hk", T.hrs[:], [T.hws[:, a:a + P] for a in o])):
+            g.wait_ge(T.sem[sem], came)
+            g.remote_dma_fused([RemoteDMATransfer(dst_ids=ids, dma_engine_mask=mask, remote_sem=T.sem["h%d" % d], srcs=[src], dsts=dsts)],
+                               local_sem=T.sem.ls)
+        g.wait_ge(T.sem.ls, 2 * bits(mask))
 
 
 def rank_program(g, core, T, topo):
     d = T.rank_of(core)
     if d is None:
+        hand_on(g, core, T, topo)
         return
     cores = T.cores
     Q = {"v": g.vector, "s": g.scalar, "t": g.tensor, "g": g, "y": g.sync}
@@ -77,29 +115,34 @@ def rank_program(g, core, T, topo):
     u8, u32 = dt.uint8, dt.uint32
 
     others = [(d + k) % N for k in range(1, N)]
-    ids = []
-    for i in others:
-        rid, pid, _ = topo.addr(cores[i])
-        ids.append(DstId(rid=rid, pnc=pid))
+
+    def dst(c):
+        rid, pid, _ = topo.addr(c)
+        return DstId(rid=rid, pnc=pid)
+
     mask = topo.mask(core, cores[others[0]])
     for i in others:
         mask &= topo.mask(core, cores[i])
     engs = [e for e in topo.engines(core, cores[others[0]]) if mask >> e & 1]
     neng = len(engs)
+    far, helper = relayed(d, cores, topo)
+    near = [i for i in others if i not in far]
 
     def sent(name, n):
         total[name] = total.get(name, 0) + n
         return (name, total[name])
 
-    def send_all(deps, sem, src, dsts, local="ls"):
+    def send(deps, sem, src, to, dsts, local="ls", m=mask):
         wait("g", deps)
-        g.remote_dma_fused([RemoteDMATransfer(dst_ids=ids, dma_engine_mask=mask, remote_sem=T.sem[sem], srcs=[src], dsts=dsts)],
+        g.remote_dma_fused([RemoteDMATransfer(dst_ids=[dst(c) for c in to], dma_engine_mask=m, remote_sem=T.sem[sem], srcs=[src], dsts=dsts)],
                            local_sem=T.sem[local])
-        return sent(local, neng)
+        return sent(local, bits(m))
+
+    all_ = [cores[i] for i in others]
 
     def send_each(deps, sem, pairs):
         wait("g", deps)
-        g.remote_dma_fused([RemoteDMATransfer(dst_ids=[ids[k]], dma_engine_mask=1 << engs[k], remote_sem=T.sem[sem], srcs=[a], dsts=[b])
+        g.remote_dma_fused([RemoteDMATransfer(dst_ids=[dst(all_[k])], dma_engine_mask=1 << engs[k], remote_sem=T.sem[sem], srcs=[a], dsts=[b])
                             for k, (a, b) in enumerate(pairs)], local_sem=T.sem.ls)
         return sent("ls", len(pairs))
 
@@ -110,21 +153,35 @@ def rank_program(g, core, T, topo):
     uu = D("y", [], "du", T.ut[:, 0:8], T.u[:, 0:8])
     for k in range(8):
         p1 = D("y", [], "dp1", T.pt[16 * k:16 * k + 16, 0:32], T.p1[:, 32 * (k % 2):32 * (k % 2) + 32])
-    for k in range(8):
-        p2 = D("y", [], "dp2", T.pt[16 * k:16 * k + 16, 32:64], T.p2[:, 32 * (k % 2):32 * (k % 2) + 32])
     da = D("y", [e0], "da", T.at[:], T.a[:, :])
 
-    gi = G(g.iota, [], T.iot[:, 0:512], [[1, 512]], 0, 0, allow_small_or_imprecise_dtypes=True)
     gp = G(g.iota, [], T.ic[:, 0:1], [[0, 1]], 0, 1)
+    gi = G(g.iota, [], T.iot[:, 0:512], [[1, 512]], 0, 0, allow_small_or_imprecise_dtypes=True)
     giy = G(g.iota, [], T.iy[:], [[16, 16], [0, 2]], 0, 0)
     giz = G(g.iota, [], T.iz[:], [[16, 2], [32, 4], [0, 2]], 0, 0)
     for k in (1, 2, 3):
         io = S([gi], T.iot[:, 512 * k:512 * k + 512], T.iot[:, 0:512], F.Identity, bias=512.0 * k)
     on = V(ms, [], T.ones[:], 1.0)
+    r1 = V(ms, [], T.rs[:], BIG)
+    r2 = V(ms, [], T.rsb[:, 0:256], BIG)
+    zr = V(ms, [], T.zer[:], 0.0)
+    sb0 = V(ms, [], T.sb[:], 0.0)
+    fl0 = {1: V(ms, [], T.fl1[:, 0:512:4], 0.0)}
+    rs = V(ms, [r1], T.rs[:, 0:512:4], -BIG)
+    rsb = V(ms, [r2], T.rsb[:, 0:256:16], -BIG)
+
     q0 = V(qz, [e0], T.hw[:, 0:P], T.hws[:, 0:P], T.e0t[:])
-    send_all([q0], "h%d" % d, T.hw[:, 0:P].bitcast(u8), [T.hw[:, P * rel(d, i):P * rel(d, i) + P].bitcast(u8) for i in others], "l0")
-    l0 = send_all([q0], "h%d" % d, T.hws[:, 0:P], [T.hws[:, P * rel(d, i):P * rel(d, i) + P] for i in others], "l0")
+    hcode, hscale = T.hw[:, 0:P].bitcast(u8), T.hws[:, 0:P]
+    if far:
+        send([q0], "hc", hcode, [helper], [T.hr[:].bitcast(u8)], "l0", topo.mask(core, helper) & ~mask)
+    to = [cores[i] for i in near]
+    send([q0], "h%d" % d, hcode, to, [T.hw[:, P * rel(d, i):P * rel(d, i) + P].bitcast(u8) for i in near], "l0")
+    if far:
+        send([q0], "hk", hscale, [helper], [T.hrs[:]], "l0", topo.mask(core, helper) & ~mask)
+    l0 = send([q0], "h%d" % d, hscale, to, [T.hws[:, P * rel(d, i):P * rel(d, i) + P] for i in near], "l0")
     e1 = D("y", [l0], "de1", T.e1t[:], T.e1[:, :])
+    for k in range(8):
+        p2 = D("y", [l0], "dp2", T.pt[16 * k:16 * k + 16, 32:64], T.p2[:, 32 * (k % 2):32 * (k % 2) + 32])
     e2 = D("y", [l0], "de2", T.e2t[:], T.e2[:, :])
     dw = D("y", [l0], "dw", T.wt[:], T.w[:, :])
 
@@ -132,62 +189,42 @@ def rank_program(g, core, T, topo):
         ubk = V(ts, [on, uu], T.ub[:, k:512:4], T.ones[:], T.ut[:, k:k + 1], None, A.mult)
     quq = V(qz, [ubk], T.uq[:], T.uqs[:], T.ub[:])
 
-    x = V(ts, [p1, p2], T.pa[:], T.pt[:], float(2048 - P * d), None, A.add)
-    x = V(ts, [x], T.np[:], T.pa[:], 2047, None, A.bitwise_and)
-    of = V(tc, [x], T.of[:], T.np[:])
-    n2 = T.np[:, 32:64]
-    a1 = V(ts, [x], T.lo[:], n2, 127, None, A.bitwise_and)
-    a2 = V(ts, [x], T.hb[:], n2, 7, 1, A.logical_shift_right, A.bitwise_and)
-    a3 = V(tt, [a1], T.tl[:], n2, T.lo[:], A.add)
-    a4 = V(ts, [a2], T.hm[:], T.hb[:], -127.0, None, A.mult)
-    a5 = V(tt, [a3, a4], T.po[:], T.tl[:], T.hm[:], A.add)
-    op2 = V(tc, [a5], T.op2[:], T.po[:])
-    nr = {}
-    for t in (1, 2):
-        nr[t] = S([gi, io, of], T["nr%d" % t][:], T.iot[:].indirect(T.of[:, 32 * t - 32:32 * t]), F.Copy, scale=U)
+    def listed(t, dep):
+        o = slice(32 * t - 32, 32 * t)
+        x = V(ts, [dep], T.pa[:, o], T.pt[:, o], float(2048 - P * d), None, A.add)
+        x = V(ts, [x], T.np[:, o], T.pa[:, o], 2047, None, A.bitwise_and)
+        return x, V(tc, [x], T.of[:, o], T.np[:, o])
 
+    def row(t, of):
+        return S([gi, io, of], T["nr%d" % t][:], T.iot[:].indirect(T.of[:, 32 * t - 32:32 * t]), F.Copy, scale=U)
+
+    def deltas(t, nr):
+        r, v = T["nr%d" % t], T["vd%d" % t]
+        z = V(tt, [nr], v[:, 0:511], r[:, 0:511], r[:, 1:512], A.subtract)
+        return V(tc, [z], v[:, 3:512:4], r[:, 3:512:4])
+
+    of1 = listed(1, p1)[1]
+    nr, vd = {1: row(1, of1)}, {}
     ic, fc = T.ic, T.fc
     b1 = V(ts, [gp], ic[:, 1:2], ic[:, 0:1], 7, None, A.bitwise_and)
-    b2 = V(ts, [b1], ic[:, 2:3], ic[:, 1:2], float(N - d), None, A.add)
-    b3 = V(ts, [b2], ic[:, 3:4], ic[:, 2:3], 7, None, A.bitwise_and)
     b4 = V(ts, [gp], ic[:, 4:5], ic[:, 0:1], 3, None, A.logical_shift_right)
     b5 = V(ts, [gp], ic[:, 5:6], ic[:, 0:1], 15, None, A.bitwise_and)
+    b2 = V(ts, [b1], ic[:, 2:3], ic[:, 1:2], float(N - d), None, A.add)
+    b3 = V(ts, [b2], ic[:, 3:4], ic[:, 2:3], 7, None, A.bitwise_and)
     b6 = V(tc, [b3, b4, b5], fc[:, 0:3], ic[:, 3:6])
     c1 = V(ts, [b6], fc[:, 3:4], fc[:, 0:1], -256.0 * U, -127.5 * U, A.mult, A.add)
     c2 = V(ts, [b6], fc[:, 4:5], fc[:, 0:1], 0.0, -100.0, A.is_equal, A.mult)
     c4 = V(ts, [b6], fc[:, 10:11], fc[:, 0:1], 0.0, None, A.is_equal)
-    nbc = V(tt, [c1, c2], fc[:, 5:6], fc[:, 3:4], fc[:, 4:5], A.add)
-    i5c = V(ts, [b6], fc[:, 6:7], fc[:, 0:1], 512.0, None, A.mult)
-    c3 = V(ts, [b6], fc[:, 7:8], fc[:, 0:1], 512.0 + 256.0 * U, 1.0, A.mult, A.add)
-    t0c = V(tt, [c3], fc[:, 8:9], fc[:, 7:8], fc[:, 1:2], A.add)
-    t1c = V(ts, [t0c], fc[:, 9:10], fc[:, 8:9], -1.0, -16.0, A.mult, A.add)
     dup = V(ts, [b6, giy], T.dup[:], T.iy[:], fc[:, 2:3], None, A.add)
-    dup4 = V(ts, [b6, giy], T.dup4[:], T.iy[:], fc[:, 2:3], 4.0, A.add, A.mult)
-    rj = V(tc, [giz], T.rj[:], T.iz[:])
-    r1 = V(ms, [], T.rs[:], BIG)
-    rs = V(ms, [r1], T.rs[:, 0:512:4], -BIG)
-    zr = V(ms, [], T.zer[:], 0.0)
-    sb0 = V(ms, [], T.sb[:], 0.0)
-    fl0 = {t: V(ms, [], T["fl%d" % t][:], 0.0) for t in (1, 2)}
-    vd = {}
-    for t in (1, 2):
-        r, v = T["nr%d" % t], T["vd%d" % t]
-        z = V(tt, [nr[t]], v[:, 0:511], r[:, 0:511], r[:, 1:512], A.subtract)
-        vd[t] = V(tc, [z], v[:, 3:512:4], r[:, 3:512:4])
+    nbc = V(tt, [c1, c2], fc[:, 5:6], fc[:, 3:4], fc[:, 4:5], A.add)
+    vd[1] = deltas(1, nr[1])
     nq = V(ts, [nr[1], c4], T.nq[:], T.nr1[:, 0:512:4], fc[:, 10:11], None, A.mult)
-    z = S([nr[2], dup4], T.nx2[:], T.nr2[:].indirect(T.dup4[:, 0:16]), F.Copy)
-    z = V(tp, [z], T.nt2[:], T.nx2[:])
-    n0 = V(ts, [z], T.ti[:, 0:8], T.nt2[:, 0:256:32], 4096.0, None, A.mult)
-    n0 = V(ts, [z], T.ti[:, 8:16], T.nt2[:, 16:256:32], 4096.0, None, A.mult)
     qa = V(qz, [da], T.aq[:], T.aqs[:], T.at[:])
-    s20 = V(ms, [], T.s2[:], 0.0)
-    cut = 2048 - P * d
-    ga = S([gi, io], T.ab[:, 0:cut], T.iot[:, 0:cut], F.Identity, bias=float(P * d))
-    if d:
-        ga = S([gi, io], T.ab[:, cut:2048], T.iot[:, cut:2048], F.Identity, bias=float(P * d - 2048))
 
     scd = []
-    for j, k in enumerate([0] + list(range(N - 1, 0, -1))):
+    slots = [rel(i, d) for i in range(N) if i != d]
+    slots.sort(key=lambda k: (d in relayed((d + k) % N, cores, topo)[0], -k))
+    for j, k in enumerate([0] + slots):
         b = j % 4
         deps = [quq, q0] + ([("h%d" % ((d + k) % N), 2 * neng)] if k else []) + ([scd[j - 4]] if j > 3 else [])
         mt = MM(deps, T.ps[:, 512 * b:512 * b + P], T.uq[:], T.uqs[:], T.hw[:, P * k:P * k + P], T.hws[:, P * k:P * k + P])
@@ -201,7 +238,7 @@ def rank_program(g, core, T, topo):
         m = V(scan, [x1, x2, rs], mx_[:], T.rs[:], ga_[:], -BIG, A.min, A.max)
         for k in (1, 2, 3):
             f = V(tt, [m, fl0[t]], fl_[:, k:512:4], ga_[:, k:512:4], mx_[:, k - 1:512:4], A.is_le)
-        return V(scan, [f, vd[t]], cn_[:], fl_[:], T["vd%d" % t][:], 0.0, A.mult, A.add)
+        return V(scan, [f, vd[t]], cn_[:], fl_[:], T["vd%d" % t][:], 0.0, A.mult, A.add), x1, x2
 
     def keep1(c, deps):
         x = S(deps + [nbc], T.ad1[:, 0:128], c, F.Abs, bias=fc[:, 5:6])
@@ -210,10 +247,11 @@ def rank_program(g, core, T, topo):
         y = V(tt, [mk] + deps, T.mc[:], T.mk1[:, 0:128], c, A.mult)
         x = V(tp, [x], T.ta[:], T.ct1[:, 96:128])
         y = V(tt, [y, nq], T.mn[:], T.mc[:], T.nq[:], A.add)
+        y = S([y, dup], T.exm[:], T.mn[:].indirect(T.dup[:, 0:16]), F.Copy)
         x = V(tc, [x, sb0], T.sb[:, 16:32], T.ta[:, 0:16])
         x = V(tp, [x], T.tb[:], T.sb[:])
         x = V(ts, [x], T.k2[:], T.ct1[:, 0:128], T.tb[:, 31:32], float(CAP), A.add, A.is_le)
-        return V(tt, [x, y], T.zz1[:, 0:128], T.k2[:], T.mn[:], A.mult)
+        return V(tt, [x, y], T.ex1[:, 0:256], T.k2[:].indirect(T.dup[:, 0:16]), T.exm[:], A.mult)
 
     def whole(cn, deps):
         x = V(tc, deps, T.cc[:], cn)
@@ -222,32 +260,22 @@ def rank_program(g, core, T, topo):
         x2 = S([x, rj], T.cx[:, 128:256], T.cct[:].indirect(T.rj[:, 8:16]), F.Copy)
         return V(tp, [x1, x2], T.cr[:], T.cx[:])
 
-    def onto(t, z):
-        ex, tr, m4, m2, m1 = [T[n + str(t)] for n in ("ex", "tr", "m4", "m2", "m1")]
+    def onto(t, deps):
         w = P * t
-        zz = T["zz%d" % t][:, 0:w // 2]
-        x1 = V(tc, [z, dup], ex[:, 0:w // 2], zz.indirect(T.dup[:, 0:8 * t]))
-        x2 = S([z, dup], ex[:, w // 2:w], zz.indirect(T.dup[:, 8 * t:16 * t]), F.Copy)
-        x = V(tp, [x1, x2], tr[:, 0:w], ex[:, 0:w])
-        for k in range(4):
-            y = V(tt, [x], m4[:, 16 * k:16 * k + 16], tr[:, k:w:16 * t], tr[:, k + 4:w:16 * t], A.max)
-        y = V(tt, [y], m2[:], m4[:, 0:32], m4[:, 32:64], A.max)
-        return V(tt, [y], m1[:], m2[:, 0:16], m2[:, 16:32], A.max)
-
-    def product(i, x, xs, ps, tm, deps):
-        m = MM(deps + [qa], ps[:, 512 * i:512 * i + P], T.aq[:, 128 * i:128 * i + 128], T.aqs[:, 128 * i:128 * i + 128], x[:], xs[:])
-        return S([m], tm[:, P * i:P * i + P], ps[:, 512 * i:512 * i + P], F.Copy, scale=0.05)
+        x = V(tp, deps, T["tr%d" % t][:, 0:w], T["ex%d" % t][:, 0:w])
+        return V(scan, [x, rsb], T["mr%d" % t][:, 0:w], T.rsb[:, 0:w], T["tr%d" % t][:, 0:w], -BIG, A.min, A.max)
 
     def states(x, xs, ps, et, h, tm, edep, deps):
         for i in range(4):
-            s = product(i, x, xs, ps, tm, deps)
+            m = MM(deps + [qa], ps[:, 512 * i:512 * i + P], T.aq[:, 128 * i:128 * i + 128], T.aqs[:, 128 * i:128 * i + 128], x[:], xs[:])
+            s = S([m], tm[:, P * i:P * i + P], ps[:, 512 * i:512 * i + P], F.Copy, scale=0.05)
             a = V(tt, [s, edep], h[:, i:1024:4], tm[:, P * i:P * i + P], et[:, i:1024:4], A.add)
         return a
 
-    ch = choose(1, T.sc[:], T.of[:, 0:32], scd + [of])
-    z = onto(1, keep1(T.cn1[:, 3:512:4], [ch]))
-    ox = V(ts, [z], T.ofx1[:, 0:8], T.m11[:, 0:16:2], 4096.0, None, A.mult)
-    ox = V(ts, [z], T.ofx1[:, 8:16], T.m11[:, 1:16:2], 4096.0, None, A.mult)
+    ch, g1v, g1s = choose(1, T.sc[:], T.of[:, 0:32], scd + [of1])
+    z = onto(1, [keep1(T.cn1[:, 3:512:4], [ch])])
+    ox = V(ts, [z], T.ofx1[:, 0:8], T.mr1[:, 7:256:32], 4096.0, None, A.mult)
+    ox = V(ts, [z], T.ofx1[:, 8:16], T.mr1[:, 23:256:32], 4096.0, None, A.mult)
     pc = V(tc, [ox], T.x1[:].bitcast(u32), T.hw[:].bitcast(u32).indirect(T.ofx1[:]))
     pk = S([ox], T.x1s[:], T.hws[:].indirect(T.ofx1[:]), F.Copy)
     sr = S([ox], T.scr1[:], T.sc[:].indirect(T.ofx1[:]), F.Copy)
@@ -256,21 +284,42 @@ def rank_program(g, core, T, topo):
     hd = states(T.x1, T.x1s, T.pr, T.e1t, T.h1, T.tm1, e1, [pc, pk])
     for k in (0, 1):
         sc1 = S([dg], T.dgo[:, 128 * k:128 * k + 128], T.dg[:, 128 * k:128 * k + 128], F.Copy, accum_out=T.scc[:, k:k + 1])
-    c1r = S([ox, ga], T.chr1[:], T.ab[:].indirect(T.ofx1[:]), F.Copy)
     q1 = V(qz, [hd], T.hq[:], T.hqs[:], T.h1[:])
     for k in (0, 1):
         mg = MM([q1] + scd, T.ps[:, 512 * k:512 * k + 128], T.hq[:, 128 * k:128 * k + 128], T.hqs[:, 128 * k:128 * k + 128], T.uq[:], T.uqs[:])
     q1b = V(qz, [hd], T.w2[:, 0:P], T.w2s[:, 0:P], T.h1[:])
     g1 = V(tt, [mg, sc1], T.g1c[:], T.ps[:, 0:1024:512], T.scc[:], A.add)
 
-    dc1 = D("s", [c1r], "dch1", T.ch[0:1, :], T.chr1[0:1, :])
-    send_all([g1], "rg", T.g1c[:], [T.sld[rel(d, i)] for i in others])
+    send([g1], "rg", T.g1c[:], all_, [T.sld[rel(d, i)] for i in others])
     og = D("y", [g1], "dog", T.sld[0], T.g1c[:])
+    x, of2 = listed(2, p2)
+    nr[2] = row(2, of2)
+    n2 = T.np[:, 32:64]
+    a1 = V(ts, [x], T.lo[:], n2, 127, None, A.bitwise_and)
+    a2 = V(ts, [x], T.hb[:], n2, 7, 1, A.logical_shift_right, A.bitwise_and)
+    a3 = V(tt, [a1], T.tl[:], n2, T.lo[:], A.add)
+    a4 = V(ts, [a2], T.hm[:], T.hb[:], -127.0, None, A.mult)
+    dup4 = V(ts, [b6, giy], T.dup4[:], T.iy[:], fc[:, 2:3], 4.0, A.add, A.mult)
+    a5 = V(tt, [a3, a4], T.po[:], T.tl[:], T.hm[:], A.add)
+    fl0[2] = V(ms, [], T.fl2[:, 0:512:4], 0.0)
+    op2 = V(tc, [a5], T.op2[:], T.po[:])
+    i5c = V(ts, [b6], fc[:, 6:7], fc[:, 0:1], 512.0, None, A.mult)
+    c3 = V(ts, [b6], fc[:, 7:8], fc[:, 0:1], 512.0 + 256.0 * U, 1.0, A.mult, A.add)
+    rj = V(tc, [giz], T.rj[:], T.iz[:])
+    t0c = V(tt, [c3], fc[:, 8:9], fc[:, 7:8], fc[:, 1:2], A.add)
+    r2 = V(ms, [], T.rsb[:, 256:512], BIG)
+    t1c = V(ts, [t0c], fc[:, 9:10], fc[:, 8:9], -1.0, -16.0, A.mult, A.add)
+    vd[2] = deltas(2, nr[2])
+    z = S([nr[2], dup4], T.nx2[:], T.nr2[:].indirect(T.dup4[:, 0:16]), F.Copy)
+    z = V(tp, [z], T.nt2[:], T.nx2[:])
+    rsb = V(ms, [r2], T.rsb[:, 256:512:16], -BIG)
+    n0 = V(ts, [z], T.ti[:, 0:8], T.nt2[:, 0:256:32], 4096.0, None, A.mult)
+    n0 = V(ts, [z], T.ti[:, 8:16], T.nt2[:, 16:256:32], 4096.0, None, A.mult)
     qw = V(qz, [dw], T.wq[:], T.wqs[:], T.wt[:])
     for k in range(8):
-        D("ys"[k % 2], [og, ("rg", 7 * neng), s20], ("ds2", "ds3")[k % 2], T.s2[16 * k:16 * k + 1, :], T.sld[:])
+        D("ys"[k % 2], [og, ("rg", 7 * neng), g1v, g1s, sr], ("ds2", "ds3")[k % 2], T.sc[16 * k:16 * k + 1, :], T.sld[:])
 
-    ch = choose(2, T.s2[:], T.op2, [("ds2", 64), ("ds3", 64), op2])
+    ch = choose(2, T.sc[:], T.op2, [("ds2", 64), ("ds3", 64), op2])[0]
     cr = whole(T.cn2[:, 3:512:4], [ch])
     x = S([cr, nbc], T.ad2[:], T.cr[:], F.Abs, bias=fc[:, 5:6])
     y1 = S([cr, t1c], T.cb[:], T.cr[:], F.Identity, bias=fc[:, 9:10])
@@ -283,19 +332,25 @@ def rank_program(g, core, T, topo):
     y0 = V(red, [y0], T.rv[:, 0:1], T.d0[:], AxisListType.X, A.min, apply_absolute_value=True)
     y1 = V(red, [y1], T.rv[:, 1:2], T.d1[:], AxisListType.X, A.min, apply_absolute_value=True)
     rq = V(ts, [y0, y1], T.rq[:], T.rv[:], 255.0 * U, 4096.0, A.min, A.mult)
-    send_all([rq], "rr", T.rq[:], [T.rqs[:, 2 * rel(d, i):2 * rel(d, i) + 2] for i in others])
+    send([rq], "rr", T.rq[:], all_, [T.rqs[:, 2 * rel(d, i):2 * rel(d, i) + 2] for i in others])
+    cut = 2048 - P * d
+    ga = S([gi, io], T.ab[:, 0:cut], T.iot[:, 0:cut], F.Identity, bias=float(P * d))
+    if d:
+        ga = S([gi, io], T.ab[:, cut:2048], T.iot[:, cut:2048], F.Identity, bias=float(P * d - 2048))
     for k in range(8):
-        oq = D("y", [("rr", 7 * neng)], "dofq", T.ofq[16 * k:16 * k + 16, 2:16], T.rqs[d:128:8, 2:16])
+        D("ys"[k % 2], [("rr", 7 * neng)], ("dofq", "dofs")[k % 2], T.ofq[16 * k:16 * k + 16, 2:16], T.rqs[d:128:8, 2:16])
+    oq = [("dofq", 64), ("dofs", 64)]
     z = V(tt, [kb, cr], T.zz2[:], T.kb2[:], T.cr[:], A.add)
-    z = onto(2, z)
+    z = V(tc, [z, dup], T.ex2[:], T.zz2[:].indirect(T.dup[:]))
+    z = onto(2, [z])
     ti = T.ti
-    zi = V(ts, [z], ti[:, 16:32], T.m12[:], 4096.0, None, A.mult)
+    zi = V(ts, [z], ti[:, 16:32], T.mr2[:, 7:512:32], 4096.0, None, A.mult)
     ky = V(ts, [zi], ti[:, 48:64], ti[:, 16:32], 12, 511, A.logical_shift_right, A.bitwise_and)
     ci = V(ts, [zi], ti[:, 32:48], ti[:, 16:32], 4095, None, A.bitwise_and)
     kq = V(ts, [zi], ti[:, 112:128], ti[:, 16:32], 21, None, A.logical_shift_right)
     kf = V(ts, [ky], ti[:, 64:80], ti[:, 48:64], float(CAP), None, A.is_le)
-    pc = V(tc, [oq, q1], T.sp[:].bitcast(u32), T.hq[:].bitcast(u32).indirect(T.ofq[:, 2:16]))
-    pk = S([oq, q1], T.sps[:], T.hqs[:].indirect(T.ofq[:, 2:16]), F.Copy)
+    pc = V(tc, oq + [q1], T.sp[:].bitcast(u32), T.hq[:].bitcast(u32).indirect(T.ofq[:, 2:16]))
+    pk = S(oq + [q1], T.sps[:], T.hqs[:].indirect(T.ofq[:, 2:16]), F.Copy)
     ca, cb = [], []
     for i in others:
         a, b = CAP * (rel(i, d) - 1), P + CAP * (rel(d, i) - 1)
@@ -319,9 +374,11 @@ def rank_program(g, core, T, topo):
     hm = V(ts, [hb], ti[:, 176:192], ti[:, 128:144], -127.0, None, A.mult)
     x = V(tt, [tl, hm], ti[:, 224:240], ti[:, 144:160], ti[:, 176:192], A.add)
     os2 = V(tc, [x], T.ofs2[:], ti[:, 224:240])
-    sr2 = S([os2], T.scr2[:], T.s2[:].indirect(T.ofs2[:]), F.Copy)
+    sr2 = S([os2], T.scr2[:], T.sc[:].indirect(T.ofs2[:]), F.Copy)
+    c1r = S([ox, ga], T.chr1[:], T.ab[:].indirect(T.ofx1[:]), F.Copy)
     c2r = S([oc2, ga], T.chr2[:], T.ab[:].indirect(T.ofc2[:]), F.Copy)
-    dc2 = D("s", [c2r], "dch2", T.ch[1:2, :], T.chr2[0:1, :])
+    D("s", [c1r], "dch1", T.ch[0:1, :], T.chr1[0:1, :])
+    D("s", [c2r], "dch2", T.ch[1:2, :], T.chr2[0:1, :])
 
     arr = ("rc", 14)
     pc = V(tc, [arr, ox2, q1b], T.x2[:].bitcast(u32), T.w2[:, 0:480].bitcast(u32).indirect(T.ofx2[:]))

@@ -2,19 +2,20 @@ from concourse.bass import DstId, RemoteDMATransfer
 from concourse.mybir import dt, AluOpType as A, AxisListType, ActivationFunctionType as F
 
 N, P, CAP = 8, 256, 32
-RELAYED = 2
+HALF = P // 2
+PIECES = 2
 BIG = 9e29
 U = 1.0 / 4096.0
 
 _f32, _i32, _u16, _bf = "float32", "int32", "uint16", "bfloat16"
-SCRATCH = {"ps": ("psum", [128, 2048], _f32), "pr": ("psum", [128, 2048], _f32), "sld": ("dram", [8, 128, 2], _f32)}
+SCRATCH = {"ps": ("psum", [128, 2048], _f32), "pr": ("psum", [128, 2048], _f32), "sld1": ("dram", [8, 128, 2], _f32), "sld2": ("dram", [8, 128, 2], _f32)}
 for _d, _l in (
-        (_bf, "e0t 1024 e1t 1024 e2t 1024 ut 16 ub 512 ones 128 at 2048 wt 512 h1 1024 h2 1024"),
-        (_f32, "tm1 1024 tm2 1024 sc 2048 iot 2048 ab 2048 rs 512 rsb 512 zer 256 ta 32 sb 32 tb 32 nq 128 cc 128 cct 128 cx 256 "
-               "fc 16 cr 256 ca 256 cb 256 d0 256 d1 256 rv 2 scr1 256 scr2 256 dg 256 dgo 256 scc 2 g1c 2 chr1 256 chr2 256 go 256 ys 256 "
-               "mc 128 mn 128 exm 256 k2 128 nx2 256 nt2 256 kb2 256 zz2 256"),
-        (_i32, "pt 64 pa 64 np 64 lo 32 hb 32 tl 32 hm 32 po 32 iz 16 ic 8 iy 32 ti 256"),
-        (_u16, "of 64 op2 32 rj 16 dup 32 dup4 32 rq 2 rqs 16 ofq 16 ofx1 16 ofx2 16 ofs2 16 ofc2 16")):
+        (_bf, "e0t 1024 e1t 1024 e2t 1024 ut 512 at 2048 wt 512 h1 1024 h2 1024"),
+        (_f32, "tm1 1024 tm2 1024 sc 2048 iot 2048 rs 512 rsb 512 zer 256 ta 32 sb 32 tb 32 nq 128 cc1 128 cct1 128 cx1 128 cr1 128 "
+               "cc2 128 cct2 128 cx2 256 cr2 288 fc 16 d0 256 d1 256 rv 2 scr1 256 scr2 256 scc 2 g0c 2 g1c 2 chr1 256 chr2 256 go 256 ys 256 "
+               "mc 128 mn 128 exm 256 k2 128 nx2 256 nt2 256 dc 256 zz2 256"),
+        (_i32, "pt 64 pa 64 np 64 lo 64 hb 64 tl 64 hm 64 po 64 iz 16 ij 8 ic 8 iy 32 ti 256 tj 256"),
+        (_u16, "of 64 op 64 rj 16 rh 8 dup 32 dup4 32 rq 2 rqs 16 ofq 16 ofx1 16 ofs1 16 ofa1 16 ofx2 16 ofs2 16 ofa2 16")):
     _w = _l.split()
     for _k in range(0, len(_w), 2):
         SCRATCH[_w[_k]] = ("sbuf", [128, int(_w[_k + 1])], _d)
@@ -27,44 +28,68 @@ for _t in ("1", "2"):
                    ("ad", 256), ("mk", 256), ("ct", 256), ("ex", 512), ("tr", 512), ("mr", 512)):
         SCRATCH[_n + _t] = ("sbuf", [128, _c], _f32)
 
-SEMAPHORES = ["cv", "cs", "ct", "cg", "l0", "ls", "rg", "rr", "rc", "hc", "hk"] + ["h%d" % i for i in range(N)]
-SEMAPHORES += ["de0", "du", "dp1", "dp2", "da", "de1", "dw", "de2", "dog", "ds2", "ds3", "dofq", "dofs", "dch1", "dch2", "dout"]
-
-
-def relayed(d, cores, topo):
-    me = cores[d]
-    here = topo.chip(me)
-    far = [i for i in range(N) if i != d and not topo.mates(here, topo.chip(cores[i])) and not topo.same_plane(here, topo.chip(cores[i]))]
-    far.sort(key=lambda i: (-min((i - d) % N, (d - i) % N), (i - d) % N))
-    far = far[:RELAYED]
-    for h in topo.cores_of(me):
-        if topo.die(h) != topo.die(me) and all(topo.may_write(h, cores[i]) for i in far):
-            return far, h
-    return [], None
+SEMAPHORES = ["cv", "cs", "ct", "cg", "l0", "ls", "r0", "rg", "rr", "rc", "hk"] + ["h%d" % i for i in range(N)] + ["hc%d" % i for i in range(PIECES)]
+SEMAPHORES += ["de0", "du", "dp1", "dp2", "da", "de1", "dw", "de2", "dog0", "dog1", "ds0", "ds1", "ds2", "ds3", "dsc", "dofq", "dofs", "dch", "dout"]
 
 
 def bits(m):
     return bin(m).count("1")
 
 
+def plan(d, cores, topo):
+    me = cores[d]
+    here = topo.chip(me)
+    order = sorted([i for i in range(N) if i != d], key=lambda i: (-min((i - d) % N, (d - i) % N), (i - d) % N))
+    mate = [i for i in order if topo.mates(here, topo.chip(cores[i]))]
+    plane = [i for i in order if topo.same_plane(here, topo.chip(cores[i]))]
+    far = [i for i in order if i not in mate + plane]
+    used, out = [me], []
+    for same, ranks in ((True, far[2:] + mate), (True, plane[1:]), (False, far[:1] + plane[:1]), (False, far[1:2])):
+        able = [h for h in topo.cores_of(me) if h not in used and (topo.die(h) == topo.die(me)) == same and all(topo.may_write(h, cores[i]) for i in ranks)]
+        able.sort(key=lambda h: sum(topo.may_write(h, cores[i]) for i in order))
+        used.append(able[0])
+        out.append((able[0], ranks))
+    return [(h, r, out[k + 1][0] if k % 2 == 0 else None) for k, (h, r) in enumerate(out)]
+
+
+def chip_engines(topo, core, near, far):
+    return topo.mask(core, near) & ~topo.mask(core, far)
+
+
+def pieces(T):
+    w = P // PIECES
+    out = []
+    for k in range(PIECES):
+        out.append(("hc%d" % k, T.hr[:, w * k:w * k + w].bitcast(dt.uint8), lambda q, k=k: T.hw[:, P * q + w * k:P * q + w * k + w].bitcast(dt.uint8)))
+    out.append(("hk", T.hrs[:], lambda q: T.hws[:, P * q:P * q + P]))
+    return out
+
+
+def dst_of(topo, c):
+    rid, pid, _ = topo.addr(c)
+    return DstId(rid=rid, pnc=pid)
+
+
 def hand_on(g, core, T, topo):
     for d in range(N):
-        far, h = relayed(d, T.cores, topo)
-        if h != core:
-            continue
-        came = bits(topo.mask(T.cores[d], core) & ~topo.mask(T.cores[d], T.cores[far[0]]))
-        mask = topo.mask(core, T.cores[far[0]])
-        ids = []
-        for i in far:
-            rid, pid, _ = topo.addr(T.cores[i])
-            ids.append(DstId(rid=rid, pnc=pid))
-        o = [P * ((d - i) % N) for i in far]
-        for sem, src, dsts in (("hc", T.hr[:].bitcast(dt.uint8), [T.hw[:, a:a + P].bitcast(dt.uint8) for a in o]),
-                               ("hk", T.hrs[:], [T.hws[:, a:a + P] for a in o])):
-            g.wait_ge(T.sem[sem], came)
-            g.remote_dma_fused([RemoteDMATransfer(dst_ids=ids, dma_engine_mask=mask, remote_sem=T.sem["h%d" % d], srcs=[src], dsts=dsts)],
-                               local_sem=T.sem.ls)
-        g.wait_ge(T.sem.ls, 2 * bits(mask))
+        for h, ranks, sub in plan(d, T.cores, topo):
+            if h != core:
+                continue
+            far = T.cores[ranks[0]]
+            mask = topo.mask(core, far)
+            came = bits(chip_engines(topo, T.cores[d], core, far))
+            n = 0
+            for sem, here, land in pieces(T):
+                g.wait_ge(T.sem[sem], came)
+                ts = [RemoteDMATransfer(dst_ids=[dst_of(topo, T.cores[i]) for i in ranks], dma_engine_mask=mask, remote_sem=T.sem["h%d" % d], srcs=[here],
+                                        dsts=[land((d - i) % N) for i in ranks])]
+                n += bits(mask)
+                if sub is not None:
+                    m = chip_engines(topo, core, sub, far)
+                    ts.insert(0, RemoteDMATransfer(dst_ids=[dst_of(topo, sub)], dma_engine_mask=m, remote_sem=T.sem[sem], srcs=[here], dsts=[here]))
+                    n += bits(m)
+                g.remote_dma_fused(ts, local_sem=T.sem.ls)
+            g.wait_ge(T.sem.ls, n)
 
 
 def rank_program(g, core, T, topo):
@@ -115,18 +140,14 @@ def rank_program(g, core, T, topo):
     u8, u32 = dt.uint8, dt.uint32
 
     others = [(d + k) % N for k in range(1, N)]
-
-    def dst(c):
-        rid, pid, _ = topo.addr(c)
-        return DstId(rid=rid, pnc=pid)
-
-    mask = topo.mask(core, cores[others[0]])
-    for i in others:
-        mask &= topo.mask(core, cores[i])
-    engs = [e for e in topo.engines(core, cores[others[0]]) if mask >> e & 1]
+    all_ = [cores[i] for i in others]
+    mask = topo.mask(core, all_[0])
+    for c in all_:
+        mask &= topo.mask(core, c)
+    engs = [e for e in topo.engines(core, all_[0]) if mask >> e & 1]
     neng = len(engs)
-    far, helper = relayed(d, cores, topo)
-    near = [i for i in others if i not in far]
+    helpers = [h for h, r, sub in plan(d, cores, topo)][0::2]
+    inner = chip_engines(topo, core, helpers[0], all_[0])
 
     def sent(name, n):
         total[name] = total.get(name, 0) + n
@@ -134,15 +155,13 @@ def rank_program(g, core, T, topo):
 
     def send(deps, sem, src, to, dsts, local="ls", m=mask):
         wait("g", deps)
-        g.remote_dma_fused([RemoteDMATransfer(dst_ids=[dst(c) for c in to], dma_engine_mask=m, remote_sem=T.sem[sem], srcs=[src], dsts=dsts)],
+        g.remote_dma_fused([RemoteDMATransfer(dst_ids=[dst_of(topo, c) for c in to], dma_engine_mask=m, remote_sem=T.sem[sem], srcs=[src], dsts=dsts)],
                            local_sem=T.sem[local])
         return sent(local, bits(m))
 
-    all_ = [cores[i] for i in others]
-
     def send_each(deps, sem, pairs):
         wait("g", deps)
-        g.remote_dma_fused([RemoteDMATransfer(dst_ids=[dst(all_[k])], dma_engine_mask=1 << engs[k], remote_sem=T.sem[sem], srcs=[a], dsts=[b])
+        g.remote_dma_fused([RemoteDMATransfer(dst_ids=[dst_of(topo, all_[k])], dma_engine_mask=1 << engs[k], remote_sem=T.sem[sem], srcs=[a], dsts=[b])
                             for k, (a, b) in enumerate(pairs)], local_sem=T.sem.ls)
         return sent("ls", len(pairs))
 
@@ -150,50 +169,58 @@ def rank_program(g, core, T, topo):
         return (s - r) % N
 
     e0 = D("y", [], "de0", T.e0t[:], T.e0[:, :])
-    uu = D("y", [], "du", T.ut[:, 0:8], T.u[:, 0:8])
+    uu = D("s", [], "du", T.ut[:], T.u[:, :])
     for k in range(8):
         p1 = D("y", [], "dp1", T.pt[16 * k:16 * k + 16, 0:32], T.p1[:, 32 * (k % 2):32 * (k % 2) + 32])
-    da = D("y", [e0], "da", T.at[:], T.a[:, :])
+    da = D("y", [], "da", T.at[:], T.a[:, :])
 
-    gp = G(g.iota, [], T.ic[:, 0:1], [[0, 1]], 0, 1)
     gi = G(g.iota, [], T.iot[:, 0:512], [[1, 512]], 0, 0, allow_small_or_imprecise_dtypes=True)
+    gp = G(g.iota, [], T.ic[:, 0:1], [[0, 1]], 0, 1)
     giy = G(g.iota, [], T.iy[:], [[16, 16], [0, 2]], 0, 0)
     giz = G(g.iota, [], T.iz[:], [[16, 2], [32, 4], [0, 2]], 0, 0)
+    gij = G(g.iota, [], T.ij[:], [[16, 8]], 0, 0)
+    c0 = V(ms, [], T.sc[:, 0:512], 0.0)
+    zr = V(ms, [], T.zer[:], 0.0)
+    r1 = V(ms, [], T.rs[:], BIG)
+    for k in (1, 2, 3):
+        sc0 = S([c0], T.sc[:, 512 * k:512 * k + 512], T.sc[:, 0:512], F.Copy)
     for k in (1, 2, 3):
         io = S([gi], T.iot[:, 512 * k:512 * k + 512], T.iot[:, 0:512], F.Identity, bias=512.0 * k)
-    on = V(ms, [], T.ones[:], 1.0)
-    r1 = V(ms, [], T.rs[:], BIG)
-    r2 = V(ms, [], T.rsb[:, 0:256], BIG)
-    zr = V(ms, [], T.zer[:], 0.0)
-    sb0 = V(ms, [], T.sb[:], 0.0)
-    fl0 = {1: V(ms, [], T.fl1[:, 0:512:4], 0.0)}
     rs = V(ms, [r1], T.rs[:, 0:512:4], -BIG)
-    rsb = V(ms, [r2], T.rsb[:, 0:256:16], -BIG)
 
     q0 = V(qz, [e0], T.hw[:, 0:P], T.hws[:, 0:P], T.e0t[:])
-    hcode, hscale = T.hw[:, 0:P].bitcast(u8), T.hws[:, 0:P]
-    if far:
-        send([q0], "hc", hcode, [helper], [T.hr[:].bitcast(u8)], "l0", topo.mask(core, helper) & ~mask)
-    to = [cores[i] for i in near]
-    send([q0], "h%d" % d, hcode, to, [T.hw[:, P * rel(d, i):P * rel(d, i) + P].bitcast(u8) for i in near], "l0")
-    if far:
-        send([q0], "hk", hscale, [helper], [T.hrs[:]], "l0", topo.mask(core, helper) & ~mask)
-    l0 = send([q0], "h%d" % d, hscale, to, [T.hws[:, P * rel(d, i):P * rel(d, i) + P] for i in near], "l0")
-    e1 = D("y", [l0], "de1", T.e1t[:], T.e1[:, :])
-    for k in range(8):
-        p2 = D("y", [l0], "dp2", T.pt[16 * k:16 * k + 16, 32:64], T.p2[:, 32 * (k % 2):32 * (k % 2) + 32])
-    e2 = D("y", [l0], "de2", T.e2t[:], T.e2[:, :])
-    dw = D("y", [l0], "dw", T.wt[:], T.w[:, :])
+    quq = V(qz, [uu], T.uq[:], T.uqs[:], T.ut[:])
 
-    for k in range(4):
-        ubk = V(ts, [on, uu], T.ub[:, k:512:4], T.ones[:], T.ut[:, k:k + 1], None, A.mult)
-    quq = V(qz, [ubk], T.uq[:], T.uqs[:], T.ub[:])
+    def scores(deps, w, ws, ps):
+        return MM(deps + [quq], ps, w, ws, T.uq[:], T.uqs[:])
+
+    for k in (0, 1):
+        m = scores([q0], T.hw[:, HALF * k:HALF * k + HALF], T.hws[:, HALF * k:HALF * k + HALF], T.ps[:, 512 * k:512 * k + 128])
+    g0 = V(tc, [m], T.g0c[:], T.ps[:, 0:1024:512])
+    parts = pieces(T)
+    send([q0], parts[0][0], parts[0][2](0), helpers, [parts[0][1]] * 2, "l0", inner)
+    send([g0], "r0", T.g0c[:], all_, [T.sld1[rel(d, i)] for i in others])
+    for sem, there, here in parts[1:]:
+        send([q0], sem, here(0), helpers, [there] * 2, "l0", inner)
+    og = D("y", [g0], "dog0", T.sld1[0], T.g0c[:])
+
+    def places(n, lo, hb, tl, hm, po):
+        a1 = V(ts, [n[0]], lo, n[1], 127, None, A.bitwise_and)
+        a2 = V(ts, [n[0]], hb, n[1], 7, 1, A.logical_shift_right, A.bitwise_and)
+
+        def rest():
+            a3 = V(tt, [a1], tl, n[1], lo, A.add)
+            a4 = V(ts, [a2], hm, hb, -127.0, None, A.mult)
+            return V(tt, [a3, a4], po, tl, hm, A.add)
+        return rest
 
     def listed(t, dep):
         o = slice(32 * t - 32, 32 * t)
         x = V(ts, [dep], T.pa[:, o], T.pt[:, o], float(2048 - P * d), None, A.add)
         x = V(ts, [x], T.np[:, o], T.pa[:, o], 2047, None, A.bitwise_and)
-        return x, V(tc, [x], T.of[:, o], T.np[:, o])
+        of = V(tc, [x], T.of[:, o], T.np[:, o])
+        x = places((x, T.np[:, o]), T.lo[:, o], T.hb[:, o], T.tl[:, o], T.hm[:, o], T.po[:, o])()
+        return of, V(tc, [x], T.op[:, o], T.po[:, o])
 
     def row(t, of):
         return S([gi, io, of], T["nr%d" % t][:], T.iot[:].indirect(T.of[:, 32 * t - 32:32 * t]), F.Copy, scale=U)
@@ -203,42 +230,53 @@ def rank_program(g, core, T, topo):
         z = V(tt, [nr], v[:, 0:511], r[:, 0:511], r[:, 1:512], A.subtract)
         return V(tc, [z], v[:, 3:512:4], r[:, 3:512:4])
 
-    of1 = listed(1, p1)[1]
-    nr, vd = {1: row(1, of1)}, {}
+    nr, vd, fl0, ops = {}, {}, {}, {}
+    of1, ops[1] = listed(1, p1)
+    nr[1] = row(1, of1)
     ic, fc = T.ic, T.fc
     b1 = V(ts, [gp], ic[:, 1:2], ic[:, 0:1], 7, None, A.bitwise_and)
     b4 = V(ts, [gp], ic[:, 4:5], ic[:, 0:1], 3, None, A.logical_shift_right)
     b5 = V(ts, [gp], ic[:, 5:6], ic[:, 0:1], 15, None, A.bitwise_and)
     b2 = V(ts, [b1], ic[:, 2:3], ic[:, 1:2], float(N - d), None, A.add)
     b3 = V(ts, [b2], ic[:, 3:4], ic[:, 2:3], 7, None, A.bitwise_and)
+    fl0[1] = V(ms, [], T.fl1[:, 0:512:4], 0.0)
     b6 = V(tc, [b3, b4, b5], fc[:, 0:3], ic[:, 3:6])
+    rh = V(tc, [gij], T.rh[:], T.ij[:])
     c1 = V(ts, [b6], fc[:, 3:4], fc[:, 0:1], -256.0 * U, -127.5 * U, A.mult, A.add)
     c2 = V(ts, [b6], fc[:, 4:5], fc[:, 0:1], 0.0, -100.0, A.is_equal, A.mult)
     c4 = V(ts, [b6], fc[:, 10:11], fc[:, 0:1], 0.0, None, A.is_equal)
     dup = V(ts, [b6, giy], T.dup[:], T.iy[:], fc[:, 2:3], None, A.add)
     nbc = V(tt, [c1, c2], fc[:, 5:6], fc[:, 3:4], fc[:, 4:5], A.add)
-    vd[1] = deltas(1, nr[1])
-    nq = V(ts, [nr[1], c4], T.nq[:], T.nr1[:, 0:512:4], fc[:, 10:11], None, A.mult)
+    nq = S([nr[1], c4], T.nq[:], T.nr1[:, 0:512:4], F.Copy, scale=fc[:, 10:11])
+    r2 = V(ms, [], T.rsb[:, 0:256], BIG)
+    sb0 = V(ms, [], T.sb[:], 0.0)
+    rsb = V(ms, [r2], T.rsb[:, 0:256:16], -BIG)
     qa = V(qz, [da], T.aq[:], T.aqs[:], T.at[:])
+    vd[1] = deltas(1, nr[1])
 
-    scd = []
-    slots = [rel(i, d) for i in range(N) if i != d]
-    slots.sort(key=lambda k: (d in relayed((d + k) % N, cores, topo)[0], -k))
-    for j, k in enumerate([0] + slots):
-        b = j % 4
-        deps = [quq, q0] + ([("h%d" % ((d + k) % N), 2 * neng)] if k else []) + ([scd[j - 4]] if j > 3 else [])
-        mt = MM(deps, T.ps[:, 512 * b:512 * b + P], T.uq[:], T.uqs[:], T.hw[:, P * k:P * k + P], T.hws[:, P * k:P * k + P])
-        o, i = T.sc[:, P * k:P * k + P], T.ps[:, 512 * b:512 * b + P]
-        scd.append(V(tc, [mt], o, i) if j % 2 else S([mt], o, i, F.Copy))
+    def spread(land, deps, sems):
+        for k in range(8):
+            D("ys"[k % 2], deps, sems[k % 2], T.sc[16 * k:16 * k + 1, :], land[:])
+        return [(n, total[n]) for n in sems]
 
-    def choose(t, win, off, deps):
+    def choose(t, deps):
         ga_, mx_, fl_, cn_ = T["ga%d" % t], T["mx%d" % t], T["fl%d" % t], T["cn%d" % t]
-        x1 = V(tc, deps, ga_[:, 0:256], win.indirect(off[:, 0:16]))
-        x2 = S(deps, ga_[:, 256:512], win.indirect(off[:, 16:32]), F.Copy)
+        deps = deps + [ops[t]]
+        x1 = V(tc, deps, ga_[:, 0:256], T.sc[:].indirect(T.op[:, 32 * t - 32:32 * t - 16]))
+        x2 = S(deps, ga_[:, 256:512], T.sc[:].indirect(T.op[:, 32 * t - 16:32 * t]), F.Copy)
         m = V(scan, [x1, x2, rs], mx_[:], T.rs[:], ga_[:], -BIG, A.min, A.max)
         for k in (1, 2, 3):
             f = V(tt, [m, fl0[t]], fl_[:, k:512:4], ga_[:, k:512:4], mx_[:, k - 1:512:4], A.is_le)
         return V(scan, [f, vd[t]], cn_[:], fl_[:], T["vd%d" % t][:], 0.0, A.mult, A.add), x1, x2
+
+    def whole(t, n, lists, out, deps):
+        cc, cct, cx, cn = T["cc%d" % t], T["cct%d" % t], T["cx%d" % t], T["cn%d" % t]
+        w, k = n // 2, lists.shape[1] // 2
+        x = V(tc, deps, cc[:], cn[:, 3:512:4])
+        x = V(tp, [x], cct[:], cc[:])
+        x1 = V(tc, [x], cx[:, 0:w], cct[:].indirect(lists[:, 0:k]))
+        x2 = S([x], cx[:, w:n], cct[:].indirect(lists[:, k:2 * k]), F.Copy)
+        return V(tp, [x1, x2], out, cx[:])
 
     def keep1(c, deps):
         x = S(deps + [nbc], T.ad1[:, 0:128], c, F.Abs, bias=fc[:, 5:6])
@@ -253,95 +291,107 @@ def rank_program(g, core, T, topo):
         x = V(ts, [x], T.k2[:], T.ct1[:, 0:128], T.tb[:, 31:32], float(CAP), A.add, A.is_le)
         return V(tt, [x, y], T.ex1[:, 0:256], T.k2[:].indirect(T.dup[:, 0:16]), T.exm[:], A.mult)
 
-    def whole(cn, deps):
-        x = V(tc, deps, T.cc[:], cn)
-        x = V(tp, [x], T.cct[:], T.cc[:])
-        x1 = V(tc, [x, rj], T.cx[:, 0:128], T.cct[:].indirect(T.rj[:, 0:8]))
-        x2 = S([x, rj], T.cx[:, 128:256], T.cct[:].indirect(T.rj[:, 8:16]), F.Copy)
-        return V(tp, [x1, x2], T.cr[:], T.cx[:])
-
     def onto(t, deps):
         w = P * t
         x = V(tp, deps, T["tr%d" % t][:, 0:w], T["ex%d" % t][:, 0:w])
         return V(scan, [x, rsb], T["mr%d" % t][:, 0:w], T.rsb[:, 0:w], T["tr%d" % t][:, 0:w], -BIG, A.min, A.max)
 
-    def states(x, xs, ps, et, h, tm, edep, deps):
-        for i in range(4):
-            m = MM(deps + [qa], ps[:, 512 * i:512 * i + P], T.aq[:, 128 * i:128 * i + 128], T.aqs[:, 128 * i:128 * i + 128], x[:], xs[:])
-            s = S([m], tm[:, P * i:P * i + P], ps[:, 512 * i:512 * i + P], F.Copy, scale=0.05)
-            a = V(tt, [s, edep], h[:, i:1024:4], tm[:, P * i:P * i + P], et[:, i:1024:4], A.add)
-        return a
+    def states(x, xs, banks, et, h, tm, q, qs, edep, picks, between=None):
+        m, s, out = {}, {}, []
+        for k in (0, 1):
+            for i in range(4):
+                m[k, i] = MM(picks[k] + [qa], banks[k][:, 512 * i:512 * i + HALF], T.aq[:, 128 * i:128 * i + 128], T.aqs[:, 128 * i:128 * i + 128],
+                             x[:, HALF * k:HALF * k + HALF], xs[:, HALF * k:HALF * k + HALF])
+        for k in (0, 1):
+            for i in range(4):
+                o = P * i + HALF * k
+                s[k, i] = S([m[k, i]], tm[:, o:o + HALF], banks[k][:, 512 * i:512 * i + HALF], F.Copy, scale=0.05)
+            if k == 0 and between is not None:
+                between()
+        for k in (0, 1):
+            for i in range(4):
+                o = P * i + HALF * k
+                c = slice(4 * HALF * k + i, 4 * HALF * (k + 1), 4)
+                a = V(tt, [s[k, i], edep], h[:, c], tm[:, o:o + HALF], et[:, c], A.add)
+            out.append(V(qz, [a], q[:, HALF * k:HALF * k + HALF], qs[:, HALF * k:HALF * k + HALF], h[:, 4 * HALF * k:4 * HALF * (k + 1)]))
+        return out
 
-    ch, g1v, g1s = choose(1, T.sc[:], T.of[:, 0:32], scd + [of1])
-    z = onto(1, [keep1(T.cn1[:, 3:512:4], [ch])])
-    ox = V(ts, [z], T.ofx1[:, 0:8], T.mr1[:, 7:256:32], 4096.0, None, A.mult)
-    ox = V(ts, [z], T.ofx1[:, 8:16], T.mr1[:, 23:256:32], 4096.0, None, A.mult)
-    pc = V(tc, [ox], T.x1[:].bitcast(u32), T.hw[:].bitcast(u32).indirect(T.ofx1[:]))
-    pk = S([ox], T.x1s[:], T.hws[:].indirect(T.ofx1[:]), F.Copy)
-    sr = S([ox], T.scr1[:], T.sc[:].indirect(T.ofx1[:]), F.Copy)
-    for k in (0, 1):
-        dg = G(g.affine_select, [sr], T.dg[:, 128 * k:128 * k + 128], T.scr1[:, 128 * k:128 * k + 128], [[-1, 128]], A.is_equal, 0.0, 0, 1)
-    hd = states(T.x1, T.x1s, T.pr, T.e1t, T.h1, T.tm1, e1, [pc, pk])
-    for k in (0, 1):
-        sc1 = S([dg], T.dgo[:, 128 * k:128 * k + 128], T.dg[:, 128 * k:128 * k + 128], F.Copy, accum_out=T.scc[:, k:k + 1])
-    q1 = V(qz, [hd], T.hq[:], T.hqs[:], T.h1[:])
-    for k in (0, 1):
-        mg = MM([q1] + scd, T.ps[:, 512 * k:512 * k + 128], T.hq[:, 128 * k:128 * k + 128], T.hqs[:, 128 * k:128 * k + 128], T.uq[:], T.uqs[:])
-    q1b = V(qz, [hd], T.w2[:, 0:P], T.w2s[:, 0:P], T.h1[:])
-    g1 = V(tt, [mg, sc1], T.g1c[:], T.ps[:, 0:1024:512], T.scc[:], A.add)
+    got = spread(T.sld1, [og, ("r0", 7 * neng), c0, sc0], ("ds0", "ds1"))
+    e1 = D("y", got, "de1", T.e1t[:], T.e1[:, :])
+    for k in range(8):
+        p2 = D("y", [], "dp2", T.pt[16 * k:16 * k + 16, 32:64], T.p2[:, 32 * (k % 2):32 * (k % 2) + 32])
+    e2 = D("y", [], "de2", T.e2t[:], T.e2[:, :])
+    dw = D("y", [], "dw", T.wt[:], T.w[:, :])
+    ch, g0v, g0s = choose(1, got)
+    cr = whole(1, 128, T.rh, T.cr1[:], [ch, rh])
+    z = onto(1, [keep1(T.cr1[:], [cr])])
+    o1 = V(ts, [z], T.ofx1[:, 0:8], T.mr1[:, 7:256:32], 4096.0, None, A.mult)
+    o2 = V(ts, [z], T.ofx1[:, 8:16], T.mr1[:, 23:256:32], 4096.0, None, A.mult)
+    arr = [("h%d" % i, (PIECES + 1) * neng) for i in others]
+    tj = T.tj
+    ji = V(tc, [o2], tj[:, 0:16], T.ofx1[:])
+    rest = places((ji, tj[:, 0:16]), tj[:, 16:32], tj[:, 32:48], tj[:, 48:64], tj[:, 64:80], tj[:, 80:96])
 
-    send([g1], "rg", T.g1c[:], all_, [T.sld[rel(d, i)] for i in others])
-    og = D("y", [g1], "dog", T.sld[0], T.g1c[:])
-    x, of2 = listed(2, p2)
+    def pick(x, xs, w, ws, o, k, deps):
+        c = slice(HALF * k, HALF * k + HALF)
+        a = V(tc, deps, x[:, c].bitcast(u32), w.bitcast(u32).indirect(o[:, 8 * k:8 * k + 8]))
+        return [a, S(deps, xs[:, c], ws.indirect(o[:, 8 * k:8 * k + 8]), F.Copy)]
+
+    picks = [pick(T.x1, T.x1s, T.hw[:], T.hws[:], T.ofx1, k, [o1, o2] + arr) for k in (0, 1)]
+    os1 = V(tc, [rest()], T.ofs1[:], tj[:, 80:96])
+    srs = []
+
+    def chosen_scores():
+        srs.append(S([os1], T.scr1[:], T.sc[:].indirect(T.ofs1[:]), F.Copy))
+        for k in (0, 1):
+            srs.append(D("y", [srs[0]], "dsc", T.scc[:, k:k + 1], T.scr1[0:1, HALF * k:HALF * k + HALF]))
+
+    q1 = states(T.x1, T.x1s, (T.pr, T.ps), T.e1t, T.h1, T.tm1, T.hq, T.hqs, e1, picks, chosen_scores)
+    for k in (0, 1):
+        mg = scores([q1[k]], T.hq[:, HALF * k:HALF * k + HALF], T.hqs[:, HALF * k:HALF * k + HALF], T.pr[:, 512 * k:512 * k + 128])
+    g1 = V(tt, [mg, srs[2]], T.g1c[:], T.pr[:, 0:1024:512], T.scc[:], A.add)
+
+    send([g1], "rg", T.g1c[:], all_, [T.sld2[rel(d, i)] for i in others])
+    og = D("y", [g1], "dog1", T.sld2[0], T.g1c[:])
+    of2, ops[2] = listed(2, p2)
     nr[2] = row(2, of2)
-    n2 = T.np[:, 32:64]
-    a1 = V(ts, [x], T.lo[:], n2, 127, None, A.bitwise_and)
-    a2 = V(ts, [x], T.hb[:], n2, 7, 1, A.logical_shift_right, A.bitwise_and)
-    a3 = V(tt, [a1], T.tl[:], n2, T.lo[:], A.add)
-    a4 = V(ts, [a2], T.hm[:], T.hb[:], -127.0, None, A.mult)
     dup4 = V(ts, [b6, giy], T.dup4[:], T.iy[:], fc[:, 2:3], 4.0, A.add, A.mult)
-    a5 = V(tt, [a3, a4], T.po[:], T.tl[:], T.hm[:], A.add)
     fl0[2] = V(ms, [], T.fl2[:, 0:512:4], 0.0)
-    op2 = V(tc, [a5], T.op2[:], T.po[:])
     i5c = V(ts, [b6], fc[:, 6:7], fc[:, 0:1], 512.0, None, A.mult)
     c3 = V(ts, [b6], fc[:, 7:8], fc[:, 0:1], 512.0 + 256.0 * U, 1.0, A.mult, A.add)
     rj = V(tc, [giz], T.rj[:], T.iz[:])
     t0c = V(tt, [c3], fc[:, 8:9], fc[:, 7:8], fc[:, 1:2], A.add)
     r2 = V(ms, [], T.rsb[:, 256:512], BIG)
     t1c = V(ts, [t0c], fc[:, 9:10], fc[:, 8:9], -1.0, -16.0, A.mult, A.add)
+    cz = V(ms, [], T.cr2[:, 0:32], 0.0)
     vd[2] = deltas(2, nr[2])
     z = S([nr[2], dup4], T.nx2[:], T.nr2[:].indirect(T.dup4[:, 0:16]), F.Copy)
     z = V(tp, [z], T.nt2[:], T.nx2[:])
     rsb = V(ms, [r2], T.rsb[:, 256:512:16], -BIG)
     n0 = V(ts, [z], T.ti[:, 0:8], T.nt2[:, 0:256:32], 4096.0, None, A.mult)
     n0 = V(ts, [z], T.ti[:, 8:16], T.nt2[:, 16:256:32], 4096.0, None, A.mult)
+    q1b = V(qz, q1, T.w2[:, 0:P], T.w2s[:, 0:P], T.h1[:])
     qw = V(qz, [dw], T.wq[:], T.wqs[:], T.wt[:])
-    for k in range(8):
-        D("ys"[k % 2], [og, ("rg", 7 * neng), g1v, g1s, sr], ("ds2", "ds3")[k % 2], T.sc[16 * k:16 * k + 1, :], T.sld[:])
+    got = spread(T.sld2, [og, ("rg", 7 * neng), g0v, g0s, srs[0]], ("ds2", "ds3"))
 
-    ch = choose(2, T.sc[:], T.op2, [("ds2", 64), ("ds3", 64), op2])[0]
-    cr = whole(T.cn2[:, 3:512:4], [ch])
-    x = S([cr, nbc], T.ad2[:], T.cr[:], F.Abs, bias=fc[:, 5:6])
-    y1 = S([cr, t1c], T.cb[:], T.cr[:], F.Identity, bias=fc[:, 9:10])
-    y0 = V(ts, [cr, t0c], T.ca[:], T.cr[:], fc[:, 8:9], None, A.subtract)
-    x = V(ts, [x], T.mk2[:], T.ad2[:], 128.0 * U, None, A.is_lt)
-    x = V(scan, [x, zr, i5c], T.ct2[:], T.mk2[:], T.zer[:], fc[:, 6:7], A.add, A.add)
-    kb = V(tt, [x], T.kb2[:], T.mk2[:], T.ct2[:], A.mult)
-    y0 = V(tt, [kb, y0], T.d0[:], T.kb2[:], T.ca[:], A.add)
-    y1 = V(tt, [kb, y1], T.d1[:], T.kb2[:], T.cb[:], A.add)
+    ch = choose(2, got)[0]
+    cr_ = T.cr2[:, 32:288]
+    cr = whole(2, 256, T.rj, cr_, [ch, rj])
+    x = S([cr, nbc], T.ad2[:], cr_, F.Abs, bias=fc[:, 5:6])
+    y = V(tt, [cr, cz], T.dc[:], cr_, T.cr2[:, 31:287], A.subtract)
+    mk = V(ts, [x], T.mk2[:], T.ad2[:], 128.0 * U, None, A.is_lt)
+    z = V(scan, [mk, y, i5c], T.ct2[:], T.mk2[:], T.dc[:], fc[:, 6:7], A.add, A.add)
+    zz = V(tt, [z], T.zz2[:], T.mk2[:], T.ct2[:], A.mult)
+    y1 = S([zz, t1c], T.d1[:], T.zz2[:], F.Identity, bias=fc[:, 9:10])
+    y0 = V(ts, [zz, t0c], T.d0[:], T.zz2[:], fc[:, 8:9], None, A.subtract)
     y0 = V(red, [y0], T.rv[:, 0:1], T.d0[:], AxisListType.X, A.min, apply_absolute_value=True)
     y1 = V(red, [y1], T.rv[:, 1:2], T.d1[:], AxisListType.X, A.min, apply_absolute_value=True)
     rq = V(ts, [y0, y1], T.rq[:], T.rv[:], 255.0 * U, 4096.0, A.min, A.mult)
     send([rq], "rr", T.rq[:], all_, [T.rqs[:, 2 * rel(d, i):2 * rel(d, i) + 2] for i in others])
-    cut = 2048 - P * d
-    ga = S([gi, io], T.ab[:, 0:cut], T.iot[:, 0:cut], F.Identity, bias=float(P * d))
-    if d:
-        ga = S([gi, io], T.ab[:, cut:2048], T.iot[:, cut:2048], F.Identity, bias=float(P * d - 2048))
     for k in range(8):
         D("ys"[k % 2], [("rr", 7 * neng)], ("dofq", "dofs")[k % 2], T.ofq[16 * k:16 * k + 16, 2:16], T.rqs[d:128:8, 2:16])
     oq = [("dofq", 64), ("dofs", 64)]
-    z = V(tt, [kb, cr], T.zz2[:], T.kb2[:], T.cr[:], A.add)
-    z = V(tc, [z, dup], T.ex2[:], T.zz2[:].indirect(T.dup[:]))
+    z = V(tc, [zz, dup], T.ex2[:], T.zz2[:].indirect(T.dup[:]))
     z = onto(2, [z])
     ti = T.ti
     zi = V(ts, [z], ti[:, 16:32], T.mr2[:, 7:512:32], 4096.0, None, A.mult)
@@ -349,8 +399,8 @@ def rank_program(g, core, T, topo):
     ci = V(ts, [zi], ti[:, 32:48], ti[:, 16:32], 4095, None, A.bitwise_and)
     kq = V(ts, [zi], ti[:, 112:128], ti[:, 16:32], 21, None, A.logical_shift_right)
     kf = V(ts, [ky], ti[:, 64:80], ti[:, 48:64], float(CAP), None, A.is_le)
-    pc = V(tc, oq + [q1], T.sp[:].bitcast(u32), T.hq[:].bitcast(u32).indirect(T.ofq[:, 2:16]))
-    pk = S(oq + [q1], T.sps[:], T.hqs[:].indirect(T.ofq[:, 2:16]), F.Copy)
+    pc = V(tc, oq + q1, T.sp[:].bitcast(u32), T.hq[:].bitcast(u32).indirect(T.ofq[:, 2:16]))
+    pk = S(oq + q1, T.sps[:], T.hqs[:].indirect(T.ofq[:, 2:16]), F.Copy)
     ca, cb = [], []
     for i in others:
         a, b = CAP * (rel(i, d) - 1), P + CAP * (rel(d, i) - 1)
@@ -367,32 +417,35 @@ def rank_program(g, core, T, topo):
     x = V(tt, [y], ti[:, 192:208], ti[:, 160:176], ti[:, 176:192], A.add)
     x = V(tt, [x], ti[:, 208:224], ti[:, 192:208], ti[:, 0:16], A.max)
     ox2 = V(tc, [x], T.ofx2[:], ti[:, 208:224])
-    oc2 = V(tc, [cf], T.ofc2[:], ti[:, 96:112])
-    lo = V(ts, [cf], ti[:, 112:128], ti[:, 96:112], 127, None, A.bitwise_and)
-    hb = V(ts, [cf, ox2], ti[:, 128:144], ti[:, 96:112], 7, 1, A.logical_shift_right, A.bitwise_and)
-    tl = V(tt, [lo], ti[:, 144:160], ti[:, 96:112], ti[:, 112:128], A.add)
-    hm = V(ts, [hb], ti[:, 176:192], ti[:, 128:144], -127.0, None, A.mult)
-    x = V(tt, [tl, hm], ti[:, 224:240], ti[:, 144:160], ti[:, 176:192], A.add)
-    os2 = V(tc, [x], T.ofs2[:], ti[:, 224:240])
-    sr2 = S([os2], T.scr2[:], T.sc[:].indirect(T.ofs2[:]), F.Copy)
-    c1r = S([ox, ga], T.chr1[:], T.ab[:].indirect(T.ofx1[:]), F.Copy)
-    c2r = S([oc2, ga], T.chr2[:], T.ab[:].indirect(T.ofc2[:]), F.Copy)
-    D("s", [c1r], "dch1", T.ch[0:1, :], T.chr1[0:1, :])
-    D("s", [c2r], "dch2", T.ch[1:2, :], T.chr2[0:1, :])
+    jp = places((cf, ti[:, 96:112]), ti[:, 224:240], ti[:, 240:256], tj[:, 96:112], tj[:, 112:128], tj[:, 128:144])()
+    os2 = V(tc, [jp], T.ofs2[:], tj[:, 128:144])
 
-    arr = ("rc", 14)
-    pc = V(tc, [arr, ox2, q1b], T.x2[:].bitcast(u32), T.w2[:, 0:480].bitcast(u32).indirect(T.ofx2[:]))
-    pk = S([arr, ox2, q1b], T.x2s[:], T.w2s[:, 0:480].indirect(T.ofx2[:]), F.Copy)
-    hd = states(T.x2, T.x2s, T.ps, T.e2t, T.h2, T.tm2, e2, [pc, pk, g1])
-    q2 = V(qz, [hd], T.zq[:], T.zqs[:], T.h2[:])
-    m1 = MM([q2, qw], T.ps[:, 0:P], T.wq[:], T.wqs[:], T.zq[:], T.zqs[:])
-    m2 = MM([q2], T.ps[:, 512:512 + P], T.uq[:], T.uqs[:], T.zq[:], T.zqs[:])
-    D("y", [q2], "dout", T.oc[:, :], T.zq[:].bitcast(u8))
-    yy = S([m1], T.ys[:], T.ps[:, 0:P], F.Copy)
-    gg = V(tt, [m2, sr2], T.go[0:1, :], T.ps[0:1, 512:512 + P], T.scr2[0:1, :], A.add)
-    D("y", [yy], "dout", T.y[:, :], T.ys[:])
-    for k in range(4):
-        D("s", [q2], "dch2", T.osc[4 * k:4 * k + 4, :], T.zqs[32 * k:32 * k + 4, :])
-    D("y", [gg], "dout", T.g[0:1, :], T.go[0:1, :])
+    def absolute(x, n, a, b, out):
+        x = V(ts, [x], a, n, float(P * d), None, A.add)
+        x = V(ts, [x], b, a, 2047, None, A.bitwise_and)
+        return V(tc, [x], out, b)
+
+    oa1 = absolute(ji, tj[:, 0:16], tj[:, 144:160], tj[:, 160:176], T.ofa1[:])
+    oa2 = absolute(cf, ti[:, 96:112], tj[:, 176:192], tj[:, 192:208], T.ofa2[:])
+    sr2 = S([os2], T.scr2[:], T.sc[:].indirect(T.ofs2[:]), F.Copy)
+    c1r = S([oa1, gi, io], T.chr1[:], T.iot[:].indirect(T.ofa1[:]), F.Copy)
+    c2r = S([oa2], T.chr2[:], T.iot[:].indirect(T.ofa2[:]), F.Copy)
+    D("s", [c1r], "dch", T.ch[0:1, :], T.chr1[0:1, :])
+    D("s", [c2r], "dch", T.ch[1:2, :], T.chr2[0:1, :])
+
+    picks = [pick(T.x2, T.x2s, T.w2[:, 0:480], T.w2s[:, 0:480], T.ofx2, k, [("rc", 14), ox2, q1b]) for k in (0, 1)]
+    q2 = states(T.x2, T.x2s, (T.ps, T.pr), T.e2t, T.h2, T.tm2, T.zq, T.zqs, e2, [p + [g1] for p in picks])
+    for k in (0, 1):
+        c = slice(HALF * k, HALF * k + HALF)
+        m1 = MM([q2[k], qw], T.ps[:, 512 * k:512 * k + HALF], T.wq[:], T.wqs[:], T.zq[:, c], T.zqs[:, c])
+        m2 = MM([q2[k]], T.ps[:, 1024 + 512 * k:1024 + 512 * k + HALF], T.uq[:], T.uqs[:], T.zq[:, c], T.zqs[:, c])
+        D("y", [q2[k]], "dout", T.oc[:, 4 * HALF * k:4 * HALF * (k + 1)], T.zq[:, c].bitcast(u8))
+        yy = S([m1], T.ys[:, c], T.ps[:, 512 * k:512 * k + HALF], F.Copy)
+        gg = V(tt, [m2, sr2], T.go[0:1, c], T.ps[0:1, 1024 + 512 * k:1024 + 512 * k + HALF], T.scr2[0:1, c], A.add)
+        if k:
+            for i in range(4):
+                D("y", [q2[k]], "dout", T.osc[4 * i:4 * i + 4, :], T.zqs[32 * i:32 * i + 4, :])
+        D("y" if k == 0 else "s", [yy], ("dout", "dch")[k], T.y[:, c], T.ys[:, c])
+    D("s", [gg], "dch", T.g[0:1, :], T.go[0:1, :])
 
     wait("g", [(n, total[n]) for n in total])

from concourse.bass import DstId, RemoteDMATransfer
from concourse.mybir import dt, AluOpType as A, AxisListType, ActivationFunctionType as F

N, P, CAP = 8, 256, 32
HALF = P // 2
PIECES = 2
BIG = 9e29
U = 1.0 / 4096.0

_f32, _i32, _u16, _bf = "float32", "int32", "uint16", "bfloat16"
SCRATCH = {"ps": ("psum", [128, 2048], _f32), "pr": ("psum", [128, 2048], _f32), "sld1": ("dram", [8, 128, 2], _f32), "sld2": ("dram", [8, 128, 2], _f32)}
for _d, _l in (
        (_bf, "e0t 1024 e1t 1024 e2t 1024 ut 512 at 2048 wt 512 h1 1024 h2 1024"),
        (_f32, "tm1 1024 tm2 1024 sc 2048 iot 2048 rs 512 rsb 512 zer 256 ta 32 sb 32 tb 32 nq 128 cc1 128 cct1 128 cx1 128 cr1 128 "
               "cc2 128 cct2 128 cx2 256 cr2 288 fc 16 d0 256 d1 256 rv 2 scr1 256 scr2 256 scc 2 g0c 2 g1c 2 chr1 256 chr2 256 go 256 ys 256 "
               "mc 128 mn 128 exm 256 k2 128 nx2 256 nt2 256 dc 256 zz2 256"),
        (_i32, "pt 64 pa 64 np 64 lo 64 hb 64 tl 64 hm 64 po 64 iz 16 ij 8 ic 8 iy 32 ti 256 tj 256"),
        (_u16, "of 64 op 64 rj 16 rh 8 dup 32 dup4 32 rq 2 rqs 16 ofq 16 ofx1 16 ofs1 16 ofa1 16 ofx2 16 ofs2 16 ofa2 16")):
    _w = _l.split()
    for _k in range(0, len(_w), 2):
        SCRATCH[_w[_k]] = ("sbuf", [128, int(_w[_k + 1])], _d)
for _n, _c in (("uq", 128), ("aq", 512), ("wq", 128), ("hw", 2048), ("hr", 256), ("x1", 256), ("hq", 256), ("sp", 224), ("w2", 512), ("x2", 256),
               ("zq", 256)):
    SCRATCH[_n] = ("sbuf", [128, _c], "float8_e4m3fn_x4")
    SCRATCH[_n + "s"] = ("sbuf", [128, _c], "uint8")
for _t in ("1", "2"):
    for _n, _c in (("ga", 512), ("mx", 512), ("fl", 512), ("cn", 512), ("nr", 512), ("vd", 512),
                   ("ad", 256), ("mk", 256), ("ct", 256), ("ex", 512), ("tr", 512), ("mr", 512)):
        SCRATCH[_n + _t] = ("sbuf", [128, _c], _f32)

SEMAPHORES = ["cv", "cs", "ct", "cg", "l0", "ls", "r0", "rg", "rr", "rc", "hk"] + ["h%d" % i for i in range(N)] + ["hc%d" % i for i in range(PIECES)]
SEMAPHORES += ["de0", "du", "dp1", "dp2", "da", "de1", "dw", "de2", "dog0", "dog1", "ds0", "ds1", "ds2", "ds3", "dsc", "dofq", "dofs", "dch", "dout"]


def bits(m):
    return bin(m).count("1")


def plan(d, cores, topo):
    me = cores[d]
    here = topo.chip(me)
    order = sorted([i for i in range(N) if i != d], key=lambda i: (-min((i - d) % N, (d - i) % N), (i - d) % N))
    mate = [i for i in order if topo.mates(here, topo.chip(cores[i]))]
    plane = [i for i in order if topo.same_plane(here, topo.chip(cores[i]))]
    far = [i for i in order if i not in mate + plane]
    used, out = [me], []
    for same, ranks in ((True, far[2:] + mate), (True, plane[1:]), (False, far[:1] + plane[:1]), (False, far[1:2])):
        able = [h for h in topo.cores_of(me) if h not in used and (topo.die(h) == topo.die(me)) == same and all(topo.may_write(h, cores[i]) for i in ranks)]
        able.sort(key=lambda h: sum(topo.may_write(h, cores[i]) for i in order))
        used.append(able[0])
        out.append((able[0], ranks))
    return [(h, r, out[k + 1][0] if k % 2 == 0 else None) for k, (h, r) in enumerate(out)]


def chip_engines(topo, core, near, far):
    return topo.mask(core, near) & ~topo.mask(core, far)


def pieces(T):
    w = P // PIECES
    out = []
    for k in range(PIECES):
        out.append(("hc%d" % k, T.hr[:, w * k:w * k + w].bitcast(dt.uint8), lambda q, k=k: T.hw[:, P * q + w * k:P * q + w * k + w].bitcast(dt.uint8)))
    out.append(("hk", T.hrs[:], lambda q: T.hws[:, P * q:P * q + P]))
    return out


def dst_of(topo, c):
    rid, pid, _ = topo.addr(c)
    return DstId(rid=rid, pnc=pid)


def hand_on(g, core, T, topo):
    for d in range(N):
        for h, ranks, sub in plan(d, T.cores, topo):
            if h != core:
                continue
            far = T.cores[ranks[0]]
            mask = topo.mask(core, far)
            came = bits(chip_engines(topo, T.cores[d], core, far))
            n = 0
            for sem, here, land in pieces(T):
                g.wait_ge(T.sem[sem], came)
                ts = [RemoteDMATransfer(dst_ids=[dst_of(topo, T.cores[i]) for i in ranks], dma_engine_mask=mask, remote_sem=T.sem["h%d" % d], srcs=[here],
                                        dsts=[land((d - i) % N) for i in ranks])]
                n += bits(mask)
                if sub is not None:
                    m = chip_engines(topo, core, sub, far)
                    ts.insert(0, RemoteDMATransfer(dst_ids=[dst_of(topo, sub)], dma_engine_mask=m, remote_sem=T.sem[sem], srcs=[here], dsts=[here]))
                    n += bits(m)
                g.remote_dma_fused(ts, local_sem=T.sem.ls)
            g.wait_ge(T.sem.ls, n)


def rank_program(g, core, T, topo):
    d = T.rank_of(core)
    if d is None:
        hand_on(g, core, T, topo)
        return
    cores = T.cores
    Q = {"v": g.vector, "s": g.scalar, "t": g.tensor, "g": g, "y": g.sync}
    total, seen = {}, {}

    def wait(q, deps):
        need = {}
        for name, val in deps:
            need[name] = max(val, need.get(name, 0))
        for name in need:
            if seen.get((q, name), 0) < need[name]:
                Q[q].wait_ge(T.sem[name], need[name])
                seen[(q, name)] = need[name]

    def note(ins, name, n):
        ins.then_inc(T.sem[name], n)
        total[name] = total.get(name, 0) + n
        return (name, total[name])

    def V(call, deps, *args, **kw):
        wait("v", deps)
        return note(call(*args, **kw), "cv", 1)

    def S(deps, *args, **kw):
        wait("s", deps)
        return note(g.scalar.activation(*args, **kw), "cs", 1)

    def MM(deps, out, w, ws, x, xs):
        wait("t", deps)
        return note(g.tensor.matmul_mx(out, w, ws, x, xs, True, True), "ct", 1)

    def G(call, deps, *args, **kw):
        wait("g", deps)
        return note(call(*args, **kw), "cg", 1)

    def D(q, deps, name, out, in_):
        wait(q, deps)
        return note(Q[q].dma_start(out, in_), name, 16)

    tt, ts, tc = g.vector.tensor_tensor, g.vector.tensor_scalar, g.vector.tensor_copy
    ms, qz, scan, red, tp = g.vector.memset, g.vector.quantize_mx, g.vector.tensor_tensor_scan, g.vector.tensor_reduce, g.vector.transpose
    u8, u32 = dt.uint8, dt.uint32

    others = [(d + k) % N for k in range(1, N)]
    all_ = [cores[i] for i in others]
    mask = topo.mask(core, all_[0])
    for c in all_:
        mask &= topo.mask(core, c)
    engs = [e for e in topo.engines(core, all_[0]) if mask >> e & 1]
    neng = len(engs)
    helpers = [h for h, r, sub in plan(d, cores, topo)][0::2]
    inner = chip_engines(topo, core, helpers[0], all_[0])

    def sent(name, n):
        total[name] = total.get(name, 0) + n
        return (name, total[name])

    def send(deps, sem, src, to, dsts, local="ls", m=mask):
        wait("g", deps)
        g.remote_dma_fused([RemoteDMATransfer(dst_ids=[dst_of(topo, c) for c in to], dma_engine_mask=m, remote_sem=T.sem[sem], srcs=[src], dsts=dsts)],
                           local_sem=T.sem[local])
        return sent(local, bits(m))

    def send_each(deps, sem, pairs):
        wait("g", deps)
        g.remote_dma_fused([RemoteDMATransfer(dst_ids=[dst_of(topo, all_[k])], dma_engine_mask=1 << engs[k], remote_sem=T.sem[sem], srcs=[a], dsts=[b])
                            for k, (a, b) in enumerate(pairs)], local_sem=T.sem.ls)
        return sent("ls", len(pairs))

    def rel(s, r):
        return (s - r) % N

    e0 = D("y", [], "de0", T.e0t[:], T.e0[:, :])
    uu = D("s", [], "du", T.ut[:], T.u[:, :])
    for k in range(8):
        p1 = D("y", [], "dp1", T.pt[16 * k:16 * k + 16, 0:32], T.p1[:, 32 * (k % 2):32 * (k % 2) + 32])
    da = D("y", [], "da", T.at[:], T.a[:, :])

    gi = G(g.iota, [], T.iot[:, 0:512], [[1, 512]], 0, 0, allow_small_or_imprecise_dtypes=True)
    gp = G(g.iota, [], T.ic[:, 0:1], [[0, 1]], 0, 1)
    giy = G(g.iota, [], T.iy[:], [[16, 16], [0, 2]], 0, 0)
    giz = G(g.iota, [], T.iz[:], [[16, 2], [32, 4], [0, 2]], 0, 0)
    gij = G(g.iota, [], T.ij[:], [[16, 8]], 0, 0)
    c0 = V(ms, [], T.sc[:, 0:512], 0.0)
    zr = V(ms, [], T.zer[:], 0.0)
    r1 = V(ms, [], T.rs[:], BIG)
    for k in (1, 2, 3):
        sc0 = S([c0], T.sc[:, 512 * k:512 * k + 512], T.sc[:, 0:512], F.Copy)
    for k in (1, 2, 3):
        io = S([gi], T.iot[:, 512 * k:512 * k + 512], T.iot[:, 0:512], F.Identity, bias=512.0 * k)
    rs = V(ms, [r1], T.rs[:, 0:512:4], -BIG)

    q0 = V(qz, [e0], T.hw[:, 0:P], T.hws[:, 0:P], T.e0t[:])
    quq = V(qz, [uu], T.uq[:], T.uqs[:], T.ut[:])

    def scores(deps, w, ws, ps):
        return MM(deps + [quq], ps, w, ws, T.uq[:], T.uqs[:])

    for k in (0, 1):
        m = scores([q0], T.hw[:, HALF * k:HALF * k + HALF], T.hws[:, HALF * k:HALF * k + HALF], T.ps[:, 512 * k:512 * k + 128])
    g0 = V(tc, [m], T.g0c[:], T.ps[:, 0:1024:512])
    parts = pieces(T)
    send([q0], parts[0][0], parts[0][2](0), helpers, [parts[0][1]] * 2, "l0", inner)
    send([g0], "r0", T.g0c[:], all_, [T.sld1[rel(d, i)] for i in others])
    for sem, there, here in parts[1:]:
        send([q0], sem, here(0), helpers, [there] * 2, "l0", inner)
    og = D("y", [g0], "dog0", T.sld1[0], T.g0c[:])

    def places(n, lo, hb, tl, hm, po):
        a1 = V(ts, [n[0]], lo, n[1], 127, None, A.bitwise_and)
        a2 = V(ts, [n[0]], hb, n[1], 7, 1, A.logical_shift_right, A.bitwise_and)

        def rest():
            a3 = V(tt, [a1], tl, n[1], lo, A.add)
            a4 = V(ts, [a2], hm, hb, -127.0, None, A.mult)
            return V(tt, [a3, a4], po, tl, hm, A.add)
        return rest

    def listed(t, dep):
        o = slice(32 * t - 32, 32 * t)
        x = V(ts, [dep], T.pa[:, o], T.pt[:, o], float(2048 - P * d), None, A.add)
        x = V(ts, [x], T.np[:, o], T.pa[:, o], 2047, None, A.bitwise_and)
        of = V(tc, [x], T.of[:, o], T.np[:, o])
        x = places((x, T.np[:, o]), T.lo[:, o], T.hb[:, o], T.tl[:, o], T.hm[:, o], T.po[:, o])()
        return of, V(tc, [x], T.op[:, o], T.po[:, o])

    def row(t, of):
        return S([gi, io, of], T["nr%d" % t][:], T.iot[:].indirect(T.of[:, 32 * t - 32:32 * t]), F.Copy, scale=U)

    def deltas(t, nr):
        r, v = T["nr%d" % t], T["vd%d" % t]
        z = V(tt, [nr], v[:, 0:511], r[:, 0:511], r[:, 1:512], A.subtract)
        return V(tc, [z], v[:, 3:512:4], r[:, 3:512:4])

    nr, vd, fl0, ops = {}, {}, {}, {}
    of1, ops[1] = listed(1, p1)
    nr[1] = row(1, of1)
    ic, fc = T.ic, T.fc
    b1 = V(ts, [gp], ic[:, 1:2], ic[:, 0:1], 7, None, A.bitwise_and)
    b4 = V(ts, [gp], ic[:, 4:5], ic[:, 0:1], 3, None, A.logical_shift_right)
    b5 = V(ts, [gp], ic[:, 5:6], ic[:, 0:1], 15, None, A.bitwise_and)
    b2 = V(ts, [b1], ic[:, 2:3], ic[:, 1:2], float(N - d), None, A.add)
    b3 = V(ts, [b2], ic[:, 3:4], ic[:, 2:3], 7, None, A.bitwise_and)
    fl0[1] = V(ms, [], T.fl1[:, 0:512:4], 0.0)
    b6 = V(tc, [b3, b4, b5], fc[:, 0:3], ic[:, 3:6])
    rh = V(tc, [gij], T.rh[:], T.ij[:])
    c1 = V(ts, [b6], fc[:, 3:4], fc[:, 0:1], -256.0 * U, -127.5 * U, A.mult, A.add)
    c2 = V(ts, [b6], fc[:, 4:5], fc[:, 0:1], 0.0, -100.0, A.is_equal, A.mult)
    c4 = V(ts, [b6], fc[:, 10:11], fc[:, 0:1], 0.0, None, A.is_equal)
    dup = V(ts, [b6, giy], T.dup[:], T.iy[:], fc[:, 2:3], None, A.add)
    nbc = V(tt, [c1, c2], fc[:, 5:6], fc[:, 3:4], fc[:, 4:5], A.add)
    nq = S([nr[1], c4], T.nq[:], T.nr1[:, 0:512:4], F.Copy, scale=fc[:, 10:11])
    r2 = V(ms, [], T.rsb[:, 0:256], BIG)
    sb0 = V(ms, [], T.sb[:], 0.0)
    rsb = V(ms, [r2], T.rsb[:, 0:256:16], -BIG)
    qa = V(qz, [da], T.aq[:], T.aqs[:], T.at[:])
    vd[1] = deltas(1, nr[1])

    def spread(land, deps, sems):
        for k in range(8):
            D("ys"[k % 2], deps, sems[k % 2], T.sc[16 * k:16 * k + 1, :], land[:])
        return [(n, total[n]) for n in sems]

    def choose(t, deps):
        ga_, mx_, fl_, cn_ = T["ga%d" % t], T["mx%d" % t], T["fl%d" % t], T["cn%d" % t]
        deps = deps + [ops[t]]
        x1 = V(tc, deps, ga_[:, 0:256], T.sc[:].indirect(T.op[:, 32 * t - 32:32 * t - 16]))
        x2 = S(deps, ga_[:, 256:512], T.sc[:].indirect(T.op[:, 32 * t - 16:32 * t]), F.Copy)
        m = V(scan, [x1, x2, rs], mx_[:], T.rs[:], ga_[:], -BIG, A.min, A.max)
        for k in (1, 2, 3):
            f = V(tt, [m, fl0[t]], fl_[:, k:512:4], ga_[:, k:512:4], mx_[:, k - 1:512:4], A.is_le)
        return V(scan, [f, vd[t]], cn_[:], fl_[:], T["vd%d" % t][:], 0.0, A.mult, A.add), x1, x2

    def whole(t, n, lists, out, deps):
        cc, cct, cx, cn = T["cc%d" % t], T["cct%d" % t], T["cx%d" % t], T["cn%d" % t]
        w, k = n // 2, lists.shape[1] // 2
        x = V(tc, deps, cc[:], cn[:, 3:512:4])
        x = V(tp, [x], cct[:], cc[:])
        x1 = V(tc, [x], cx[:, 0:w], cct[:].indirect(lists[:, 0:k]))
        x2 = S([x], cx[:, w:n], cct[:].indirect(lists[:, k:2 * k]), F.Copy)
        return V(tp, [x1, x2], out, cx[:])

    def keep1(c, deps):
        x = S(deps + [nbc], T.ad1[:, 0:128], c, F.Abs, bias=fc[:, 5:6])
        mk = V(ts, [x], T.mk1[:, 0:128], T.ad1[:, 0:128], 128.0 * U, None, A.is_lt)
        x = V(scan, [mk, zr], T.ct1[:, 0:128], T.mk1[:, 0:128], T.zer[:, 0:128], 0.0, A.add, A.add)
        y = V(tt, [mk] + deps, T.mc[:], T.mk1[:, 0:128], c, A.mult)
        x = V(tp, [x], T.ta[:], T.ct1[:, 96:128])
        y = V(tt, [y, nq], T.mn[:], T.mc[:], T.nq[:], A.add)
        y = S([y, dup], T.exm[:], T.mn[:].indirect(T.dup[:, 0:16]), F.Copy)
        x = V(tc, [x, sb0], T.sb[:, 16:32], T.ta[:, 0:16])
        x = V(tp, [x], T.tb[:], T.sb[:])
        x = V(ts, [x], T.k2[:], T.ct1[:, 0:128], T.tb[:, 31:32], float(CAP), A.add, A.is_le)
        return V(tt, [x, y], T.ex1[:, 0:256], T.k2[:].indirect(T.dup[:, 0:16]), T.exm[:], A.mult)

    def onto(t, deps):
        w = P * t
        x = V(tp, deps, T["tr%d" % t][:, 0:w], T["ex%d" % t][:, 0:w])
        return V(scan, [x, rsb], T["mr%d" % t][:, 0:w], T.rsb[:, 0:w], T["tr%d" % t][:, 0:w], -BIG, A.min, A.max)

    def states(x, xs, banks, et, h, tm, q, qs, edep, picks, between=None):
        m, s, out = {}, {}, []
        for k in (0, 1):
            for i in range(4):
                m[k, i] = MM(picks[k] + [qa], banks[k][:, 512 * i:512 * i + HALF], T.aq[:, 128 * i:128 * i + 128], T.aqs[:, 128 * i:128 * i + 128],
                             x[:, HALF * k:HALF * k + HALF], xs[:, HALF * k:HALF * k + HALF])
        for k in (0, 1):
            for i in range(4):
                o = P * i + HALF * k
                s[k, i] = S([m[k, i]], tm[:, o:o + HALF], banks[k][:, 512 * i:512 * i + HALF], F.Copy, scale=0.05)
            if k == 0 and between is not None:
                between()
        for k in (0, 1):
            for i in range(4):
                o = P * i + HALF * k
                c = slice(4 * HALF * k + i, 4 * HALF * (k + 1), 4)
                a = V(tt, [s[k, i], edep], h[:, c], tm[:, o:o + HALF], et[:, c], A.add)
            out.append(V(qz, [a], q[:, HALF * k:HALF * k + HALF], qs[:, HALF * k:HALF * k + HALF], h[:, 4 * HALF * k:4 * HALF * (k + 1)]))
        return out

    got = spread(T.sld1, [og, ("r0", 7 * neng), c0, sc0], ("ds0", "ds1"))
    e1 = D("y", got, "de1", T.e1t[:], T.e1[:, :])
    for k in range(8):
        p2 = D("y", [], "dp2", T.pt[16 * k:16 * k + 16, 32:64], T.p2[:, 32 * (k % 2):32 * (k % 2) + 32])
    e2 = D("y", [], "de2", T.e2t[:], T.e2[:, :])
    dw = D("y", [], "dw", T.wt[:], T.w[:, :])
    ch, g0v, g0s = choose(1, got)
    cr = whole(1, 128, T.rh, T.cr1[:], [ch, rh])
    z = onto(1, [keep1(T.cr1[:], [cr])])
    o1 = V(ts, [z], T.ofx1[:, 0:8], T.mr1[:, 7:256:32], 4096.0, None, A.mult)
    o2 = V(ts, [z], T.ofx1[:, 8:16], T.mr1[:, 23:256:32], 4096.0, None, A.mult)
    arr = [("h%d" % i, (PIECES + 1) * neng) for i in others]
    tj = T.tj
    ji = V(tc, [o2], tj[:, 0:16], T.ofx1[:])
    rest = places((ji, tj[:, 0:16]), tj[:, 16:32], tj[:, 32:48], tj[:, 48:64], tj[:, 64:80], tj[:, 80:96])

    def pick(x, xs, w, ws, o, k, deps):
        c = slice(HALF * k, HALF * k + HALF)
        a = V(tc, deps, x[:, c].bitcast(u32), w.bitcast(u32).indirect(o[:, 8 * k:8 * k + 8]))
        return [a, S(deps, xs[:, c], ws.indirect(o[:, 8 * k:8 * k + 8]), F.Copy)]

    picks = [pick(T.x1, T.x1s, T.hw[:], T.hws[:], T.ofx1, k, [o1, o2] + arr) for k in (0, 1)]
    os1 = V(tc, [rest()], T.ofs1[:], tj[:, 80:96])
    srs = []

    def chosen_scores():
        srs.append(S([os1], T.scr1[:], T.sc[:].indirect(T.ofs1[:]), F.Copy))
        for k in (0, 1):
            srs.append(D("y", [srs[0]], "dsc", T.scc[:, k:k + 1], T.scr1[0:1, HALF * k:HALF * k + HALF]))

    q1 = states(T.x1, T.x1s, (T.pr, T.ps), T.e1t, T.h1, T.tm1, T.hq, T.hqs, e1, picks, chosen_scores)
    for k in (0, 1):
        mg = scores([q1[k]], T.hq[:, HALF * k:HALF * k + HALF], T.hqs[:, HALF * k:HALF * k + HALF], T.pr[:, 512 * k:512 * k + 128])
    g1 = V(tt, [mg, srs[2]], T.g1c[:], T.pr[:, 0:1024:512], T.scc[:], A.add)

    send([g1], "rg", T.g1c[:], all_, [T.sld2[rel(d, i)] for i in others])
    og = D("y", [g1], "dog1", T.sld2[0], T.g1c[:])
    of2, ops[2] = listed(2, p2)
    nr[2] = row(2, of2)
    dup4 = V(ts, [b6, giy], T.dup4[:], T.iy[:], fc[:, 2:3], 4.0, A.add, A.mult)
    fl0[2] = V(ms, [], T.fl2[:, 0:512:4], 0.0)
    i5c = V(ts, [b6], fc[:, 6:7], fc[:, 0:1], 512.0, None, A.mult)
    c3 = V(ts, [b6], fc[:, 7:8], fc[:, 0:1], 512.0 + 256.0 * U, 1.0, A.mult, A.add)
    rj = V(tc, [giz], T.rj[:], T.iz[:])
    t0c = V(tt, [c3], fc[:, 8:9], fc[:, 7:8], fc[:, 1:2], A.add)
    r2 = V(ms, [], T.rsb[:, 256:512], BIG)
    t1c = V(ts, [t0c], fc[:, 9:10], fc[:, 8:9], -1.0, -16.0, A.mult, A.add)
    cz = V(ms, [], T.cr2[:, 0:32], 0.0)
    vd[2] = deltas(2, nr[2])
    z = S([nr[2], dup4], T.nx2[:], T.nr2[:].indirect(T.dup4[:, 0:16]), F.Copy)
    z = V(tp, [z], T.nt2[:], T.nx2[:])
    rsb = V(ms, [r2], T.rsb[:, 256:512:16], -BIG)
    n0 = V(ts, [z], T.ti[:, 0:8], T.nt2[:, 0:256:32], 4096.0, None, A.mult)
    n0 = V(ts, [z], T.ti[:, 8:16], T.nt2[:, 16:256:32], 4096.0, None, A.mult)
    q1b = V(qz, q1, T.w2[:, 0:P], T.w2s[:, 0:P], T.h1[:])
    qw = V(qz, [dw], T.wq[:], T.wqs[:], T.wt[:])
    got = spread(T.sld2, [og, ("rg", 7 * neng), g0v, g0s, srs[0]], ("ds2", "ds3"))

    ch = choose(2, got)[0]
    cr_ = T.cr2[:, 32:288]
    cr = whole(2, 256, T.rj, cr_, [ch, rj])
    x = S([cr, nbc], T.ad2[:], cr_, F.Abs, bias=fc[:, 5:6])
    y = V(tt, [cr, cz], T.dc[:], cr_, T.cr2[:, 31:287], A.subtract)
    mk = V(ts, [x], T.mk2[:], T.ad2[:], 128.0 * U, None, A.is_lt)
    z = V(scan, [mk, y, i5c], T.ct2[:], T.mk2[:], T.dc[:], fc[:, 6:7], A.add, A.add)
    zz = V(tt, [z], T.zz2[:], T.mk2[:], T.ct2[:], A.mult)
    y1 = S([zz, t1c], T.d1[:], T.zz2[:], F.Identity, bias=fc[:, 9:10])
    y0 = V(ts, [zz, t0c], T.d0[:], T.zz2[:], fc[:, 8:9], None, A.subtract)
    y0 = V(red, [y0], T.rv[:, 0:1], T.d0[:], AxisListType.X, A.min, apply_absolute_value=True)
    y1 = V(red, [y1], T.rv[:, 1:2], T.d1[:], AxisListType.X, A.min, apply_absolute_value=True)
    rq = V(ts, [y0, y1], T.rq[:], T.rv[:], 255.0 * U, 4096.0, A.min, A.mult)
    send([rq], "rr", T.rq[:], all_, [T.rqs[:, 2 * rel(d, i):2 * rel(d, i) + 2] for i in others])
    for k in range(8):
        D("ys"[k % 2], [("rr", 7 * neng)], ("dofq", "dofs")[k % 2], T.ofq[16 * k:16 * k + 16, 2:16], T.rqs[d:128:8, 2:16])
    oq = [("dofq", 64), ("dofs", 64)]
    z = V(tc, [zz, dup], T.ex2[:], T.zz2[:].indirect(T.dup[:]))
    z = onto(2, [z])
    ti = T.ti
    zi = V(ts, [z], ti[:, 16:32], T.mr2[:, 7:512:32], 4096.0, None, A.mult)
    ky = V(ts, [zi], ti[:, 48:64], ti[:, 16:32], 12, 511, A.logical_shift_right, A.bitwise_and)
    ci = V(ts, [zi], ti[:, 32:48], ti[:, 16:32], 4095, None, A.bitwise_and)
    kq = V(ts, [zi], ti[:, 112:128], ti[:, 16:32], 21, None, A.logical_shift_right)
    kf = V(ts, [ky], ti[:, 64:80], ti[:, 48:64], float(CAP), None, A.is_le)
    pc = V(tc, oq + q1, T.sp[:].bitcast(u32), T.hq[:].bitcast(u32).indirect(T.ofq[:, 2:16]))
    pk = S(oq + q1, T.sps[:], T.hqs[:].indirect(T.ofq[:, 2:16]), F.Copy)
    ca, cb = [], []
    for i in others:
        a, b = CAP * (rel(i, d) - 1), P + CAP * (rel(d, i) - 1)
        ca.append((T.sp[:, a:a + CAP].bitcast(u8), T.w2[:, b:b + CAP].bitcast(u8)))
        cb.append((T.sps[:, a:a + CAP], T.w2s[:, b:b + CAP]))
    send_each([pc], "rc", ca)
    send_each([pk], "rc", cb)
    kc = V(tt, [kf, ci], ti[:, 80:96], ti[:, 64:80], ti[:, 32:48], A.mult)
    x = V(ts, [kq], ti[:, 128:144], ti[:, 112:128], 32.0, None, A.mult)
    cf = V(tt, [kc, n0], ti[:, 96:112], ti[:, 80:96], ti[:, 0:16], A.max)
    x = V(tt, [x, ky], ti[:, 144:160], ti[:, 128:144], ti[:, 48:64], A.add)
    x = V(tt, [x, kf], ti[:, 160:176], ti[:, 144:160], ti[:, 64:80], A.mult)
    y = V(ts, [x], ti[:, 176:192], ti[:, 160:176], 0.0, 223.0, A.is_gt, A.mult)
    x = V(tt, [y], ti[:, 192:208], ti[:, 160:176], ti[:, 176:192], A.add)
    x = V(tt, [x], ti[:, 208:224], ti[:, 192:208], ti[:, 0:16], A.max)
    ox2 = V(tc, [x], T.ofx2[:], ti[:, 208:224])
    jp = places((cf, ti[:, 96:112]), ti[:, 224:240], ti[:, 240:256], tj[:, 96:112], tj[:, 112:128], tj[:, 128:144])()
    os2 = V(tc, [jp], T.ofs2[:], tj[:, 128:144])

    def absolute(x, n, a, b, out):
        x = V(ts, [x], a, n, float(P * d), None, A.add)
        x = V(ts, [x], b, a, 2047, None, A.bitwise_and)
        return V(tc, [x], out, b)

    oa1 = absolute(ji, tj[:, 0:16], tj[:, 144:160], tj[:, 160:176], T.ofa1[:])
    oa2 = absolute(cf, ti[:, 96:112], tj[:, 176:192], tj[:, 192:208], T.ofa2[:])
    sr2 = S([os2], T.scr2[:], T.sc[:].indirect(T.ofs2[:]), F.Copy)
    c1r = S([oa1, gi, io], T.chr1[:], T.iot[:].indirect(T.ofa1[:]), F.Copy)
    c2r = S([oa2], T.chr2[:], T.iot[:].indirect(T.ofa2[:]), F.Copy)
    D("s", [c1r], "dch", T.ch[0:1, :], T.chr1[0:1, :])
    D("s", [c2r], "dch", T.ch[1:2, :], T.chr2[0:1, :])

    picks = [pick(T.x2, T.x2s, T.w2[:, 0:480], T.w2s[:, 0:480], T.ofx2, k, [("rc", 14), ox2, q1b]) for k in (0, 1)]
    q2 = states(T.x2, T.x2s, (T.ps, T.pr), T.e2t, T.h2, T.tm2, T.zq, T.zqs, e2, [p + [g1] for p in picks])
    for k in (0, 1):
        c = slice(HALF * k, HALF * k + HALF)
        m1 = MM([q2[k], qw], T.ps[:, 512 * k:512 * k + HALF], T.wq[:], T.wqs[:], T.zq[:, c], T.zqs[:, c])
        m2 = MM([q2[k]], T.ps[:, 1024 + 512 * k:1024 + 512 * k + HALF], T.uq[:], T.uqs[:], T.zq[:, c], T.zqs[:, c])
        D("y", [q2[k]], "dout", T.oc[:, 4 * HALF * k:4 * HALF * (k + 1)], T.zq[:, c].bitcast(u8))
        yy = S([m1], T.ys[:, c], T.ps[:, 512 * k:512 * k + HALF], F.Copy)
        gg = V(tt, [m2, sr2], T.go[0:1, c], T.ps[0:1, 1024 + 512 * k:1024 + 512 * k + HALF], T.scr2[0:1, c], A.add)
        if k:
            for i in range(4):
                D("y", [q2[k]], "dout", T.osc[4 * i:4 * i + 4, :], T.zqs[32 * i:32 * i + 4, :])
        D("y" if k == 0 else "s", [yy], ("dout", "dch")[k], T.y[:, c], T.ys[:, c])
    D("s", [gg], "dch", T.g[0:1, :], T.go[0:1, :])

    wait("g", [(n, total[n]) for n in total])
